import numpy as np, ml_dtypes
CORES = [3,11,19,27,35,43,51,59]
N = 8
import mx_ref
BF = ml_dtypes.bfloat16
def cols(t, e):
    v = np.concatenate([t.reshape(128, -1, 4), np.zeros((128, 1, 4), BF)], axis=1)
    return np.ascontiguousarray(v[:, e]).reshape(128, -1)
def cut(t, i, w=512):
    return t[:, w * i:w * i + w]
def tile(rs):
    return np.stack(rs, axis=2).reshape(128, -1).astype(BF)
def pick(q, e):
    c = np.concatenate([q[0].reshape(128, -1, 4), np.zeros((128, 1, 4), np.uint8)], axis=1); s = np.concatenate([q[1], np.ones((16, 1), np.uint8)], axis=1)
    return (np.ascontiguousarray(c[:, e].reshape(128, -1)), np.ascontiguousarray(s[:, e]))
def join(*qs):
    return (np.concatenate([q[0] for q in qs], axis=1), np.concatenate([q[1] for q in qs], axis=1))
def put(q, e, v):
    c, s = q[0].reshape(128, -1, 4).copy(), q[1].copy(); c[:, e] = v[0].reshape(128, -1, 4); s[:, e] = v[1]
    return (c.reshape(128, -1), s)
def pk(c, s):
    return (np.ascontiguousarray(c), mx_ref.live(s))
def emit(q):
    return q[0], q[1]
def decode(q):
    o = []
    for b in range(4):
        e = np.zeros((128, 128, 4), np.float32); e[np.arange(128), np.arange(128), b] = 1
        o.append(mx_ref.matmul(mx_ref.quantize(e.reshape(128, 512).astype(BF)), q))
    return np.stack(o, axis=2).reshape(128, -1)
def f(rng, *shape):
    return mx_ref.flush((rng.standard_normal(shape, dtype=np.float32) * np.exp2(rng.integers(-2, 3, shape[:-1] + (1,)))).astype(BF))
def wide(rng, *shape, cols=0):
    v = rng.standard_normal(shape, dtype=np.float32) * np.exp2(rng.integers(-12, 13, shape)).astype(np.float32)
    if cols: v *= np.repeat(np.exp2(rng.integers(-cols, cols + 1, shape[:-2] + (1, shape[-1] // 4))) * (rng.random(shape[:-2] + (1, shape[-1] // 4)) > 0.0625), 4, axis=-1).astype(np.float32)
    return mx_ref.flush(v.astype(BF))
T, A, KM, CAPP, FA = 128, 32, 48, 16, 2
def big(t):
    t = np.array(t)
    t[np.abs(t.astype(np.float32)) < np.float32(2.0 ** -16)] = 0
    return t
def plain(rng):
    x = np.concatenate([f(rng, N, 128, 4 * A), f(rng, N, 128, 4 * (T - A))], axis=2)
    return {"x": big(x), "w": f(rng, N, 128, 2048), "v": f(rng, N, 128, 512)}
def pull(rng, x, at, who, n=8, bare=False):
    x = np.array(x).reshape(N, 128, T, 4)
    x[:, :n * len(at)] = 0
    for i, (q, a) in enumerate(at):
        if bare: x[q, :, a] = 0
        x[q, n * i:n * i + n, a] = (32 * (1 + rng.random((n, 4)))).astype(np.float32).astype(BF)
        r, j = np.nonzero(who == i)
        x[r, n * i:n * i + n, j] = (8 * (1 + rng.random((len(r), n, 4)))).astype(np.float32).astype(BF)
    return x.reshape(N, 128, 4 * T)
def setup_inputs(rng):
    return plain(rng)
def setup_inputs_crowd(rng):
    d, who = plain(rng), np.full((N, T), -1)
    z, q = int(rng.integers(1, N)), rng.permutation(N)[:2]
    for r in range(N):
        e = A + rng.permutation(T - A)[:KM * 5 // 6 + FA]
        who[r, e] = 0
        who[r, e[:FA]] = 1
    who[z, A:] = rng.integers(0, 2, T - A)
    d["x"] = pull(rng, d["x"], [(int(q[i]), int(rng.integers(0, A))) for i in range(2)], who)
    return d
def setup_inputs_full(rng):
    d, who, o = plain(rng), np.full((N, T), -1), rng.permutation(N)
    g = FA * A // CAPP
    e = np.tile(rng.permutation(A), FA).reshape(g, CAPP)
    for i, s in enumerate(np.sort(o[1:g + 1])):
        who[s, A:A + CAPP] = rng.permutation(e[i])
        who[s, A + CAPP:A + CAPP + 4] = e[-1, -1]
    d["x"] = pull(rng, d["x"], [(int(o[0]), a) for a in range(A)], who, 2, True)
    return d
def setup_inputs_ties(rng):
    d = plain(rng)
    x = np.array(d["x"])
    part = np.arange(128) // 8
    m = rng.permutation(N * A) % (N * A // 4)
    k = cols(np.concatenate([x[q][:, :4 * A] for q in range(N)], axis=1), rng.permutation(N * A)[m])
    k = np.abs(k.astype(np.float32)) * np.repeat(np.where(part[:, None] == m % 16, 2.0 ** -8, 1.0), 4, axis=1)
    k = big(k.astype(np.float32).astype(BF))
    for r in range(N):
        g = rng.permutation(np.arange(T - A) // 7)
        u = cols(np.ascontiguousarray(x[r][:, 4 * A:]), g)
        if r == 0:
            on = part[:, None] == (m[0] + 1 + g % 15) % 16
            u = (-np.abs(u.astype(np.float32)) * np.repeat(on, 4, axis=1)).astype(BF)
        if r == 1:
            u = np.abs(u.astype(np.float32)).reshape(128, T - A, 4)
            o = np.append(0, 1 + rng.permutation(T - A - 1)[KM // 2:])
            u[:, o[::2]] = -0.0
            u[:, o[1::2]] = 0.0
            u = u.astype(BF).reshape(128, -1)
        x[r][:, 4 * A:] = u
        x[r][:, :4 * A] = cut(k, r, 4 * A)
    d["x"] = x
    return d
def setup_inputs_own(rng):
    d = plain(rng)
    x = np.array(d["x"])
    x[:, :, 2 * A:4 * A] = -x[:, :, :2 * A]
    x[(np.arange(128) // (128 // N))[None, :] != np.arange(N)[:, None]] = 0
    d["x"] = x
    return d
def setup_inputs_spread(rng):
    return {**plain(rng), "x": big(wide(rng, N, 128, 4 * T, cols=4))}
def check_inputs(d):
    b = []
    for k in ("x", "w", "v"):
        t = np.abs(d[k].astype(np.float32))
        if not (np.isfinite(t).all() and ((t == 0) | (t >= 2.0 ** -30) & (t <= 2.0 ** 30)).all()): b.append("a value of " + k)
    return b
def choose(x):
    k = np.concatenate([x[q][:, :4 * A] for q in range(N)], axis=1)
    k = [mx_ref.quantize(np.ascontiguousarray(cut(k, i))) for i in range(N * A // 128)]
    goal, took, have = np.full((N, T), -1), np.full((N, A, FA), -1), np.zeros((N, A), int)
    for s in range(N):
        u = mx_ref.quantize(np.ascontiguousarray(x[s][:, 4 * A:]))
        z = np.concatenate([mx_ref.matmul(t, u) for t in k]) + np.float32(0.0)
        best = np.argmax(z, axis=0)
        offers = np.sort(np.argsort(-z.max(axis=0), kind="stable")[:KM])
        stand = np.zeros(N, int)
        for j in offers:
            q, a = best[j] // A, best[j] % A
            if stand[q] == CAPP: continue
            stand[q] += 1
            if have[q, a] == FA: continue
            took[q, a, have[q, a]] = s * T + A + j
            have[q, a] += 1
            goal[s, A + j] = q * T + a
    return goal, took
def reference(x, w, v):
    goal, took = choose(x)
    c = [mx_ref.quantize(np.ascontiguousarray(x[r])) for r in range(N)]
    d = np.concatenate([decode(c[r]).reshape(128, T, 4) for r in range(N)], axis=1)
    h = []
    for q in range(N):
        m = d[:, q * T:q * T + A].copy()
        for t in range(FA):
            a = np.flatnonzero(took[q, :, t] >= 0)
            m[:, a] = m[:, a] + d[:, took[q, a, t]]
        new = mx_ref.quantize(np.ascontiguousarray((m * np.float32(0.5)).reshape(128, -1).astype(BF)))
        a = np.flatnonzero(took[q, :, 0] >= 0)
        k = put(c[q], a, pick(new, a))
        rs = [np.maximum(mx_ref.matmul(mx_ref.quantize(np.ascontiguousarray(cut(w[q], i))), k), np.float32(0.0)) * np.float32(0.0625) for i in range(4)]
        h.append(mx_ref.quantize(np.ascontiguousarray(tile(rs))))
    every = join(*h)
    oc, osc = np.zeros((N, 128, 4 * T), np.uint8), np.zeros((N, 16, T), np.uint8)
    mg, y = np.zeros((N, 1, T), np.float32), np.zeros((N, 128, T), np.float32)
    for s in range(N):
        g = pick(every, np.where(goal[s] >= 0, goal[s], s * T + np.arange(T)))
        oc[s], osc[s] = emit(g)
        mg[s, 0] = goal[s]
        y[s] = mx_ref.matmul(mx_ref.quantize(np.ascontiguousarray(v[s])), g)
    return {"oc": oc, "osc": osc, "mg": mg, "y": y}

@@ -1,0 +1,449 @@
+from concourse.bass import DstId, RemoteDMATransfer
+from concourse.mybir import dt, AluOpType, AxisListType, ActivationFunctionType
+
+F32, BF, U16, I32, MXC, U8 = "float32", "bfloat16", "uint16", "int32", "float8_e4m3fn_x4", "uint8"
+SCRATCH = {}
+
+
+def _buf(name, cols, dtype):
+    SCRATCH[name] = ("sbuf", [128, cols], dtype)
+
+
+def _mx(name, cols):
+    _buf(name, cols, MXC)
+    _buf(name + "s", cols, U8)
+
+
+for _n, _c in (("qx", 128), ("qn", 128), ("anc", 288), ("qtri", 128), ("qa2", 128), ("qe", 512), ("qz", 128), ("qab", 144),
+               ("qb2", 128), ("snd", 128), ("slots", 256), ("pk", 192), ("qw", 512), ("qv", 128), ("km", 128),
+               ("hq", 128), ("hw", 384), ("fo", 128)):
+    _mx(_n, _c)
+_buf("rl", 64, MXC)
+_buf("rms", 64, U8)
+_buf("rhs", 32, U8)
+for _n, _c in (("xt", 512), ("xa", 512), ("wt", 2048), ("vt", 512), ("ct", 512), ("ct2", 512), ("et", 516), ("ztb", 608),
+               ("att", 576), ("zz", 512), ("mz", 640), ("hot", 512), ("ones", 128), ("ident", 128),
+               ("tri", 128), ("pm1", 256), ("lx", 128), ("arow", 128), ("eq", 256), ("cc", 256), ("c2", 256),
+               ("j12", 256), ("aw", 192), ("at", 128), ("adm4", 8), ("land3", 64), ("ax", 256), ("ar", 272), ("aj", 256),
+               ("ajt", 256)):
+    _buf(_n, _c, BF)
+for _n, _c in (("R", 288), ("mrow", 32), ("thr", 64), ("t1", 64), ("t2", 97), ("sc", 16), ("jr", 256),
+               ("j7", 16), ("ab", 32), ("pen", 32), ("msk", 32), ("num", 32), ("qi", 8), ("qc", 32), ("ri", 16), ("qh", 16),
+               ("crow", 32), ("row8", 8), ("row16", 16), ("pf", 4), ("pc", 8), ("m8", 8), ("m16", 16), ("jw", 8), ("jn", 8),
+               ("lst", 8), ("landL", 32), ("F4", 4), ("tb", 128), ("n1", 4), ("n2", 4), ("n3", 4), ("tmp", 8),
+               ("jf", 8), ("f1", 8), ("f2", 8), ("mw2", 8), ("yo", 128)):
+    _buf(_n, _c, F32)
+for _n, _c in (("il", 2), ("off", 8), ("fs", 4), ("sof", 4), ("posD", 16), ("fin", 8)):
+    _buf(_n, _c, U16)
+_buf("pi", 1, I32)
+_buf("pin", 4, I32)
+for _i in range(8):
+    SCRATCH["ps%d" % _i] = ("psum", [128, 512], F32)
+SEMAPHORES = (["cV", "cA", "cP", "cG", "a1", "o1s", "l2", "c2r", "o2a", "o2b", "o2c", "m3", "o3a", "h3", "o3b", "o3c",
+               "rc", "rp", "rk", "hl"] + ["d%d" % _i for _i in range(12)])
+
+
+def to(topo, c):
+    return DstId(rid=topo.addr(c)[0], pnc=topo.addr(c)[1])
+
+
+def plan(own, r, T, topo):
+    for b in ((2, 1, 0), (0, 2, 1), (1, 2, 0)):
+        order = [r ^ sum((c >> (2 - i) & 1) << b[i] for i in range(3)) for c in range(8)]
+        if all(topo.same_plane(topo.chip(own), topo.chip(T.cores[q])) for q in order[1:4]):
+            break
+    near, far = [T.cores[q] for q in order[1:4]], [T.cores[q] for q in order[4:]]
+    rest = sorted([c for c in topo.cores_of(own) if c != own], key=lambda c: topo.die(c) == topo.die(own))
+    f = [c for c in rest if all(topo.may_write(c, d) for d in far)][:2]
+    n = [c for c in rest if c not in f and all(topo.may_write(c, d) for d in near)][:2]
+    return order, near, far, [f[0], n[0], f[1], n[1]]
+
+
+def hand_on(g, core, r, role, near, far, T, topo):
+    S, CAPP, A = T.sem, 16, 32
+    goal, first = (near, 1) if role % 2 else (far, 0)
+    eng = topo.engines(core, goal[0])
+
+    def piece(i):
+        a = CAPP * (i + first)
+        return T.rms[:, a:a + CAPP] if role >= 2 else T.rl[:, a:a + CAPP].bitcast(dt.uint8)
+
+    land = T.slotss[:, CAPP * r:CAPP * r + CAPP] if role >= 2 else T.slots[:, CAPP * r:CAPP * r + CAPP].bitcast(dt.uint8)
+    g.wait_ge(S.rp if role >= 2 else S.rc, 4)
+    g.remote_dma_fused([RemoteDMATransfer(dst_ids=[to(topo, d)], dma_engine_mask=1 << eng[2 * i] | 1 << eng[2 * i + 1],
+                                          remote_sem=S.c2r, src=piece(i), dst=land) for i, d in enumerate(goal)], local_sem=S.hl)
+    n = 2 * len(goal)
+    if role >= 2:
+        g.wait_ge(S.rk, 4)
+        g.remote_dma_fused([RemoteDMATransfer(dst_ids=[to(topo, d) for d in goal], dma_engine_mask=topo.mask(core, goal[0]),
+                                              remote_sem=S.h3, srcs=[T.rhs[:, 0:A]],
+                                              dsts=[T.hws[:, 128 + A * r:128 + A * r + A]] * len(goal))], local_sem=S.hl)
+        n += len(eng)
+    g.wait_ge(S.hl, n)
+
+
+def rank_program(g, core, T, topo):
+    N, S = len(T.cores), T.sem
+    A, CAPP, KM = 32, 16, 48
+    mine = [c for c in T.cores if topo.chip(c) == topo.chip(core)]
+    if not mine:
+        return
+    r = T.rank_of(mine[0])
+    order, near, far, help4 = plan(mine[0], r, T, topo)
+    if core != mine[0]:
+        if core in help4:
+            hand_on(g, core, r, help4.index(core), near, far, T, topo)
+        return
+    OP, AF, X = AluOpType, ActivationFunctionType, AxisListType.X
+    V, AC, PE, SY = g.vector, g.scalar, g.tensor, g.sync
+    tiny = 1e-29
+
+    qs = {"V": V, "A": AC, "P": PE, "G": g, "S": SY}
+    count, known = {}, {q: {} for q in qs}
+    writer, readers = {}, {}
+
+    def before(q, rd, wr):
+        need = [writer[k] for k in rd if k in writer]
+        for k in list(wr) + [k for k in rd if k.startswith("ps")]:
+            if k in writer:
+                need.append(writer[k])
+            need += readers.get(k, [])
+        best = {}
+        for s, v, clk in need:
+            if known[q].get(s, 0) < v and best.get(s, (0,))[0] < v:
+                best[s] = (v, clk)
+        for s in list(best):
+            if not any(o != s and best[o][1].get(s, 0) >= best[s][0] for o in best):
+                qs[q].wait_ge(S[s], best[s][0])
+        for s, (v, clk) in best.items():
+            known[q][s] = max(known[q].get(s, 0), v)
+            for a, b in clk.items():
+                known[q][a] = max(known[q].get(a, 0), b)
+
+    def after(tok, rd, wr):
+        for k in wr:
+            writer[k] = tok
+            readers[k] = []
+        for k in rd:
+            readers.setdefault(k, []).append(tok)
+
+    def op(q, rd, wr, fn, *args, **kw):
+        rd, wr = rd.split(), wr.split()
+        before(q, rd, wr)
+        s = "c" + q
+        count[s] = count.get(s, 0) + 1
+        fn(*args, **kw).then_inc(S[s], 1)
+        after((s, count[s], dict(known[q])), rd, wr)
+
+    dn = [0]
+
+    def dma(q, rd, wr, out, in_):
+        rd, wr = rd.split(), wr.split()
+        before(q, rd, wr)
+        s = "d%d" % dn[0]
+        dn[0] += 1
+        count[s] = 16
+        qs[q].dma_start(out, in_).then_inc(S[s], 16)
+        after((s, 16, dict(known[q])), rd, wr)
+
+    def arrive(s, n, wr):
+        count[s] = n
+        after((s, n, {}), [], wr.split())
+
+    others = [T.cores[q] for q in order[1:]]
+    allm = topo.mask(core, others[0])
+    for c in others:
+        allm &= topo.mask(core, c)
+    eng = [e for e in topo.engines(core, others[0]) if allm >> e & 1]
+    width = len(eng)
+    side = [e for e in topo.engines(core, help4[0]) if e not in eng]
+
+    def to_all(rd, src, dstap, sem, loc):
+        before("G", rd.split(), [])
+        g.remote_dma_fused([RemoteDMATransfer(dst_ids=[to(topo, c) for c in others], dma_engine_mask=allm, remote_sem=S[sem],
+                                              srcs=[src], dsts=[dstap] * len(others))], local_sem=S[loc])
+        count[loc] = count.get(loc, 0) + width
+
+    def to_each(rd, src, dstap, sem, loc):
+        before("G", rd.split(), [])
+        g.remote_dma_fused([RemoteDMATransfer(dst_ids=[to(topo, others[c - 1])], dma_engine_mask=1 << eng[c - 1],
+                                              remote_sem=S[sem], src=src(c), dst=dstap) for c in range(1, N)],
+                           local_sem=S[loc])
+        count[loc] = count.get(loc, 0) + N - 1
+
+    def to_two(rd, src, dstap, sem, loc, roles):
+        before("G", rd.split(), [])
+        h = len(side) // 2
+        g.remote_dma_fused([RemoteDMATransfer(dst_ids=[to(topo, help4[k])],
+                                              dma_engine_mask=sum(1 << e for e in side[h * i:h * i + h]),
+                                              remote_sem=S[sem], src=src[i], dst=dstap) for i, k in enumerate(roles)],
+                           local_sem=S[loc])
+        count[loc] = count.get(loc, 0) + 2 * h
+
+    def ts(rd, wr, out, in0, s1, s2, *ops):
+        op("V", rd, wr, V.tensor_scalar, out, in0, s1, s2, *ops)
+
+    def tt(rd, wr, out, in0, in1, o):
+        op("V", rd, wr, V.tensor_tensor, out, in0, in1, o)
+
+    def cp(rd, wr, out, in_):
+        op("V", rd, wr, V.tensor_copy, out, in_)
+
+    def fill(rd, wr, out, c):
+        op("V", rd, wr, V.memset, out, c)
+
+    def act(rd, wr, out, in_, f, **kw):
+        op("A", rd, wr, AC.activation, out, in_, f, **kw)
+
+    def iota(wr, out, pattern, base=0, mult=0):
+        op("G", "", wr, g.iota, out, pattern, base, mult, allow_small_or_imprecise_dtypes=True)
+
+    def mm(bank, w, wv, x, n, rd, xv=0, start=True, stop=True):
+        op("P", rd, "ps%d" % bank, PE.matmul_mx, T["ps%d" % bank][:, 0:n], T[w][:, wv:wv + 128], T[w + "s"][:, wv:wv + 128],
+           T[x][:, xv:xv + n], T[x + "s"][:, xv:xv + n], start, stop)
+
+    def quant(out, a, n, tile, rd, wr, at=0):
+        op("V", rd, wr, V.quantize_mx, T[out][:, a:a + n], T[out + "s"][:, a:a + n], T[tile][:, at:at + 4 * n])
+
+    def pick(out, a, b, win, w, lists, la, lb, rd, wr, at=0):
+        cp(rd, wr, T[out][:, a:b].bitcast(dt.uint32), T[win][:, at:w].bitcast(dt.uint32).indirect(T[lists][:, la:lb]))
+        act(rd, wr + "s", T[out + "s"][:, a:b], T[win + "s"][:, at:w].indirect(T[lists][:, la:lb]), AF.Copy)
+
+    def layer(i, tile, a, n, wr, both):
+        src, out = T["ps%d" % i][:, 0:n], T[tile][:, a + i:a + 4 * n:4]
+        if i % 2 and both:
+            ts("ps%d" % i, wr, out, src, 0.0, 0.0625, OP.max, OP.mult)
+        else:
+            act("ps%d" % i, wr, out, src, AF.Relu, scale=0.0625)
+
+    dma("S", "", "xa", T.xa[:, 0:4 * A], T.x[:, 0:4 * A])
+    dma("S", "", "xt", T.xt[:], T.x[:])
+    op("G", "", "pi", g.iota, T.pi[:], [[0, 1]], 0, 1)
+    iota("qi", T.qi[:], [[A * (order[c] - r), 2] for c in (4, 2, 1)], A * r)
+    fill("", "ones", T.ones[:], 1.0)
+    op("G", "ones", "tri", g.affine_select, T.tri[:], T.ones[:], [[1, 128]], OP.is_ge, 0.0, 0, -1)
+    fill("", "xaz", T.xa[:, 4 * A:], 0.0)
+    fill("", "zz", T.zz[:], 0.0)
+    ts("pi", "pin", T.pin[:, 0:1], T.pi[:], 15, None, OP.bitwise_and)
+    quant("qn", 0, 128, "xa", "xa xaz", "qn")
+
+    to_all("qn", T.qn[:, 0:A].bitcast(dt.uint8), T.anc[:, A * r:A * r + A].bitcast(dt.uint8), "a1", "o1s")
+    to_all("qn", T.qns[:, 0:A], T.ancs[:, A * r:A * r + A], "a1", "o1s")
+    arrive("a1", 2 * width * (N - 1), "anc")
+    SY.wait_ge(S.o1s, 2 * width)
+    known["S"]["o1s"] = 2 * width
+    dma("S", "", "wt", T.wt[:], T.w[:])
+    dma("S", "", "vt", T.vt[:], T.v[:])
+
+    op("G", "ones", "ident", g.affine_select, T.ident[:], T.ones[:], [[1, 128]], OP.is_equal, 0.0, 0, -1)
+    iota("ri", T.ri[:, 0:15], [[A, 15]], -7 * A)
+    iota("crow", T.crow[:], [[1, 32]])
+    iota("pm1", T.pm1[:], [[0, 8], [1, 16], [0, 2]], 65)
+    iota("row8", T.row8[:], [[1, 8]])
+    iota("row16", T.row16[:], [[1, 8], [0, 2]])
+    for k in range(4):
+        act("qi", "qc%d" % k, T.qc[:, k // 2 * 16 + k % 2:k // 2 * 16 + 16:2], T.qi[:], AF.Identity, bias=0.5 * A - 0.5)
+    act("zz", "num3", T.num[:, 17:32:2], T.zz[:, 0:8], AF.Identity, bias=32.0)
+    ts("pin", "il0", T.il[:, 0:1], T.pin[:, 0:1], 0, None, OP.add)
+    ts("pin", "il1", T.il[:, 1:2], T.pin[:, 0:1], 16, None, OP.add)
+    fill("", "ct", T.ct[:], 0.0)
+    for a, k in ((A * r, "own"), (N * A, "pad")):
+        pick("anc", a, a + A, "qn", 128, "il", 0, 2, "qn il0 il1", "anc" + k)
+    ts("pi", "pin1", T.pin[:, 1:2], T.pi[:], 4, None, OP.arith_shift_right)
+    ts("pi", "pin2", T.pin[:, 2:3], T.pi[:], 31, None, OP.bitwise_and)
+    cp("pin", "pm", T.pf[:, 0:1], T.pin[:, 0:1])
+    cp("pin1", "ph16", T.pf[:, 1:2], T.pin[:, 1:2])
+    cp("pin2", "p31", T.pf[:, 2:3], T.pin[:, 2:3])
+    act("tri ct", "ctri", T.ct[:, 0:512:4], T.tri[:], AF.Copy)
+    act("ident ct", "cid", T.ct[:, 2:512:4], T.ident[:], AF.Copy, scale=64.0)
+    act("zz pm", "num0", T.num[:, 0:16:2], T.zz[:, 0:8], AF.Identity, bias=T.pf[:, 0:1])
+    act("ph16", "khi", T.pc[:, 0:1], T.pf[:, 1:2], AF.Copy, scale=16.0)
+    quant("qx", 0, 128, "xt", "xt", "qx")
+    act("zz khi", "num1", T.num[:, 1:16:2], T.zz[:, 0:8], AF.Identity, bias=T.pc[:, 0:1])
+    act("pm", "a0", T.pc[:, 1:2], T.pf[:, 0:1], AF.Identity, bias=16.0)
+    act("pm", "a1c", T.pc[:, 2:3], T.pf[:, 0:1], AF.Identity, bias=32.0)
+    act("pm", "a65", T.pc[:, 4:5], T.pf[:, 0:1], AF.Identity, bias=65.0)
+    ts("crow p31", "thr0", T.thr[:, 0:32], T.crow[:], T.pf[:, 2:3], tiny, OP.is_lt, OP.mult)
+    fill("", "thr1", T.thr[:, 32:64], 0.0)
+    fill("", "kk", T.t2[:, 96:97], 16.0 - KM + 0.5)
+    fill("", "t10", T.t1[0:32, 32:64], 0.0)
+    fill("", "t20", T.t2[0:32, 64:96], 0.0)
+    fill("thr1", "thr2", T.thr[96:128, 32:64], tiny)
+    fill("kk", "kk", T.t2[0:32, 96:97], 1000.0)
+    ts("ri", "qh", T.qh[:, 0:15], T.ri[:, 0:15], -0.5, None, OP.add)
+    quant("qtri", 0, 128, "ct", "ctri cid ct", "qtri")
+    fill("", "ztb", T.ztb[:], 0.0)
+    fill("", "att", T.att[:], 0.0)
+    ts("p31", "hp", T.pc[:, 3:4], T.pf[:, 2:3], 15.5, float(r % 2), OP.is_gt, OP.is_equal)
+
+    fill("", "et", T.et[:], 0.0)
+    act("ident et", "e", T.et[:, 4:516:4], T.ident[:], AF.Copy, scale=0.5)
+    act("row8 pm", "jw", T.jw[:], T.row8[:], AF.Identity, scale=16.0, bias=T.pf[:, 0:1])
+    act("jw", "jn", T.jn[:], T.jw[:], AF.Identity, scale=-1.0, bias=144.0)
+    quant("slots", 128, 128, "zz", "zz", "slz")
+    quant("pk", 64, 128, "zz", "zz", "pkz")
+
+    best, q2, d16, u, o1, st2, st, pl, ph, q32, gn, mn, mgc = [T.sc[:, i:i + 1] for i in range(13)]
+    M = T.R[:, 255:256]
+    mm(0, "qx", 0, "anc", 128, "qx anc ancown ancowns ancpad ancpads")
+    mm(1, "qx", 0, "anc", 160, "qx anc ancown ancowns ancpad ancpads", xv=128)
+    op("V", "ps0 zz", "R0", V.tensor_tensor_scan, T.R[:, 0:128], T.ps0[:, 0:128], T.zz[:, 0:128], -9.0e29, OP.max, OP.add)
+    op("V", "ps1 zz R0", "R", V.tensor_tensor_scan, T.R[:, 128:288], T.ps1[:, 0:160], T.zz[:, 0:160], T.R[:, 127:128],
+       OP.max, OP.add)
+    op("V", "R", "m0", V.transpose, T.mrow[:], T.R[:, 256:288])
+
+    def quad(t, q, c):
+        return T[t][32 * q:32 * q + 32, c:c + 32]
+
+    ts("R m0", "t1a", T.t1[:, 0:32], T.mrow[:], M, -1.0, OP.subtract, OP.mult)
+    for a in range(1, 4):
+        Ma = T.R[32 * a:32 * a + 32, 255:256]
+        b = a % 3 + 1
+        act("R m0", "t1%d" % a, quad("t1", a, 32), quad("mrow", b, 0), AF.Identity, scale=-1.0, bias=Ma)
+        b = (a + 1) % 3 + 1
+        ts("R m0", "t2%d" % a, quad("t2", a, 64), quad("mrow", b, 0), Ma, None, OP.is_ge if b < a else OP.is_gt)
+    act("R", "best jr", T.jr[:], T.R[:, 0:256], AF.Sign, bias=M, scale=-1.0, accum_out=best)
+    act("best qc0 qc1 qc2 qc3", "ab", T.ab[:], T.qc[:], AF.Abs, bias=best, scale=-1.0)
+    act("best qh", "q2 j7", T.j7[:, 0:15], T.qh[:, 0:15], AF.Sign, bias=best, scale=-1.0, accum_out=q2)
+    act("ab", "pen", T.pen[:], T.ab[:], AF.Relu, scale=-2.0, bias=32.0)
+    act("q2 best", "d16", d16, q2, AF.Identity, bias=best, scale=-16.0)
+    act("pen", "msk", T.msk[:], T.pen[:], AF.Sign)
+    act("d16 zz", "num2", T.num[:, 16:32:2], T.zz[:, 0:8], AF.Identity, bias=d16)
+    tt("t1a t11 t12 t13 t10 thr0 thr1 thr2", "t2", T.t2[:, 0:64], T.t1[:], T.thr[:], OP.is_lt)
+    op("V", "t2 t20 t21 t22 t23 kk", "u", V.tensor_reduce, u, T.t2[:], X, OP.add)
+    ts("ab u ztb", "ztv", T.ztb[:, 96:128:2], T.ab[:, 0:16], u, 16.0, OP.max, OP.is_lt)
+    quant("qz", 0, 128, "ztb", "ztv ztb", "qz", at=96)
+    mm(1, "qtri", 0, "qz", 128, "qtri qz")
+    tt("msk num0 num1 num2 num3 att", "bt", T.att[:, 512:576:2], T.msk[:], T.num[:], OP.mult)
+    op("V", "ps1", "o1", V.tensor_reduce, o1, T.ps1[:, 0:8], X, OP.max)
+    ts("pm1 o1 att", "at0", T.att[:, 0:512:2], T.pm1[:], o1, None, OP.is_equal)
+    quant("qab", 0, 144, "att", "att at0 bt", "qab")
+    mm(2, "qab", 0, "qab", 128, "qab", xv=16)
+
+    ts("ps2 hp", "lst", T.lst[:], T.ps2[:, 120:128], T.pc[:, 3:4], None, OP.mult)
+    cp("ps2", "off", T.off[:], T.ps2[:, 112:120])
+    to_each("lst", lambda c: T.lst[:, c:c + 1], T.landL[:, 4 * r:4 * r + 1], "l2", "o2a")
+    pick("snd", 0, 128, "qx", 128, "off", 0, 8, "qx off", "snd")
+    half = CAPP * N // 2
+    to_two("snd", [T.snd[:, half:].bitcast(dt.uint8), T.snd[:, 0:half].bitcast(dt.uint8)], T.rl[:].bitcast(dt.uint8),
+           "rc", "o2b", (0, 1))
+    to_two("snds", [T.snds[:, half:], T.snds[:, 0:half]], T.rms[:], "rp", "o2c", (2, 3))
+    arrive("l2", N - 1, "landL")
+    arrive("c2r", 4 * (N - 1), "slots")
+    pick("slots", CAPP * r, CAPP * r + CAPP, "qx", 128, "off", 0, 1, "qx off", "slown")
+    act("lst", "lown", T.landL[:, 4 * r:4 * r + 1], T.lst[:, 0:1], AF.Copy)
+
+    for b in range(4):
+        quant("qe", 128 * b, 128, "et", "et e", "qe%d" % b, at=4 - b)
+        mm(4 + b, "qe", 128 * b, "qn", 128, "qe%d qn" % b, stop=False)
+    fill("", "aw", T.aw[:], 0.0)
+    fill("", "mz", T.mz[:, 4 * A:512], 0.0)
+    quant("qw", 0, 512, "wt", "wt", "qw")
+    ts("row8 ph16", "m8", T.m8[:], T.row8[:], T.pf[:, 1:2], None, OP.is_equal)
+    ts("row16 ph16", "m16", T.m16[:], T.row16[:], T.pf[:, 1:2], None, OP.is_equal)
+    fill("", "ct2", T.ct2[:], 0.0)
+
+    for c in range(4):
+        la, lb = T.landL[:, 8 * c:8 * c + 1], T.landL[:, 8 * c + 4:8 * c + 5]
+        if c < 2:
+            ts("landL lown zz", "lx%d" % c, T.lx[:, 32 * c:32 * c + 32], T.zz[:, 0:32], la, lb, OP.add, OP.add)
+        else:
+            act("landL lown ones", "lx%d" % c, T.lx[:, 32 * c:32 * c + 32], T.ones[:, 0:32], AF.Identity, bias=lb, scale=la)
+    op("V", "lx0 lx1 lx2 lx3", "arow", V.transpose, T.arow[:], T.lx[:])
+    H = [slice(0, 128), slice(128, 256)]
+    for h in range(2):
+        ts("arow a0 a1c", "eq%d" % h, T.eq[:, H[h]], T.arow[:], T.pc[:, 1 + h:2 + h], None, OP.is_equal)
+    for h in range(2):
+        op("V", "ones eq%d" % h, "cc%d" % h, V.tensor_tensor_scan, T.cc[:, H[h]], T.ones[:], T.eq[:, H[h]], 0.0, OP.mult, OP.add)
+        act("cc%d" % h, "F%d j%d" % (h, h), T.j12[:, H[h]], T.cc[:, H[h]], AF.Relu, bias=1.0, scale=-1.0,
+            accum_out=T.F4[:, h:h + 1])
+    for h in range(2):
+        ts("cc%d" % h, "c2%d" % h, T.c2[:, H[h]], T.cc[:, H[h]], 1.5, None, OP.is_lt)
+    for h in range(2):
+        op("V", "c2%d" % h, "F%d" % (2 + h), V.tensor_reduce, T.F4[:, 2 + h:3 + h], T.c2[:, H[h]], X, OP.add)
+    ts("F0 F1 F2 F3", "n1", T.n1[:], T.F4[:], 127.5, None, OP.is_gt)
+    cp("F0 F1 F2 F3", "fs", T.fs[:], T.F4[:])
+    tt("n1 jw", "n2", T.n2[:], T.n1[:], T.jw[:, 0:4], OP.mult)
+    tt("n2 F0 F1 F2 F3", "n3", T.n3[:], T.n2[:], T.F4[:], OP.add)
+    cp("n3", "sof", T.sof[:], T.n3[:])
+    cp("sof ones aw", "aws", T.aw[:, 0:192].indirect(T.sof[:, 0:4]), T.ones[:, 0:64])
+    op("V", "aws", "at", V.transpose, T.at[:], T.aw[:, 0:128])
+    cp("at", "adm4", T.adm4[:, 0:4], T.at[:, 0:128:32])
+    to_all("adm4", T.adm4[:, 0:4], T.land3[:, 8 * r:8 * r + 4], "m3", "o3a")
+
+    pick("pk", 0, 64, "slots", 256, "fs", 0, 4, "slots slown slowns slz fs", "pk")
+    for b in range(4):
+        mm(4 + b, "qe", 128 * b, "pk", 128, "qe%d pk pks pkz" % b, start=False)
+    ts("o1", "st2", st2, o1, 64.0 + CAPP + 0.5, None, OP.is_lt)
+    ts("q2", "q32", q32, q2, 16.0, -16.0, OP.mult, OP.add)
+    ts("q2 best", "gn", gn, q2, 48.0, best, OP.mult, OP.add)
+    ts("o1 st2", "st", st, o1, 64.5, st2, OP.is_gt, OP.mult)
+    for b in range(4):
+        src, tb = T["ps%d" % (4 + b)], T.tb[:, 32 * b:32 * b + 32]
+        if b < 3:
+            act("ps%d" % (4 + b), "tb%d" % b, tb, src[:, A:2 * A], AF.Copy)
+        else:
+            cp("ps%d" % (4 + b), "tb%d" % b, tb, src[:, A:2 * A])
+        tt("ps%d tb%d" % (4 + b, b), "mt%d" % b, T.mz[:, b:4 * A:4], src[:, 0:A], tb, OP.add)
+    quant("km", 0, 128, "mz", "mz mt0 mt1 mt2 mt3", "km")
+    ts("o1 st", "pl", pl, o1, -65.0, st, OP.add, OP.mult)
+    ts("q32 st", "ph", ph, q32, 16.0 * (r % 2) - 256.0, st, OP.add, OP.mult)
+    ts("gn", "gn", gn, gn, -47.0, None, OP.add)
+    for i in range(4):
+        mm(i, "qw", 128 * i, "km", 128, "qw km")
+        layer(i, "mz", 512, A, "ht%d" % i, True)
+    quant("hq", 0, 128, "mz", "mz ht0 ht1 ht2 ht3", "hq", at=128)
+
+    n0 = 128 - A
+    to_two("hq", [T.hqs[:, n0:128]] * 2, T.rhs[:], "rk", "o3c", (2, 3))
+    to_all("hq", T.hq[:, n0:128].bitcast(dt.uint8), T.hw[:, 128 + A * r:128 + A * r + A].bitcast(dt.uint8), "h3", "o3b")
+    arrive("m3", width * (N - 1), "land3")
+    arrive("h3", 2 * width * (N - 1), "hwr")
+    ts("ph", "ph", ph, ph, 256.0, None, OP.add)
+    ts("pm1 a65 ct2", "ca", T.ct2[:, 0:512:2], T.pm1[:], T.pc[:, 4:5], None, OP.is_equal)
+    for k, (c, n, m, sc, rd) in enumerate(((64, 8, "m8", d16, "d16"), (66, 8, "m8", q32, "q32"),
+                                           (0, 16, "m16", pl, "pl"), (2, 16, "m16", ph, "ph"))):
+        act(m + " ztb " + rd, "w%d" % k, T.ztb[:, c:c // 32 * 32 + 4 * n:4], T[m][:], AF.Copy, scale=sc)
+    quant("qa2", 0, 128, "ct2", "ct2 ca", "qa2")
+    cp("at", "adown", T.land3[:, 8 * r:8 * r + 4], T.at[:, 0:128:32])
+    ts("F0 F1", "jf0", T.jf[:, 0:2], T.F4[:, 0:2], 127.5, 128.0 + A * r, OP.is_lt, OP.mult)
+    pick("hw", 128 + A * r, 128 + A * r + A, "hq", 128, "il", 0, 2, "hq il0 il1", "hwn", at=n0)
+    quant("qb2", 0, 128, "ztb", "ztb ztv w0 w1 w2 w3", "qb2")
+    mm(7, "qa2", 0, "qb2", 128, "qa2 qb2")
+    for q in range(N):
+        col = T.land3[:, 8 * q + r // 2:8 * q + r // 2 + 1]
+        if q % 2:
+            ts("land3 adown ones", "ax%d" % q, T.ax[:, 32 * q:32 * q + 32], T.ones[:, 0:32], 0.0, col, OP.mult, OP.add)
+        else:
+            act("land3 adown zz", "ax%d" % q, T.ax[:, 32 * q:32 * q + 32], T.zz[:, 0:32], AF.Identity, bias=col)
+    for i in range(4):
+        mm(i, "qw", 128 * i, "qx", 128, "qw qx")
+        layer(i, "hot", 0, 128, "ho%d" % i, False)
+    cp("ps7", "posD", T.posD[:], T.ps7[:, 0:16])
+    op("V", " ".join("ax%d" % q for q in range(N)), "ar", V.transpose, T.ar[:, 0:256], T.ax[:])
+    fill("", "ar0", T.ar[:, 256:272], 0.0)
+    tt("ps7 jn", "tmp", T.tmp[:], T.ps7[:, 16:24], T.jn[:], OP.add)
+    cp("ar ar0 posD", "aj", T.aj[:], T.ar[:, 0:272].indirect(T.posD[:, 0:16]))
+    cp("jw", "jf2", T.jf[:, 2:8], T.jw[:, 2:8])
+    op("V", "aj", "ajt", V.transpose, T.ajt[:], T.aj[:])
+    tt("jf0 jw", "jf1", T.jf[:, 0:2], T.jf[:, 0:2], T.jw[:, 0:2], OP.add)
+    tt("ajt tmp", "f1", T.f1[:], T.ajt[:, 0:256:32], T.tmp[:], OP.mult)
+    tt("f1 jf1 jf2", "f2", T.f2[:], T.f1[:], T.jf[:], OP.add)
+    cp("f2", "fin", T.fin[:], T.f2[:])
+    quant("hw", 0, 128, "hot", "ho0 ho1 ho2 ho3", "hwo")
+    quant("qv", 0, 128, "vt", "vt", "qv")
+
+    pick("fo", 0, 128, "hw", 384, "fin", 0, 8, "hwo hwr hwn hwns fin", "fo")
+    mm(4, "qv", 0, "fo", 128, "qv fo fos")
+    dma("S", "fo", "oco", T.oc[:], T.fo[:].bitcast(dt.uint8))
+    for k in range(4):
+        dma("A", "fos", "osco%d" % k, T.osc[4 * k:4 * k + 4, :], T.fos[32 * k:32 * k + 4, :])
+    tt("ajt m8", "mw2", T.mw2[:], T.ajt[:, 0:256:32], T.m8[:], OP.mult)
+    op("V", "mw2", "mn", V.tensor_reduce, mn, T.mw2[:], X, OP.add)
+    cp("ps4", "yo", T.yo[:], T.ps4[:, 0:128])
+    dma("S", "yo", "yout", T.y[:], T.yo[:])
+    ts("mn gn", "mgc", mgc, mn, gn, -1.0, OP.mult, OP.add)
+    dma("S", "mgc", "mgo", T.mg[:], mgc)
+    for s, v in count.items():
+        if known["S"].get(s, 0) < v:
+            SY.wait_ge(S[s], v)

@@ -19,28 +19,27 @@ for _n, _c in (("qx", 128), ("qn", 128), ("anc", 288), ("qtri", 128), ("qa2", 12
                ("hq", 128), ("hw", 384), ("fo", 128)):
     _mx(_n, _c)
 _buf("rl", 64, MXC)
-_buf("rms", 64, U8)
 _buf("rhs", 32, U8)
+_buf("ras", 32, U8)
 for _n, _c in (("xt", 512), ("xa", 512), ("wt", 2048), ("vt", 512), ("ct", 512), ("ct2", 512), ("et", 516), ("ztb", 608),
                ("att", 576), ("zz", 512), ("mz", 640), ("hot", 512), ("ones", 128), ("ident", 128),
                ("tri", 128), ("pm1", 256), ("lx", 128), ("arow", 128), ("eq", 256), ("cc", 256), ("c2", 256),
-               ("j12", 256), ("aw", 192), ("at", 128), ("adm4", 8), ("land3", 64), ("ax", 256), ("ar", 272), ("aj", 256),
-               ("ajt", 256)):
+               ("j12", 256), ("ax", 256), ("ar", 256), ("aj", 256), ("ajt", 256)):
     _buf(_n, _c, BF)
 for _n, _c in (("R", 288), ("mrow", 32), ("thr", 64), ("t1", 64), ("t2", 97), ("sc", 16), ("jr", 256),
                ("j7", 16), ("ab", 32), ("pen", 32), ("msk", 32), ("num", 32), ("qi", 8), ("qc", 32), ("ri", 16), ("qh", 16),
                ("crow", 32), ("row8", 8), ("row16", 16), ("pf", 4), ("pc", 8), ("m8", 8), ("m16", 16), ("jw", 8), ("jn", 8),
-               ("lst", 8), ("landL", 32), ("F4", 4), ("tb", 128), ("n1", 4), ("n2", 4), ("n3", 4), ("tmp", 8),
-               ("jf", 8), ("f1", 8), ("f2", 8), ("mw2", 8), ("yo", 128)):
+               ("lst", 8), ("landL", 32), ("F4", 4), ("tb", 128), ("tmp", 8), ("lohi", 4), ("sec", 4), ("land3", 32),
+               ("sl", 8), ("adm", 8), ("jf", 8), ("f1", 8), ("f2", 8), ("mw2", 8), ("yo", 128)):
     _buf(_n, _c, F32)
-for _n, _c in (("il", 2), ("off", 8), ("fs", 4), ("sof", 4), ("posD", 16), ("fin", 8)):
+for _n, _c in (("il", 2), ("off", 8), ("fs", 4), ("posD", 16), ("fin", 8)):
     _buf(_n, _c, U16)
 _buf("pi", 1, I32)
 _buf("pin", 4, I32)
 for _i in range(8):
     SCRATCH["ps%d" % _i] = ("psum", [128, 512], F32)
 SEMAPHORES = (["cV", "cA", "cP", "cG", "a1", "o1s", "l2", "c2r", "o2a", "o2b", "o2c", "m3", "o3a", "h3", "o3b", "o3c",
-               "rc", "rp", "rk", "hl"] + ["d%d" % _i for _i in range(12)])
+               "ra", "rc", "rk", "hl"] + ["d%d" % _i for _i in range(12)])
 
 
 def to(topo, c):
@@ -55,31 +54,28 @@ def plan(own, r, T, topo):
     near, far = [T.cores[q] for q in order[1:4]], [T.cores[q] for q in order[4:]]
     rest = sorted([c for c in topo.cores_of(own) if c != own], key=lambda c: topo.die(c) == topo.die(own))
     f = [c for c in rest if all(topo.may_write(c, d) for d in far)][:2]
-    n = [c for c in rest if c not in f and all(topo.may_write(c, d) for d in near)][:2]
-    return order, near, far, [f[0], n[0], f[1], n[1]]
+    n = [c for c in rest if c not in f and all(topo.may_write(c, d) for d in near)]
+    return order, near, far, [f[0], n[0]]
 
 
 def hand_on(g, core, r, role, near, far, T, topo):
     S, CAPP, A = T.sem, 16, 32
-    goal, first = (near, 1) if role % 2 else (far, 0)
+    goal, first = (near, 1) if role else (far, 0)
     eng = topo.engines(core, goal[0])
-
-    def piece(i):
-        a = CAPP * (i + first)
-        return T.rms[:, a:a + CAPP] if role >= 2 else T.rl[:, a:a + CAPP].bitcast(dt.uint8)
-
-    land = T.slotss[:, CAPP * r:CAPP * r + CAPP] if role >= 2 else T.slots[:, CAPP * r:CAPP * r + CAPP].bitcast(dt.uint8)
-    g.wait_ge(S.rp if role >= 2 else S.rc, 4)
+    g.wait_ge(S.ra, 4)
+    g.remote_dma_fused([RemoteDMATransfer(dst_ids=[to(topo, goal[0])], dma_engine_mask=topo.mask(core, goal[0]),
+                                          remote_sem=S.a1, src=T.ras[:, 0:A], dst=T.ancs[:, A * r:A * r + A])], local_sem=S.hl)
+    g.wait_ge(S.rc, 4)
     g.remote_dma_fused([RemoteDMATransfer(dst_ids=[to(topo, d)], dma_engine_mask=1 << eng[2 * i] | 1 << eng[2 * i + 1],
-                                          remote_sem=S.c2r, src=piece(i), dst=land) for i, d in enumerate(goal)], local_sem=S.hl)
-    n = 2 * len(goal)
-    if role >= 2:
-        g.wait_ge(S.rk, 4)
-        g.remote_dma_fused([RemoteDMATransfer(dst_ids=[to(topo, d) for d in goal], dma_engine_mask=topo.mask(core, goal[0]),
-                                              remote_sem=S.h3, srcs=[T.rhs[:, 0:A]],
-                                              dsts=[T.hws[:, 128 + A * r:128 + A * r + A]] * len(goal))], local_sem=S.hl)
-        n += len(eng)
-    g.wait_ge(S.hl, n)
+                                          remote_sem=S.c2r,
+                                          src=T.rl[:, CAPP * (i + first):CAPP * (i + first + 1)].bitcast(dt.uint8),
+                                          dst=T.slots[:, CAPP * r:CAPP * r + CAPP].bitcast(dt.uint8))
+                        for i, d in enumerate(goal)], local_sem=S.hl)
+    g.wait_ge(S.rk, 4)
+    g.remote_dma_fused([RemoteDMATransfer(dst_ids=[to(topo, d) for d in goal], dma_engine_mask=topo.mask(core, goal[0]),
+                                          remote_sem=S.h3, srcs=[T.rhs[:, 0:A]],
+                                          dsts=[T.hws[:, 128 + A * r:128 + A * r + A]] * len(goal))], local_sem=S.hl)
+    g.wait_ge(S.hl, 2 * len(goal) + 2 * len(eng))
 
 
 def rank_program(g, core, T, topo):
@@ -89,10 +85,10 @@ def rank_program(g, core, T, topo):
     if not mine:
         return
     r = T.rank_of(mine[0])
-    order, near, far, help4 = plan(mine[0], r, T, topo)
+    order, near, far, aides = plan(mine[0], r, T, topo)
     if core != mine[0]:
-        if core in help4:
-            hand_on(g, core, r, help4.index(core), near, far, T, topo)
+        if core in aides:
+            hand_on(g, core, r, aides.index(core), near, far, T, topo)
         return
     OP, AF, X = AluOpType, ActivationFunctionType, AxisListType.X
     V, AC, PE, SY = g.vector, g.scalar, g.tensor, g.sync
@@ -107,7 +103,7 @@ def rank_program(g, core, T, topo):
         for k in list(wr) + [k for k in rd if k.startswith("ps")]:
             if k in writer:
                 need.append(writer[k])
-            need += readers.get(k, [])
+            need += [t for t in readers.get(k, []) if k in wr or t[0] != "c" + q]
         best = {}
         for s, v, clk in need:
             if known[q].get(s, 0) < v and best.get(s, (0,))[0] < v:
@@ -150,18 +146,22 @@ def rank_program(g, core, T, topo):
         count[s] = n
         after((s, n, {}), [], wr.split())
 
+    def left(s):
+        SY.wait_ge(S[s], count[s])
+        known["S"][s] = count[s]
+
     others = [T.cores[q] for q in order[1:]]
     allm = topo.mask(core, others[0])
     for c in others:
         allm &= topo.mask(core, c)
     eng = [e for e in topo.engines(core, others[0]) if allm >> e & 1]
     width = len(eng)
-    side = [e for e in topo.engines(core, help4[0]) if e not in eng]
+    side = [e for e in topo.engines(core, aides[0]) if e not in eng]
 
-    def to_all(rd, src, dstap, sem, loc):
+    def to_all(rd, src, dstap, sem, loc, goal=others):
         before("G", rd.split(), [])
-        g.remote_dma_fused([RemoteDMATransfer(dst_ids=[to(topo, c) for c in others], dma_engine_mask=allm, remote_sem=S[sem],
-                                              srcs=[src], dsts=[dstap] * len(others))], local_sem=S[loc])
+        g.remote_dma_fused([RemoteDMATransfer(dst_ids=[to(topo, c) for c in goal], dma_engine_mask=allm, remote_sem=S[sem],
+                                              srcs=[src], dsts=[dstap] * len(goal))], local_sem=S[loc])
         count[loc] = count.get(loc, 0) + width
 
     def to_each(rd, src, dstap, sem, loc):
@@ -171,14 +171,14 @@ def rank_program(g, core, T, topo):
                            local_sem=S[loc])
         count[loc] = count.get(loc, 0) + N - 1
 
-    def to_two(rd, src, dstap, sem, loc, roles):
+    def to_side(rd, src, dstap, sem, loc):
         before("G", rd.split(), [])
-        h = len(side) // 2
-        g.remote_dma_fused([RemoteDMATransfer(dst_ids=[to(topo, help4[k])],
+        h = len(side) // len(aides)
+        g.remote_dma_fused([RemoteDMATransfer(dst_ids=[to(topo, c)],
                                               dma_engine_mask=sum(1 << e for e in side[h * i:h * i + h]),
-                                              remote_sem=S[sem], src=src[i], dst=dstap) for i, k in enumerate(roles)],
+                                              remote_sem=S[sem], src=src[i], dst=dstap) for i, c in enumerate(aides)],
                            local_sem=S[loc])
-        count[loc] = count.get(loc, 0) + 2 * h
+        count[loc] = count.get(loc, 0) + len(aides) * h
 
     def ts(rd, wr, out, in0, s1, s2, *ops):
         op("V", rd, wr, V.tensor_scalar, out, in0, s1, s2, *ops)
@@ -227,20 +227,19 @@ def rank_program(g, core, T, topo):
     ts("pi", "pin", T.pin[:, 0:1], T.pi[:], 15, None, OP.bitwise_and)
     quant("qn", 0, 128, "xa", "xa xaz", "qn")
 
+    to_side("qn", [T.qns[:, 0:A]] * 2, T.ras[:], "ra", "o1s")
     to_all("qn", T.qn[:, 0:A].bitcast(dt.uint8), T.anc[:, A * r:A * r + A].bitcast(dt.uint8), "a1", "o1s")
-    to_all("qn", T.qns[:, 0:A], T.ancs[:, A * r:A * r + A], "a1", "o1s")
+    to_all("qn", T.qns[:, 0:A], T.ancs[:, A * r:A * r + A], "a1", "o1s", near[1:] + far[1:])
     arrive("a1", 2 * width * (N - 1), "anc")
-    SY.wait_ge(S.o1s, 2 * width)
-    known["S"]["o1s"] = 2 * width
+    left("o1s")
     dma("S", "", "wt", T.wt[:], T.w[:])
-    dma("S", "", "vt", T.vt[:], T.v[:])
 
     op("G", "ones", "ident", g.affine_select, T.ident[:], T.ones[:], [[1, 128]], OP.is_equal, 0.0, 0, -1)
     iota("ri", T.ri[:, 0:15], [[A, 15]], -7 * A)
     iota("crow", T.crow[:], [[1, 32]])
-    iota("pm1", T.pm1[:], [[0, 8], [1, 16], [0, 2]], 65)
     iota("row8", T.row8[:], [[1, 8]])
     iota("row16", T.row16[:], [[1, 8], [0, 2]])
+    iota("pm1", T.pm1[:], [[0, 8], [1, 16], [0, 2]], 65)
     for k in range(4):
         act("qi", "qc%d" % k, T.qc[:, k // 2 * 16 + k % 2:k // 2 * 16 + 16:2], T.qi[:], AF.Identity, bias=0.5 * A - 0.5)
     act("zz", "num3", T.num[:, 17:32:2], T.zz[:, 0:8], AF.Identity, bias=32.0)
@@ -252,45 +251,53 @@ def rank_program(g, core, T, topo):
     ts("pi", "pin1", T.pin[:, 1:2], T.pi[:], 4, None, OP.arith_shift_right)
     ts("pi", "pin2", T.pin[:, 2:3], T.pi[:], 31, None, OP.bitwise_and)
     cp("pin", "pm", T.pf[:, 0:1], T.pin[:, 0:1])
+    fill("", "et", T.et[:], 0.0)
     cp("pin1", "ph16", T.pf[:, 1:2], T.pin[:, 1:2])
     cp("pin2", "p31", T.pf[:, 2:3], T.pin[:, 2:3])
     act("tri ct", "ctri", T.ct[:, 0:512:4], T.tri[:], AF.Copy)
-    act("ident ct", "cid", T.ct[:, 2:512:4], T.ident[:], AF.Copy, scale=64.0)
     act("zz pm", "num0", T.num[:, 0:16:2], T.zz[:, 0:8], AF.Identity, bias=T.pf[:, 0:1])
     act("ph16", "khi", T.pc[:, 0:1], T.pf[:, 1:2], AF.Copy, scale=16.0)
     quant("qx", 0, 128, "xt", "xt", "qx")
-    act("zz khi", "num1", T.num[:, 1:16:2], T.zz[:, 0:8], AF.Identity, bias=T.pc[:, 0:1])
     act("pm", "a0", T.pc[:, 1:2], T.pf[:, 0:1], AF.Identity, bias=16.0)
     act("pm", "a1c", T.pc[:, 2:3], T.pf[:, 0:1], AF.Identity, bias=32.0)
     act("pm", "a65", T.pc[:, 4:5], T.pf[:, 0:1], AF.Identity, bias=65.0)
-    ts("crow p31", "thr0", T.thr[:, 0:32], T.crow[:], T.pf[:, 2:3], tiny, OP.is_lt, OP.mult)
+    act("zz khi", "num1", T.num[:, 1:16:2], T.zz[:, 0:8], AF.Identity, bias=T.pc[:, 0:1])
+    act("ident ct", "cid", T.ct[:, 2:512:4], T.ident[:], AF.Copy, scale=64.0)
+    act("ident et", "e", T.et[:, 4:516:4], T.ident[:], AF.Copy, scale=0.5)
     fill("", "thr1", T.thr[:, 32:64], 0.0)
     fill("", "kk", T.t2[:, 96:97], 16.0 - KM + 0.5)
     fill("", "t10", T.t1[0:32, 32:64], 0.0)
     fill("", "t20", T.t2[0:32, 64:96], 0.0)
+    fill("", "ztb", T.ztb[:], 0.0)
     fill("thr1", "thr2", T.thr[96:128, 32:64], tiny)
     fill("kk", "kk", T.t2[0:32, 96:97], 1000.0)
-    ts("ri", "qh", T.qh[:, 0:15], T.ri[:, 0:15], -0.5, None, OP.add)
-    quant("qtri", 0, 128, "ct", "ctri cid ct", "qtri")
-    fill("", "ztb", T.ztb[:], 0.0)
     fill("", "att", T.att[:], 0.0)
     ts("p31", "hp", T.pc[:, 3:4], T.pf[:, 2:3], 15.5, float(r % 2), OP.is_gt, OP.is_equal)
-
-    fill("", "et", T.et[:], 0.0)
-    act("ident et", "e", T.et[:, 4:516:4], T.ident[:], AF.Copy, scale=0.5)
-    act("row8 pm", "jw", T.jw[:], T.row8[:], AF.Identity, scale=16.0, bias=T.pf[:, 0:1])
-    act("jw", "jn", T.jn[:], T.jw[:], AF.Identity, scale=-1.0, bias=144.0)
+    ts("p31", "lo", T.lohi[:, 0:1], T.pf[:, 2:3], 15.5, None, OP.is_lt)
+    ts("p31", "hi", T.lohi[:, 1:2], T.pf[:, 2:3], 15.5, None, OP.is_gt)
     quant("slots", 128, 128, "zz", "zz", "slz")
     quant("pk", 64, 128, "zz", "zz", "pkz")
+    fill("", "mz", T.mz[:, 4 * A:512], 0.0)
+    fill("", "ct2", T.ct2[:], 0.0)
+    quant("qtri", 0, 128, "ct", "ctri cid ct", "qtri")
+    ts("ri", "qh", T.qh[:, 0:15], T.ri[:, 0:15], -0.5, None, OP.add)
+    ts("crow p31", "thr0", T.thr[:, 0:32], T.crow[:], T.pf[:, 2:3], tiny, OP.is_lt, OP.mult)
+
+    for b in range(4):
+        quant("qe", 128 * b, 128, "et", "et e", "qe%d" % b, at=4 - b)
+        mm(4 + b, "qe", 128 * b, "qn", 128, "qe%d qn" % b, stop=False)
+    act("row8 pm", "jw", T.jw[:], T.row8[:], AF.Identity, scale=16.0, bias=T.pf[:, 0:1])
+    act("jw", "jn", T.jn[:], T.jw[:], AF.Identity, scale=-1.0, bias=144.0)
+    act("jw", "jf2", T.jf[:, 2:8], T.jw[:, 2:8], AF.Copy)
+    ts("row8 ph16", "m8", T.m8[:], T.row8[:], T.pf[:, 1:2], None, OP.is_equal)
+    ts("row16 ph16", "m16", T.m16[:], T.row16[:], T.pf[:, 1:2], None, OP.is_equal)
 
     best, q2, d16, u, o1, st2, st, pl, ph, q32, gn, mn, mgc = [T.sc[:, i:i + 1] for i in range(13)]
     M = T.R[:, 255:256]
-    mm(0, "qx", 0, "anc", 128, "qx anc ancown ancowns ancpad ancpads")
-    mm(1, "qx", 0, "anc", 160, "qx anc ancown ancowns ancpad ancpads", xv=128)
-    op("V", "ps0 zz", "R0", V.tensor_tensor_scan, T.R[:, 0:128], T.ps0[:, 0:128], T.zz[:, 0:128], -9.0e29, OP.max, OP.add)
-    op("V", "ps1 zz R0", "R", V.tensor_tensor_scan, T.R[:, 128:288], T.ps1[:, 0:160], T.zz[:, 0:160], T.R[:, 127:128],
-       OP.max, OP.add)
+    mm(0, "qx", 0, "anc", 288, "qx anc ancown ancowns ancpad ancpads")
+    op("V", "ps0 zz", "R", V.tensor_tensor_scan, T.R[:], T.ps0[:, 0:288], T.zz[:, 0:288], -9.0e29, OP.max, OP.add)
     op("V", "R", "m0", V.transpose, T.mrow[:], T.R[:, 256:288])
+    act("R", "best jr", T.jr[:], T.R[:, 0:256], AF.Sign, bias=M, scale=-1.0, accum_out=best)
 
     def quad(t, q, c):
         return T[t][32 * q:32 * q + 32, c:c + 32]
@@ -302,13 +309,14 @@ def rank_program(g, core, T, topo):
         act("R m0", "t1%d" % a, quad("t1", a, 32), quad("mrow", b, 0), AF.Identity, scale=-1.0, bias=Ma)
         b = (a + 1) % 3 + 1
         ts("R m0", "t2%d" % a, quad("t2", a, 64), quad("mrow", b, 0), Ma, None, OP.is_ge if b < a else OP.is_gt)
-    act("R", "best jr", T.jr[:], T.R[:, 0:256], AF.Sign, bias=M, scale=-1.0, accum_out=best)
     act("best qc0 qc1 qc2 qc3", "ab", T.ab[:], T.qc[:], AF.Abs, bias=best, scale=-1.0)
     act("best qh", "q2 j7", T.j7[:, 0:15], T.qh[:, 0:15], AF.Sign, bias=best, scale=-1.0, accum_out=q2)
     act("ab", "pen", T.pen[:], T.ab[:], AF.Relu, scale=-2.0, bias=32.0)
     act("q2 best", "d16", d16, q2, AF.Identity, bias=best, scale=-16.0)
     act("pen", "msk", T.msk[:], T.pen[:], AF.Sign)
     act("d16 zz", "num2", T.num[:, 16:32:2], T.zz[:, 0:8], AF.Identity, bias=d16)
+    act("q2", "q32", q32, q2, AF.Identity, scale=16.0, bias=-16.0)
+    act("q2 best", "gn", gn, q2, AF.Identity, scale=48.0, bias=best)
     tt("t1a t11 t12 t13 t10 thr0 thr1 thr2", "t2", T.t2[:, 0:64], T.t1[:], T.thr[:], OP.is_lt)
     op("V", "t2 t20 t21 t22 t23 kk", "u", V.tensor_reduce, u, T.t2[:], X, OP.add)
     ts("ab u ztb", "ztv", T.ztb[:, 96:128:2], T.ab[:, 0:16], u, 16.0, OP.max, OP.is_lt)
@@ -317,31 +325,37 @@ def rank_program(g, core, T, topo):
     tt("msk num0 num1 num2 num3 att", "bt", T.att[:, 512:576:2], T.msk[:], T.num[:], OP.mult)
     op("V", "ps1", "o1", V.tensor_reduce, o1, T.ps1[:, 0:8], X, OP.max)
     ts("pm1 o1 att", "at0", T.att[:, 0:512:2], T.pm1[:], o1, None, OP.is_equal)
+    ts("o1", "st2", st2, o1, 64.0 + CAPP + 0.5, None, OP.is_lt)
     quant("qab", 0, 144, "att", "att at0 bt", "qab")
     mm(2, "qab", 0, "qab", 128, "qab", xv=16)
+    ts("o1 st2", "st", st, o1, 64.5, st2, OP.is_gt, OP.mult)
+    act("m16 ztb d16", "w2", T.ztb[:, 0:64:4], T.m16[:], AF.Copy, scale=d16)
+    act("m16 ztb q32", "w3", T.ztb[:, 2:64:4], T.m16[:], AF.Copy, scale=q32)
+    act("gn", "gn", gn, gn, AF.Identity, bias=-47.0)
 
     ts("ps2 hp", "lst", T.lst[:], T.ps2[:, 120:128], T.pc[:, 3:4], None, OP.mult)
     cp("ps2", "off", T.off[:], T.ps2[:, 112:120])
     to_each("lst", lambda c: T.lst[:, c:c + 1], T.landL[:, 4 * r:4 * r + 1], "l2", "o2a")
     pick("snd", 0, 128, "qx", 128, "off", 0, 8, "qx off", "snd")
     half = CAPP * N // 2
-    to_two("snd", [T.snd[:, half:].bitcast(dt.uint8), T.snd[:, 0:half].bitcast(dt.uint8)], T.rl[:].bitcast(dt.uint8),
-           "rc", "o2b", (0, 1))
-    to_two("snds", [T.snds[:, half:], T.snds[:, 0:half]], T.rms[:], "rp", "o2c", (2, 3))
+    to_side("snd", [T.snd[:, half:].bitcast(dt.uint8), T.snd[:, 0:half].bitcast(dt.uint8)], T.rl[:].bitcast(dt.uint8),
+            "rc", "o2b")
+    to_each("snds", lambda c: T.snds[:, CAPP * c:CAPP * c + CAPP], T.slotss[:, CAPP * r:CAPP * r + CAPP], "c2r", "o2c")
+    left("o2b")
+    dma("S", "", "vt", T.vt[:], T.v[:])
     arrive("l2", N - 1, "landL")
-    arrive("c2r", 4 * (N - 1), "slots")
+    arrive("c2r", 3 * (N - 1), "slots")
+
+    quant("qw", 0, 512, "wt", "wt", "qw")
     pick("slots", CAPP * r, CAPP * r + CAPP, "qx", 128, "off", 0, 1, "qx off", "slown")
     act("lst", "lown", T.landL[:, 4 * r:4 * r + 1], T.lst[:, 0:1], AF.Copy)
-
-    for b in range(4):
-        quant("qe", 128 * b, 128, "et", "et e", "qe%d" % b, at=4 - b)
-        mm(4 + b, "qe", 128 * b, "qn", 128, "qe%d qn" % b, stop=False)
-    fill("", "aw", T.aw[:], 0.0)
-    fill("", "mz", T.mz[:, 4 * A:512], 0.0)
-    quant("qw", 0, 512, "wt", "wt", "qw")
-    ts("row8 ph16", "m8", T.m8[:], T.row8[:], T.pf[:, 1:2], None, OP.is_equal)
-    ts("row16 ph16", "m16", T.m16[:], T.row16[:], T.pf[:, 1:2], None, OP.is_equal)
-    fill("", "ct2", T.ct2[:], 0.0)
+    ts("o1 st", "pl", pl, o1, -65.0, st, OP.add, OP.mult)
+    ts("st", "ph", ph, st, float(CAPP * r) - 256.0, 256.0, OP.mult, OP.add)
+    ts("pm1 a65 ct2", "ca", T.ct2[:, 0:512:2], T.pm1[:], T.pc[:, 4:5], None, OP.is_equal)
+    for i in range(4):
+        mm(i, "qw", 128 * i, "qx", 128, "qw qx")
+        layer(i, "hot", 0, 128, "ho%d" % i, False)
+    quant("qa2", 0, 128, "ct2", "ct2 ca", "qa2")
 
     for c in range(4):
         la, lb = T.landL[:, 8 * c:8 * c + 1], T.landL[:, 8 * c + 4:8 * c + 5]
@@ -349,6 +363,8 @@ def rank_program(g, core, T, topo):
             ts("landL lown zz", "lx%d" % c, T.lx[:, 32 * c:32 * c + 32], T.zz[:, 0:32], la, lb, OP.add, OP.add)
         else:
             act("landL lown ones", "lx%d" % c, T.lx[:, 32 * c:32 * c + 32], T.ones[:, 0:32], AF.Identity, bias=lb, scale=la)
+    act("m8 ztb pl", "w0", T.ztb[:, 64:96:4], T.m8[:], AF.Copy, scale=pl)
+    act("m8 ztb ph", "w1", T.ztb[:, 66:96:4], T.m8[:], AF.Copy, scale=ph)
     op("V", "lx0 lx1 lx2 lx3", "arow", V.transpose, T.arow[:], T.lx[:])
     H = [slice(0, 128), slice(128, 256)]
     for h in range(2):
@@ -361,89 +377,64 @@ def rank_program(g, core, T, topo):
         ts("cc%d" % h, "c2%d" % h, T.c2[:, H[h]], T.cc[:, H[h]], 1.5, None, OP.is_lt)
     for h in range(2):
         op("V", "c2%d" % h, "F%d" % (2 + h), V.tensor_reduce, T.F4[:, 2 + h:3 + h], T.c2[:, H[h]], X, OP.add)
-    ts("F0 F1 F2 F3", "n1", T.n1[:], T.F4[:], 127.5, None, OP.is_gt)
+    quant("qb2", 0, 128, "ztb", "ztb ztv w0 w1 w2 w3", "qb2")
     cp("F0 F1 F2 F3", "fs", T.fs[:], T.F4[:])
-    tt("n1 jw", "n2", T.n2[:], T.n1[:], T.jw[:, 0:4], OP.mult)
-    tt("n2 F0 F1 F2 F3", "n3", T.n3[:], T.n2[:], T.F4[:], OP.add)
-    cp("n3", "sof", T.sof[:], T.n3[:])
-    cp("sof ones aw", "aws", T.aw[:, 0:192].indirect(T.sof[:, 0:4]), T.ones[:, 0:64])
-    op("V", "aws", "at", V.transpose, T.at[:], T.aw[:, 0:128])
-    cp("at", "adm4", T.adm4[:, 0:4], T.at[:, 0:128:32])
-    to_all("adm4", T.adm4[:, 0:4], T.land3[:, 8 * r:8 * r + 4], "m3", "o3a")
+    tt("F2 F3 lo hi", "sec", T.sec[:, 0:2], T.F4[:, 2:4], T.lohi[:, 0:2], OP.mult)
+    to_all("sec", T.sec[:, 0:2], T.land3[:, 4 * r:4 * r + 2], "m3", "o3a")
+    mm(3, "qa2", 0, "qb2", 128, "qa2 qb2")
 
     pick("pk", 0, 64, "slots", 256, "fs", 0, 4, "slots slown slowns slz fs", "pk")
     for b in range(4):
         mm(4 + b, "qe", 128 * b, "pk", 128, "qe%d pk pks pkz" % b, start=False)
-    ts("o1", "st2", st2, o1, 64.0 + CAPP + 0.5, None, OP.is_lt)
-    ts("q2", "q32", q32, q2, 16.0, -16.0, OP.mult, OP.add)
-    ts("q2 best", "gn", gn, q2, 48.0, best, OP.mult, OP.add)
-    ts("o1 st2", "st", st, o1, 64.5, st2, OP.is_gt, OP.mult)
+    act("sec", "adown", T.land3[:, 4 * r:4 * r + 2], T.sec[:, 0:2], AF.Copy)
+    ts("ps3", "posD", T.posD[:], T.ps3[:, 0:16], 16.0, None, OP.add)
+    tt("ps3 jn", "tmp", T.tmp[:], T.ps3[:, 0:16:2], T.jn[:], OP.add)
+    cp("ps3", "sl", T.sl[:], T.ps3[:, 16:24])
+    quant("hw", 0, 128, "hot", "ho0 ho1 ho2 ho3", "hwo")
     for b in range(4):
         src, tb = T["ps%d" % (4 + b)], T.tb[:, 32 * b:32 * b + 32]
-        if b < 3:
-            act("ps%d" % (4 + b), "tb%d" % b, tb, src[:, A:2 * A], AF.Copy)
-        else:
-            cp("ps%d" % (4 + b), "tb%d" % b, tb, src[:, A:2 * A])
+        act("ps%d" % (4 + b), "tb%d" % b, tb, src[:, A:2 * A], AF.Copy)
         tt("ps%d tb%d" % (4 + b, b), "mt%d" % b, T.mz[:, b:4 * A:4], src[:, 0:A], tb, OP.add)
     quant("km", 0, 128, "mz", "mz mt0 mt1 mt2 mt3", "km")
-    ts("o1 st", "pl", pl, o1, -65.0, st, OP.add, OP.mult)
-    ts("q32 st", "ph", ph, q32, 16.0 * (r % 2) - 256.0, st, OP.add, OP.mult)
-    ts("gn", "gn", gn, gn, -47.0, None, OP.add)
+    ts("F0 F1", "jf0", T.jf[:, 0:2], T.F4[:, 0:2], 127.5, 128.0 + A * r, OP.is_lt, OP.mult)
     for i in range(4):
         mm(i, "qw", 128 * i, "km", 128, "qw km")
         layer(i, "mz", 512, A, "ht%d" % i, True)
     quant("hq", 0, 128, "mz", "mz ht0 ht1 ht2 ht3", "hq", at=128)
 
     n0 = 128 - A
-    to_two("hq", [T.hqs[:, n0:128]] * 2, T.rhs[:], "rk", "o3c", (2, 3))
+    to_side("hq", [T.hqs[:, n0:128]] * 2, T.rhs[:], "rk", "o3c")
     to_all("hq", T.hq[:, n0:128].bitcast(dt.uint8), T.hw[:, 128 + A * r:128 + A * r + A].bitcast(dt.uint8), "h3", "o3b")
     arrive("m3", width * (N - 1), "land3")
     arrive("h3", 2 * width * (N - 1), "hwr")
-    ts("ph", "ph", ph, ph, 256.0, None, OP.add)
-    ts("pm1 a65 ct2", "ca", T.ct2[:, 0:512:2], T.pm1[:], T.pc[:, 4:5], None, OP.is_equal)
-    for k, (c, n, m, sc, rd) in enumerate(((64, 8, "m8", d16, "d16"), (66, 8, "m8", q32, "q32"),
-                                           (0, 16, "m16", pl, "pl"), (2, 16, "m16", ph, "ph"))):
-        act(m + " ztb " + rd, "w%d" % k, T.ztb[:, c:c // 32 * 32 + 4 * n:4], T[m][:], AF.Copy, scale=sc)
-    quant("qa2", 0, 128, "ct2", "ct2 ca", "qa2")
-    cp("at", "adown", T.land3[:, 8 * r:8 * r + 4], T.at[:, 0:128:32])
-    ts("F0 F1", "jf0", T.jf[:, 0:2], T.F4[:, 0:2], 127.5, 128.0 + A * r, OP.is_lt, OP.mult)
-    pick("hw", 128 + A * r, 128 + A * r + A, "hq", 128, "il", 0, 2, "hq il0 il1", "hwn", at=n0)
-    quant("qb2", 0, 128, "ztb", "ztb ztv w0 w1 w2 w3", "qb2")
-    mm(7, "qa2", 0, "qb2", 128, "qa2 qb2")
-    for q in range(N):
-        col = T.land3[:, 8 * q + r // 2:8 * q + r // 2 + 1]
-        if q % 2:
-            ts("land3 adown ones", "ax%d" % q, T.ax[:, 32 * q:32 * q + 32], T.ones[:, 0:32], 0.0, col, OP.mult, OP.add)
-        else:
-            act("land3 adown zz", "ax%d" % q, T.ax[:, 32 * q:32 * q + 32], T.zz[:, 0:32], AF.Identity, bias=col)
-    for i in range(4):
-        mm(i, "qw", 128 * i, "qx", 128, "qw qx")
-        layer(i, "hot", 0, 128, "ho%d" % i, False)
-    cp("ps7", "posD", T.posD[:], T.ps7[:, 0:16])
-    op("V", " ".join("ax%d" % q for q in range(N)), "ar", V.transpose, T.ar[:, 0:256], T.ax[:])
-    fill("", "ar0", T.ar[:, 256:272], 0.0)
-    tt("ps7 jn", "tmp", T.tmp[:], T.ps7[:, 16:24], T.jn[:], OP.add)
-    cp("ar ar0 posD", "aj", T.aj[:], T.ar[:, 0:272].indirect(T.posD[:, 0:16]))
-    cp("jw", "jf2", T.jf[:, 2:8], T.jw[:, 2:8])
-    op("V", "aj", "ajt", V.transpose, T.ajt[:], T.aj[:])
     tt("jf0 jw", "jf1", T.jf[:, 0:2], T.jf[:, 0:2], T.jw[:, 0:2], OP.add)
-    tt("ajt tmp", "f1", T.f1[:], T.ajt[:, 0:256:32], T.tmp[:], OP.mult)
-    tt("f1 jf1 jf2", "f2", T.f2[:], T.f1[:], T.jf[:], OP.add)
-    cp("f2", "fin", T.fin[:], T.f2[:])
-    quant("hw", 0, 128, "hot", "ho0 ho1 ho2 ho3", "hwo")
+    for q in range(N):
+        la, lb = T.land3[:, 4 * q:4 * q + 1], T.land3[:, 4 * q + 1:4 * q + 2]
+        if q % 2:
+            ts("land3 adown zz", "ax%d" % q, T.ax[:, 32 * q:32 * q + 32], T.zz[:, 0:32], la, lb, OP.add, OP.add)
+        else:
+            act("land3 adown ones", "ax%d" % q, T.ax[:, 32 * q:32 * q + 32], T.ones[:, 0:32], AF.Identity, bias=lb, scale=la)
+    pick("hw", 128 + A * r, 128 + A * r + A, "hq", 128, "il", 0, 2, "hq il0 il1", "hwn", at=n0)
+    op("V", " ".join("ax%d" % q for q in range(N)), "ar", V.transpose, T.ar[:], T.ax[:])
     quant("qv", 0, 128, "vt", "vt", "qv")
+    cp("ar posD", "aj", T.aj[:], T.ar[:].indirect(T.posD[:, 0:16]))
+    op("V", "aj", "ajt", V.transpose, T.ajt[:], T.aj[:])
+    tt("ajt sl", "adm", T.adm[:], T.ajt[:, 0:256:32], T.sl[:], OP.is_ge)
+    tt("adm tmp", "f1", T.f1[:], T.adm[:], T.tmp[:], OP.mult)
+    tt("adm m8", "mw2", T.mw2[:], T.adm[:], T.m8[:], OP.mult)
+    tt("f1 jf1 jf2", "f2", T.f2[:], T.f1[:], T.jf[:], OP.add)
+    op("V", "mw2", "mn", V.tensor_reduce, mn, T.mw2[:], X, OP.add)
+    cp("f2", "fin", T.fin[:], T.f2[:])
+    ts("mn gn", "mgc", mgc, mn, gn, -1.0, OP.mult, OP.add)
+    dma("S", "mgc", "mgo", T.mg[:], mgc)
 
     pick("fo", 0, 128, "hw", 384, "fin", 0, 8, "hwo hwr hwn hwns fin", "fo")
     mm(4, "qv", 0, "fo", 128, "qv fo fos")
     dma("S", "fo", "oco", T.oc[:], T.fo[:].bitcast(dt.uint8))
     for k in range(4):
         dma("A", "fos", "osco%d" % k, T.osc[4 * k:4 * k + 4, :], T.fos[32 * k:32 * k + 4, :])
-    tt("ajt m8", "mw2", T.mw2[:], T.ajt[:, 0:256:32], T.m8[:], OP.mult)
-    op("V", "mw2", "mn", V.tensor_reduce, mn, T.mw2[:], X, OP.add)
     cp("ps4", "yo", T.yo[:], T.ps4[:, 0:128])
     dma("S", "yo", "yout", T.y[:], T.yo[:])
-    ts("mn gn", "mgc", mgc, mn, gn, -1.0, OP.mult, OP.add)
-    dma("S", "mgc", "mgo", T.mg[:], mgc)
     for s, v in count.items():
         if known["S"].get(s, 0) < v:
             SY.wait_ge(S[s], v)

@@ -3,6 +3,8 @@ from concourse.mybir import dt, AluOpType, AxisListType, ActivationFunctionType
 
 F32, BF, U16, I32, MXC, U8 = "float32", "bfloat16", "uint16", "int32", "float8_e4m3fn_x4", "uint8"
 SCRATCH = {}
+KN = 2
+W0 = 2
 
 
 def _buf(name, cols, dtype):
@@ -15,35 +17,42 @@ def _mx(name, cols):
 
 
 for _n, _c in (("qx", 128), ("qn", 128), ("anc", 288), ("qtri", 128), ("qa2", 128), ("qe", 512), ("qz", 128), ("qab", 144),
-               ("qb2", 128), ("snd", 128), ("slots", 256), ("pk", 192), ("qw", 512), ("qv", 128), ("km", 128),
-               ("hq", 128), ("hw", 384), ("fo", 128)):
+               ("qb2", 128), ("snd", 128), ("slots", 256), ("qw", 512), ("qv", 128), ("km", 128),
+               ("qs", 128), ("hq", 128), ("hw", 384), ("fo", 128)):
     _mx(_n, _c)
 _buf("rl", 64, MXC)
+_buf("rls", 32, U8)
 _buf("rhs", 32, U8)
 _buf("ras", 32, U8)
-for _n, _c in (("xt", 512), ("xa", 512), ("wt", 2048), ("vt", 512), ("ct", 512), ("ct2", 512), ("et", 516), ("ztb", 608),
-               ("att", 576), ("zz", 512), ("mz", 640), ("hot", 512), ("ones", 128), ("ident", 128),
-               ("tri", 128), ("pm1", 256), ("lx", 128), ("arow", 128), ("eq", 256), ("cc", 256), ("c2", 256),
-               ("j12", 256), ("ax", 256), ("ar", 256), ("aj", 256), ("ajt", 256)):
+for _n, _c in (("xt", 512), ("wt", 2048), ("vt", 512), ("ztb", 768), ("att", 576), ("hot", 640), ("ones", 32),
+               ("pm1", 256), ("lx", 128), ("arow", 128), ("eq", 256), ("rr", 520), ("xc", 128),
+               ("t2", 96), ("us", 48), ("ax", 256), ("ar", 256), ("aj", 256), ("ajt", 256)):
     _buf(_n, _c, BF)
-for _n, _c in (("R", 288), ("mrow", 32), ("thr", 64), ("t1", 64), ("t2", 97), ("sc", 16), ("jr", 256),
-               ("j7", 16), ("ab", 32), ("pen", 32), ("msk", 32), ("num", 32), ("qi", 8), ("qc", 32), ("ri", 16), ("qh", 16),
-               ("crow", 32), ("row8", 8), ("row16", 16), ("pf", 4), ("pc", 8), ("m8", 8), ("m16", 16), ("jw", 8), ("jn", 8),
-               ("lst", 8), ("landL", 32), ("F4", 4), ("tb", 128), ("tmp", 8), ("lohi", 4), ("sec", 4), ("land3", 32),
-               ("sl", 8), ("adm", 8), ("jf", 8), ("f1", 8), ("f2", 8), ("mw2", 8), ("yo", 128)):
+for _n, _c in (("R", 288), ("mrow", 32), ("thr", 64), ("t1", 64), ("kk", 1), ("pd", 160), ("n32", 8), ("tq", 8), ("sc", 16),
+               ("jr", 256), ("j7", 16), ("ab", 32), ("msk", 32), ("num", 32), ("qi", 8), ("qc", 32),
+               ("row8", 8), ("pf", 4), ("pc", 8), ("m8", 8), ("jw", 8), ("jn", 8),
+               ("lst", 8), ("landL", 32), ("tb", 128), ("tmp", 8), ("lohi", 4), ("sec", 4), ("land3", 32),
+               ("sl", 8), ("adm", 8), ("jf", 8), ("f1", 8), ("f2", 8), ("mw2", 8), ("mw3", 8), ("yo", 128)):
     _buf(_n, _c, F32)
-for _n, _c in (("il", 2), ("off", 8), ("fs", 4), ("posD", 16), ("fin", 8)):
+for _n, _c in (("il", 2), ("off", 10), ("ofo", 2), ("fs", 4), ("posD", 16), ("fin", 8), ("fa", 2)):
     _buf(_n, _c, U16)
 _buf("pi", 1, I32)
 _buf("pin", 4, I32)
 for _i in range(8):
     SCRATCH["ps%d" % _i] = ("psum", [128, 512], F32)
-SEMAPHORES = (["cV", "cA", "cP", "cG", "a1", "o1s", "l2", "c2r", "o2a", "o2b", "o2c", "m3", "o3a", "h3", "o3b", "o3c",
-               "ra", "rc", "rk", "hl"] + ["d%d" % _i for _i in range(12)])
+SEMAPHORES = (["cV", "cA", "cP", "cG", "a1", "a2", "o1s", "l2", "c2r", "o2a", "o2b", "o2c", "m3", "o3a", "h3", "o3b", "o3c",
+               "ra", "rs", "rc", "rk", "hl"] + ["d%d" % _i for _i in range(12)])
 
 
-def to(topo, c):
-    return DstId(rid=topo.addr(c)[0], pnc=topo.addr(c)[1])
+def move(topo, cores, engines, sem, src, dst):
+    ids = [DstId(rid=topo.addr(c)[0], pnc=topo.addr(c)[1]) for c in cores]
+    return RemoteDMATransfer(dst_ids=ids, dma_engine_mask=sum(1 << e for e in engines), remote_sem=sem, srcs=[src],
+                             dsts=[dst] * len(ids))
+
+
+def longest_first(topo, core, cores):
+    a = topo.chip(core)
+    return sorted(cores, key=lambda c: topo.mates(a, topo.chip(c)) or topo.same_plane(a, topo.chip(c)))
 
 
 def plan(own, r, T, topo):
@@ -60,22 +69,27 @@ def plan(own, r, T, topo):
 
 def hand_on(g, core, r, role, near, far, T, topo):
     S, CAPP, A = T.sem, 16, 32
-    goal, first = (near, 1) if role else (far, 0)
+    goal = near if role else far
+    s0 = 128 + CAPP * (len(T.cores) - 1 - r)
     eng = topo.engines(core, goal[0])
-    g.wait_ge(S.ra, 4)
-    g.remote_dma_fused([RemoteDMATransfer(dst_ids=[to(topo, goal[0])], dma_engine_mask=topo.mask(core, goal[0]),
-                                          remote_sem=S.a1, src=T.ras[:, 0:A], dst=T.ancs[:, A * r:A * r + A])], local_sem=S.hl)
-    g.wait_ge(S.rc, 4)
-    g.remote_dma_fused([RemoteDMATransfer(dst_ids=[to(topo, d)], dma_engine_mask=1 << eng[2 * i] | 1 << eng[2 * i + 1],
-                                          remote_sem=S.c2r,
-                                          src=T.rl[:, CAPP * (i + first):CAPP * (i + first + 1)].bitcast(dt.uint8),
-                                          dst=T.slots[:, CAPP * r:CAPP * r + CAPP].bitcast(dt.uint8))
-                        for i, d in enumerate(goal)], local_sem=S.hl)
-    g.wait_ge(S.rk, 4)
-    g.remote_dma_fused([RemoteDMATransfer(dst_ids=[to(topo, d) for d in goal], dma_engine_mask=topo.mask(core, goal[0]),
-                                          remote_sem=S.h3, srcs=[T.rhs[:, 0:A]],
-                                          dsts=[T.hws[:, 128 + A * r:128 + A * r + A]] * len(goal))], local_sem=S.hl)
-    g.wait_ge(S.hl, 2 * len(goal) + 2 * len(eng))
+    H = len(T.cores) // 2
+    late, a0 = [d for d in near + far if T.rank_of(d) // H != r // H][role:role + 1], A * (H + r % H)
+    g.wait_ge(S.ra, 8)
+    g.remote_dma_fused([move(topo, late, eng, S.a2, T.ras[:, 0:A], T.ancs[:, a0:a0 + A])], local_sem=S.hl)
+    g.wait_ge(S.rc, 8)
+    some = goal[:KN] if role else goal
+    k = len(eng) // len(some)
+    g.remote_dma_fused([move(topo, [d], eng[k * i:k * i + k], S.c2r, T.rl[:, CAPP * i:CAPP * (i + 1)].bitcast(dt.uint8),
+                             T.slots[:, s0:s0 + CAPP].bitcast(dt.uint8)) for i, d in enumerate(some)], local_sem=S.hl)
+    g.wait_ge(S.rs, 4)
+    some = goal[:KN] if role else goal[:1]
+    k = len(eng) // len(some)
+    g.remote_dma_fused([move(topo, [d], eng[k * i:k * i + k], S.c2r, T.rls[:, CAPP * i:CAPP * (i + 1)],
+                             T.slotss[:, s0:s0 + CAPP]) for i, d in enumerate(some)], local_sem=S.hl)
+    g.wait_ge(S.rk, 8)
+    g.remote_dma_fused([move(topo, longest_first(topo, core, goal), eng, S.h3, T.rhs[:, 0:A],
+                             T.hws[:, 128 + A * r:128 + A * r + A])], local_sem=S.hl)
+    g.wait_ge(S.hl, 4 * len(eng))
 
 
 def rank_program(g, core, T, topo):
@@ -92,6 +106,8 @@ def rank_program(g, core, T, topo):
         return
     OP, AF, X = AluOpType, ActivationFunctionType, AxisListType.X
     V, AC, PE, SY = g.vector, g.scalar, g.tensor, g.sync
+    rr = N - 1 - r
+    s0 = 128 + CAPP * rr
     tiny = 1e-29
 
     qs = {"V": V, "A": AC, "P": PE, "G": g, "S": SY}
@@ -151,34 +167,18 @@ def rank_program(g, core, T, topo):
         known["S"][s] = count[s]
 
     others = [T.cores[q] for q in order[1:]]
-    allm = topo.mask(core, others[0])
-    for c in others:
-        allm &= topo.mask(core, c)
-    eng = [e for e in topo.engines(core, others[0]) if allm >> e & 1]
+    ahead = longest_first(topo, core, others)
+    eng = [e for e in topo.engines(core, others[0]) if all(e in topo.engines(core, c) for c in others)]
     width = len(eng)
     side = [e for e in topo.engines(core, aides[0]) if e not in eng]
 
-    def to_all(rd, src, dstap, sem, loc, goal=others):
+    def send(rd, loc, *moves):
         before("G", rd.split(), [])
-        g.remote_dma_fused([RemoteDMATransfer(dst_ids=[to(topo, c) for c in goal], dma_engine_mask=allm, remote_sem=S[sem],
-                                              srcs=[src], dsts=[dstap] * len(goal))], local_sem=S[loc])
-        count[loc] = count.get(loc, 0) + width
+        g.remote_dma_fused([move(topo, c, e, S[s], src, dst) for c, e, s, src, dst in moves], local_sem=S[loc])
+        count[loc] = count.get(loc, 0) + sum(len(m[1]) for m in moves)
 
-    def to_each(rd, src, dstap, sem, loc):
-        before("G", rd.split(), [])
-        g.remote_dma_fused([RemoteDMATransfer(dst_ids=[to(topo, others[c - 1])], dma_engine_mask=1 << eng[c - 1],
-                                              remote_sem=S[sem], src=src(c), dst=dstap) for c in range(1, N)],
-                           local_sem=S[loc])
-        count[loc] = count.get(loc, 0) + N - 1
-
-    def to_side(rd, src, dstap, sem, loc):
-        before("G", rd.split(), [])
-        h = len(side) // len(aides)
-        g.remote_dma_fused([RemoteDMATransfer(dst_ids=[to(topo, c)],
-                                              dma_engine_mask=sum(1 << e for e in side[h * i:h * i + h]),
-                                              remote_sem=S[sem], src=src[i], dst=dstap) for i, c in enumerate(aides)],
-                           local_sem=S[loc])
-        count[loc] = count.get(loc, 0) + len(aides) * h
+    def raw(name, a, n):
+        return T[name][:, a:a + n].bitcast(dt.uint8)
 
     def ts(rd, wr, out, in0, s1, s2, *ops):
         op("V", rd, wr, V.tensor_scalar, out, in0, s1, s2, *ops)
@@ -209,231 +209,284 @@ def rank_program(g, core, T, topo):
         cp(rd, wr, T[out][:, a:b].bitcast(dt.uint32), T[win][:, at:w].bitcast(dt.uint32).indirect(T[lists][:, la:lb]))
         act(rd, wr + "s", T[out + "s"][:, a:b], T[win + "s"][:, at:w].indirect(T[lists][:, la:lb]), AF.Copy)
 
-    def layer(i, tile, a, n, wr, both):
-        src, out = T["ps%d" % i][:, 0:n], T[tile][:, a + i:a + 4 * n:4]
+    def layer(i, a, n, wr, bank, both=True):
+        src, out = T["ps%d" % bank][:, 0:n], T.hot[:, a + i:a + 4 * n:4]
         if i % 2 and both:
-            ts("ps%d" % i, wr, out, src, 0.0, 0.0625, OP.max, OP.mult)
+            ts("ps%d" % bank, wr, out, src, 0.0, 0.0625, OP.max, OP.mult)
         else:
-            act("ps%d" % i, wr, out, src, AF.Relu, scale=0.0625)
+            act("ps%d" % bank, wr, out, src, AF.Relu, scale=0.0625)
 
-    dma("S", "", "xa", T.xa[:, 0:4 * A], T.x[:, 0:4 * A])
+    def zz(n, lo=0, hi=128):
+        return T.ztb[lo:hi, 128:128 + n]
+
+    def const(wr, out, n, c, rd="", lo=0, hi=128):
+        act("zz " + rd, wr, out, zz(n, lo, hi), AF.Identity, bias=c)
+
+    n0 = 128 - A
+    dma("S", "", "xa", T.ztb[:, 640:768], T.x[:, 0:4 * A])
     dma("S", "", "xt", T.xt[:], T.x[:])
+    dma("S", "", "wt0", T.wt[:, 0:512 * W0], T.w[:, 0:512 * W0])
     op("G", "", "pi", g.iota, T.pi[:], [[0, 1]], 0, 1)
-    iota("qi", T.qi[:], [[A * (order[c] - r), 2] for c in (4, 2, 1)], A * r)
-    fill("", "ones", T.ones[:], 1.0)
-    op("G", "ones", "tri", g.affine_select, T.tri[:], T.ones[:], [[1, 128]], OP.is_ge, 0.0, 0, -1)
-    fill("", "xaz", T.xa[:, 4 * A:], 0.0)
-    fill("", "zz", T.zz[:], 0.0)
+    iota("qi", T.qi[:], [[order[c] - r, 2] for c in (4, 2, 1)], r)
+    iota("xc", T.xc[:], [[1, 128]], 128)
+    fill("", "zz ztb", T.ztb[:, 0:640], 0.0)
+    fill("", "att", T.att[:], 0.0)
     ts("pi", "pin", T.pin[:, 0:1], T.pi[:], 15, None, OP.bitwise_and)
-    quant("qn", 0, 128, "xa", "xa xaz", "qn")
+    quant("qn", 0, 128, "ztb", "xa zz", "qn", at=256)
 
-    to_side("qn", [T.qns[:, 0:A]] * 2, T.ras[:], "ra", "o1s")
-    to_all("qn", T.qn[:, 0:A].bitcast(dt.uint8), T.anc[:, A * r:A * r + A].bitcast(dt.uint8), "a1", "o1s")
-    to_all("qn", T.qns[:, 0:A], T.ancs[:, A * r:A * r + A], "a1", "o1s", near[1:] + far[1:])
-    arrive("a1", 2 * width * (N - 1), "anc")
+    H = N // 2
+    p1 = A * (r % H)
+    p2 = p1 + A * H
+    first = [c for c in ahead if T.rank_of(c) // H == r // H]
+    late = [c for c in others if c not in first]
+    send("qn", "o1s", (aides, side, "ra", T.qns[:, n0:128], T.ras[:]))
+    send("qn", "o1s", (first, eng, "a1", raw("qn", n0, A), raw("anc", p1, A)))
+    send("qn", "o1s", (first, eng, "a1", T.qns[:, n0:128], T.ancs[:, p1:p1 + A]))
+    send("qn", "o1s", (late[len(aides):], eng, "a2", T.qns[:, n0:128], T.ancs[:, p2:p2 + A]))
+    send("qn", "o1s", (longest_first(topo, core, late), eng, "a2", raw("qn", n0, A), raw("anc", p2, A)))
+    arrive("a1", 2 * width * len(first), "anc1")
+    arrive("a2", 2 * width * len(late), "anc2")
     left("o1s")
-    dma("S", "", "wt", T.wt[:], T.w[:])
+    dma("S", "", "wt1", T.wt[:, 512 * W0:], T.w[:, 512 * W0:])
+    dma("S", "", "vt", T.vt[:], T.v[:])
 
-    op("G", "ones", "ident", g.affine_select, T.ident[:], T.ones[:], [[1, 128]], OP.is_equal, 0.0, 0, -1)
-    iota("ri", T.ri[:, 0:15], [[A, 15]], -7 * A)
-    iota("crow", T.crow[:], [[1, 32]])
-    iota("row8", T.row8[:], [[1, 8]])
-    iota("row16", T.row16[:], [[1, 8], [0, 2]])
-    iota("pm1", T.pm1[:], [[0, 8], [1, 16], [0, 2]], 65)
     for k in range(4):
-        act("qi", "qc%d" % k, T.qc[:, k // 2 * 16 + k % 2:k // 2 * 16 + 16:2], T.qi[:], AF.Identity, bias=0.5 * A - 0.5)
-    act("zz", "num3", T.num[:, 17:32:2], T.zz[:, 0:8], AF.Identity, bias=32.0)
+        act("qi", "qc%d" % k, T.qc[:, k // 2 * 16 + k % 2:k // 2 * 16 + 16:2], T.qi[:], AF.Copy)
+    for k in range(2):
+        act("xc", "pm1%d" % k, T.pm1[:, k:32:2], T.xc[:, 0:16], AF.Identity, scale=-1.0, bias=192.0 + CAPP)
+    const("thr1", T.thr[:, 32:64], 32, 0.0)
+    act("pm10 pm11", "pm12", T.pm1[:, 32:64], T.pm1[:, 0:32], AF.Copy)
+    const("kk", T.kk[:], 1, 1.0 - KM)
     ts("pin", "il0", T.il[:, 0:1], T.pin[:, 0:1], 0, None, OP.add)
     ts("pin", "il1", T.il[:, 1:2], T.pin[:, 0:1], 16, None, OP.add)
-    fill("", "ct", T.ct[:], 0.0)
-    for a, k in ((A * r, "own"), (N * A, "pad")):
-        pick("anc", a, a + A, "qn", 128, "il", 0, 2, "qn il0 il1", "anc" + k)
+    ts("pi", "p128", T.pf[:, 3:4], T.pi[:], 128.0, None, OP.add)
     ts("pi", "pin1", T.pin[:, 1:2], T.pi[:], 4, None, OP.arith_shift_right)
+    act("pm12", "pm13", T.pm1[:, 64:128], T.pm1[:, 0:64], AF.Copy)
+    for a, k in ((p1, "own"), (N * A, "pad")):
+        pick("anc", a, a + A, "qn", 128, "il", 0, 2, "qn il0 il1", "anc" + k, at=n0)
+    act("pm13", "pm1", T.pm1[:, 128:256], T.pm1[:, 0:128], AF.Copy)
+    quant("qx", 0, 128, "xt", "xt", "qx")
+    act("xt", "xt", T.xt[:, 0:4 * A], T.xt[:, 4 * A:8 * A], AF.Copy)
     ts("pi", "pin2", T.pin[:, 2:3], T.pi[:], 31, None, OP.bitwise_and)
     cp("pin", "pm", T.pf[:, 0:1], T.pin[:, 0:1])
-    fill("", "et", T.et[:], 0.0)
+    ts("xc p128", "att", T.att[:, 0:512:4], T.xc[:], T.pf[:, 3:4], None, OP.is_ge)
     cp("pin1", "ph16", T.pf[:, 1:2], T.pin[:, 1:2])
-    cp("pin2", "p31", T.pf[:, 2:3], T.pin[:, 2:3])
-    act("tri ct", "ctri", T.ct[:, 0:512:4], T.tri[:], AF.Copy)
-    act("zz pm", "num0", T.num[:, 0:16:2], T.zz[:, 0:8], AF.Identity, bias=T.pf[:, 0:1])
+    ts("xc p128 att", "cid", T.att[:, 2:512:4], T.xc[:], T.pf[:, 3:4], 64.0, OP.is_equal, OP.mult)
+    ts("pin2", "p31", T.pf[:, 2:3], T.pin[:, 2:3], 128.0, None, OP.add)
+    quant("qs", 0, 128, "xt", "xt", "qs")
+    quant("qtri", 0, 128, "att", "att cid", "qtri")
+    const("t10", T.t1[0:32, 32:64], 32, 0.0, hi=32)
+    const("t20", T.t2[0:32, 64:96], 32, 0.0, hi=32)
+    const("thr2", T.thr[96:128, 32:64], 32, tiny, "thr1", lo=96)
+    const("kk0", T.kk[0:32, :], 1, 1000.0, "kk", hi=32)
+    if r >= H:
+        const("pdz", T.pd[:, 0:128], 128, -9.0e29)
     act("ph16", "khi", T.pc[:, 0:1], T.pf[:, 1:2], AF.Copy, scale=16.0)
-    quant("qx", 0, 128, "xt", "xt", "qx")
-    act("pm", "a0", T.pc[:, 1:2], T.pf[:, 0:1], AF.Identity, bias=16.0)
-    act("pm", "a1c", T.pc[:, 2:3], T.pf[:, 0:1], AF.Identity, bias=32.0)
-    act("pm", "a65", T.pc[:, 4:5], T.pf[:, 0:1], AF.Identity, bias=65.0)
-    act("zz khi", "num1", T.num[:, 1:16:2], T.zz[:, 0:8], AF.Identity, bias=T.pc[:, 0:1])
-    act("ident ct", "cid", T.ct[:, 2:512:4], T.ident[:], AF.Copy, scale=64.0)
-    act("ident et", "e", T.et[:, 4:516:4], T.ident[:], AF.Copy, scale=0.5)
-    fill("", "thr1", T.thr[:, 32:64], 0.0)
-    fill("", "kk", T.t2[:, 96:97], 16.0 - KM + 0.5)
-    fill("", "t10", T.t1[0:32, 32:64], 0.0)
-    fill("", "t20", T.t2[0:32, 64:96], 0.0)
-    fill("", "ztb", T.ztb[:], 0.0)
-    fill("thr1", "thr2", T.thr[96:128, 32:64], tiny)
-    fill("kk", "kk", T.t2[0:32, 96:97], 1000.0)
-    fill("", "att", T.att[:], 0.0)
-    ts("p31", "hp", T.pc[:, 3:4], T.pf[:, 2:3], 15.5, float(r % 2), OP.is_gt, OP.is_equal)
-    ts("p31", "lo", T.lohi[:, 0:1], T.pf[:, 2:3], 15.5, None, OP.is_lt)
-    ts("p31", "hi", T.lohi[:, 1:2], T.pf[:, 2:3], 15.5, None, OP.is_gt)
-    quant("slots", 128, 128, "zz", "zz", "slz")
-    quant("pk", 64, 128, "zz", "zz", "pkz")
-    fill("", "mz", T.mz[:, 4 * A:512], 0.0)
-    fill("", "ct2", T.ct2[:], 0.0)
-    quant("qtri", 0, 128, "ct", "ctri cid ct", "qtri")
-    ts("ri", "qh", T.qh[:, 0:15], T.ri[:, 0:15], -0.5, None, OP.add)
-    ts("crow p31", "thr0", T.thr[:, 0:32], T.crow[:], T.pf[:, 2:3], tiny, OP.is_lt, OP.mult)
-
+    act("pm", "a65", T.pc[:, 4:5], T.pf[:, 0:1], AF.Identity, scale=-1.0, bias=64.0 + CAPP)
+    act("zz pm", "num0", T.num[:, 0:16:2], zz(8), AF.Identity, bias=T.pf[:, 0:1])
+    act("zz khi", "num1", T.num[:, 1:16:2], zz(8), AF.Identity, bias=T.pc[:, 0:1])
+    const("num3", T.num[:, 17:32:2], 8, 32.0)
+    const("n32", T.n32[:], 8, -float(A))
+    ts("xc p31", "thr0", T.thr[:, 0:32], T.xc[:, 0:32], T.pf[:, 2:3], tiny, OP.is_lt, OP.mult)
+    fill("", "cid att", T.att[:, 2:512:4], 0.0)
+    ts("p31", "hp", T.pc[:, 3:4], T.pf[:, 2:3], 143.5, float(rr % 2), OP.is_gt, OP.is_equal)
+    ts("xc p128 att", "e", T.att[:, 4:516:4], T.xc[:], T.pf[:, 3:4], 0.5, OP.is_equal, OP.mult)
+    pick("slots", 0, CAPP, "qn", n0, "il", 0, 1, "qn il0", "slz")
     for b in range(4):
-        quant("qe", 128 * b, 128, "et", "et e", "qe%d" % b, at=4 - b)
+        quant("qe", 128 * b, 128, "att", "att e", "qe%d" % b, at=4 - b)
         mm(4 + b, "qe", 128 * b, "qn", 128, "qe%d qn" % b, stop=False)
-    act("row8 pm", "jw", T.jw[:], T.row8[:], AF.Identity, scale=16.0, bias=T.pf[:, 0:1])
-    act("jw", "jn", T.jn[:], T.jw[:], AF.Identity, scale=-1.0, bias=144.0)
-    act("jw", "jf2", T.jf[:, 2:8], T.jw[:, 2:8], AF.Copy)
-    ts("row8 ph16", "m8", T.m8[:], T.row8[:], T.pf[:, 1:2], None, OP.is_equal)
-    ts("row16 ph16", "m16", T.m16[:], T.row16[:], T.pf[:, 1:2], None, OP.is_equal)
+    quant("qw", 0, 128 * W0, "wt", "wt0", "qw0")
+    for i in range(W0):
+        mm(2 + i % 2, "qw", 128 * i, "qx", 128, "qw0 qx")
+        layer(i, 4 * A, 128, "ho%d" % i, 2 + i % 2, False)
+    ts("pm1 a65", "att e", T.att[:, 0:512:2], T.pm1[:], T.pc[:, 4:5], None, OP.is_equal)
+    quant("qa2", 0, 128, "att", "att", "qa2")
 
-    best, q2, d16, u, o1, st2, st, pl, ph, q32, gn, mn, mgc = [T.sc[:, i:i + 1] for i in range(13)]
-    M = T.R[:, 255:256]
-    mm(0, "qx", 0, "anc", 288, "qx anc ancown ancowns ancpad ancpads")
-    op("V", "ps0 zz", "R", V.tensor_tensor_scan, T.R[:], T.ps0[:, 0:288], T.zz[:, 0:288], -9.0e29, OP.max, OP.add)
+    best, q1, o1, st2, st, pl, ph, q32, gn, mn, mgc, q0, b0, qx, bx = [T.sc[:, i:i + 1] for i in range(15)]
+    M, u, d16 = T.R[:, 287:288], T.us[:, 47:48], T.num[:, 16:17]
+    M1 = T.R[:, 127:128]
+    mm(0, "qs", 0, "anc", 128, "qs anc1 ancown ancowns")
+    op("V", "ps0 zz", "R1", V.tensor_tensor_scan, T.R[:, 0:128], T.ps0[:, 0:128], zz(128), -9.0e29, OP.max, OP.add)
+    if r >= H:
+        act("R1 zz", "pd", T.pd[:, 128:160], zz(A), AF.Identity, bias=M1)
+        act("R1", "q0 j7", T.j7[:, 0:H], T.R[:, A - 1:H * A:A], AF.Sign, bias=M1, scale=-1.0, accum_out=q0)
+        act("R1", "b0 jr", T.jr[:, 0:128], T.R[:, 0:128], AF.Sign, bias=M1, scale=-1.0, accum_out=b0)
+    mm(1, "qs", 0, "anc", 160, "qs anc2 ancpad ancpads", xv=128)
+    if r >= H:
+        op("V", "ps1 pd pdz", "R", V.tensor_tensor_scan, T.R[:, 128:288], T.ps1[:, 0:160], T.pd[:], -9.0e29, OP.max, OP.max)
+    else:
+        op("V", "ps1 zz R1", "R", V.tensor_tensor_scan, T.R[:, 128:288], T.ps1[:, 0:160], zz(160), M1, OP.max, OP.add)
     op("V", "R", "m0", V.transpose, T.mrow[:], T.R[:, 256:288])
-    act("R", "best jr", T.jr[:], T.R[:, 0:256], AF.Sign, bias=M, scale=-1.0, accum_out=best)
+    flag = T.j7[:, N - 1:N]
+    if r >= H:
+        act("R", "qx fl", T.j7[:, H:N], T.R[:, (H + 1) * A - 1:N * A:A], AF.Sign, bias=M, scale=-1.0, accum_out=qx)
+    else:
+        act("R R1", "q1 j7", T.j7[:, 0:N], T.R[:, A - 1:N * A:A], AF.Sign, bias=M, scale=-1.0, accum_out=q1)
 
-    def quad(t, q, c):
-        return T[t][32 * q:32 * q + 32, c:c + 32]
+    def quad(t, q, c, n=1):
+        return T[t][32 * q:32 * (q + n), c:c + 32]
+
+    def top(q, n=1):
+        return T.R[32 * q:32 * (q + n), 287:288]
 
     ts("R m0", "t1a", T.t1[:, 0:32], T.mrow[:], M, -1.0, OP.subtract, OP.mult)
-    for a in range(1, 4):
-        Ma = T.R[32 * a:32 * a + 32, 255:256]
-        b = a % 3 + 1
-        act("R m0", "t1%d" % a, quad("t1", a, 32), quad("mrow", b, 0), AF.Identity, scale=-1.0, bias=Ma)
-        b = (a + 1) % 3 + 1
-        ts("R m0", "t2%d" % a, quad("t2", a, 64), quad("mrow", b, 0), Ma, None, OP.is_ge if b < a else OP.is_gt)
-    act("best qc0 qc1 qc2 qc3", "ab", T.ab[:], T.qc[:], AF.Abs, bias=best, scale=-1.0)
-    act("best qh", "q2 j7", T.j7[:, 0:15], T.qh[:, 0:15], AF.Sign, bias=best, scale=-1.0, accum_out=q2)
-    act("ab", "pen", T.pen[:], T.ab[:], AF.Relu, scale=-2.0, bias=32.0)
-    act("q2 best", "d16", d16, q2, AF.Identity, bias=best, scale=-16.0)
-    act("pen", "msk", T.msk[:], T.pen[:], AF.Sign)
-    act("d16 zz", "num2", T.num[:, 16:32:2], T.zz[:, 0:8], AF.Identity, bias=d16)
-    act("q2", "q32", q32, q2, AF.Identity, scale=16.0, bias=-16.0)
-    act("q2 best", "gn", gn, q2, AF.Identity, scale=48.0, bias=best)
+    for a in (1, 2):
+        act("R m0", "t1%d" % a, quad("t1", a, 32), quad("mrow", a + 1, 0), AF.Identity, scale=-1.0, bias=top(a))
+    if r >= H:
+        act("qx fl q0", "q1", q1, flag, AF.Identity, scale=q0, bias=qx)
+    ts("R m0", "t13", quad("t1", 3, 32), quad("mrow", 2, 0), top(3), -1.0, OP.subtract, OP.mult)
+    ts("R m0", "t21", quad("t2", 1, 64), quad("mrow", 3, 0), top(1), None, OP.is_gt)
+    ts("R m0", "t22", quad("t2", 2, 64, 2), quad("mrow", 0, 0, 2), top(2, 2), None, OP.is_ge)
+    act("q1 qc0 qc1 qc2 qc3", "ab", T.ab[:], T.qc[:], AF.Abs, bias=q1, scale=-1.0)
+    if r >= H:
+        act("R", "bx jr2", T.jr[:, 128:256], T.R[:, 128:256], AF.Sign, bias=M, scale=-1.0, accum_out=bx)
+    else:
+        act("R R1", "best jr", T.jr[:], T.R[:, 0:256], AF.Sign, bias=M, scale=-1.0, accum_out=best)
+    act("q1 n32", "tq", T.tq[:], T.n32[:], AF.Identity, scale=q1, bias=-16.0)
+    if r >= H:
+        act("bx fl b0", "best", best, flag, AF.Identity, scale=b0, bias=bx)
+    act("tq best", "num2", T.num[:, 16:32:2], T.tq[:], AF.Identity, bias=best)
+    act("q1", "q32", q32, q1, AF.Copy, scale=float(A))
+    act("q1 best", "gn", gn, q1, AF.Identity, scale=128.0 - A, bias=best)
     tt("t1a t11 t12 t13 t10 thr0 thr1 thr2", "t2", T.t2[:, 0:64], T.t1[:], T.thr[:], OP.is_lt)
-    op("V", "t2 t20 t21 t22 t23 kk", "u", V.tensor_reduce, u, T.t2[:], X, OP.add)
-    ts("ab u ztb", "ztv", T.ztb[:, 96:128:2], T.ab[:, 0:16], u, 16.0, OP.max, OP.is_lt)
+    op("V", "t2 t20 t21 t22 kk kk0", "u", V.tensor_tensor_scan, T.us[:], T.t2[:, 0:48], T.t2[:, 48:96], T.kk[:],
+       OP.add, OP.add)
+    ts("ab u ztb", "ztv", T.ztb[:, 96:128:2], T.ab[:, 0:16], u, 0.5, OP.max, OP.is_lt)
     quant("qz", 0, 128, "ztb", "ztv ztb", "qz", at=96)
     mm(1, "qtri", 0, "qz", 128, "qtri qz")
-    tt("msk num0 num1 num2 num3 att", "bt", T.att[:, 512:576:2], T.msk[:], T.num[:], OP.mult)
+    ts("ab", "msk", T.msk[:], T.ab[:], 0.5, None, OP.is_lt)
     op("V", "ps1", "o1", V.tensor_reduce, o1, T.ps1[:, 0:8], X, OP.max)
-    ts("pm1 o1 att", "at0", T.att[:, 0:512:2], T.pm1[:], o1, None, OP.is_equal)
-    ts("o1", "st2", st2, o1, 64.0 + CAPP + 0.5, None, OP.is_lt)
+    tt("msk num0 num1 num2 num3", "bt e", T.att[:, 512:576:2], T.msk[:], T.num[:], OP.mult)
+    ts("pm1 o1", "at0 att", T.att[:, 0:512:2], T.pm1[:], o1, None, OP.is_equal)
     quant("qab", 0, 144, "att", "att at0 bt", "qab")
     mm(2, "qab", 0, "qab", 128, "qab", xv=16)
-    ts("o1 st2", "st", st, o1, 64.5, st2, OP.is_gt, OP.mult)
-    act("m16 ztb d16", "w2", T.ztb[:, 0:64:4], T.m16[:], AF.Copy, scale=d16)
-    act("m16 ztb q32", "w3", T.ztb[:, 2:64:4], T.m16[:], AF.Copy, scale=q32)
-    act("gn", "gn", gn, gn, AF.Identity, bias=-47.0)
+    ts("o1", "st2", st2, o1, 64.0 + CAPP + 0.5, None, OP.is_lt)
+    act("xc", "row8", T.row8[:], T.xc[:, 0:8], AF.Identity, bias=-128.0)
+    act("gn", "gn", gn, gn, AF.Identity, bias=1.0)
+    act("pm", "a0", T.pc[:, 1:2], T.pf[:, 0:1], AF.Identity, bias=16.0)
+    act("pm", "a1c", T.pc[:, 2:3], T.pf[:, 0:1], AF.Identity, bias=32.0)
+    const("rrz", T.rr[:, 260:391:130], 2, 0.0)
+    const("ones", T.ones[:], 32, 1.0)
 
     ts("ps2 hp", "lst", T.lst[:], T.ps2[:, 120:128], T.pc[:, 3:4], None, OP.mult)
-    cp("ps2", "off", T.off[:], T.ps2[:, 112:120])
-    to_each("lst", lambda c: T.lst[:, c:c + 1], T.landL[:, 4 * r:4 * r + 1], "l2", "o2a")
-    pick("snd", 0, 128, "qx", 128, "off", 0, 8, "qx off", "snd")
-    half = CAPP * N // 2
-    to_side("snd", [T.snd[:, half:].bitcast(dt.uint8), T.snd[:, 0:half].bitcast(dt.uint8)], T.rl[:].bitcast(dt.uint8),
-            "rc", "o2b")
-    to_each("snds", lambda c: T.snds[:, CAPP * c:CAPP * c + CAPP], T.slotss[:, CAPP * r:CAPP * r + CAPP], "c2r", "o2c")
-    left("o2b")
-    dma("S", "", "vt", T.vt[:], T.v[:])
-    arrive("l2", N - 1, "landL")
-    arrive("c2r", 3 * (N - 1), "slots")
+    cp("ps2", "off", T.off[:, 1:9], T.ps2[:, 112:120])
+    send("lst", "o2a", *[([others[c - 1]], eng[c - 1:c], "l2", T.lst[:, c:c + 1], T.landL[:, 4 * rr:4 * rr + 1])
+                         for c in range(1, N)])
+    ts("o1 st2", "st", st, o1, 64.5, st2, OP.is_gt, OP.mult)
+    away, half, hs = CAPP * (N - 1), CAPP * H, len(side) // 2
+    pick("snd", 0, away, "qx", 128, "off", 2, 9, "qx off", "snd")
 
-    quant("qw", 0, 512, "wt", "wt", "qw")
-    pick("slots", CAPP * r, CAPP * r + CAPP, "qx", 128, "off", 0, 1, "qx off", "slown")
-    act("lst", "lown", T.landL[:, 4 * r:4 * r + 1], T.lst[:, 0:1], AF.Copy)
-    ts("o1 st", "pl", pl, o1, -65.0, st, OP.add, OP.mult)
-    ts("st", "ph", ph, st, float(CAPP * r) - 256.0, 256.0, OP.mult, OP.add)
-    ts("pm1 a65 ct2", "ca", T.ct2[:, 0:512:2], T.pm1[:], T.pc[:, 4:5], None, OP.is_equal)
-    for i in range(4):
-        mm(i, "qw", 128 * i, "qx", 128, "qw qx")
-        layer(i, "hot", 0, 128, "ho%d" % i, False)
-    quant("qa2", 0, 128, "ct2", "ct2 ca", "qa2")
+    def sc(c, n=1):
+        return T.snds[:, CAPP * c:CAPP * (c + n)]
+
+    send("snd", "o2b", (aides[:1], side, "rc", raw("snd", away - half, half), raw("rl", 0, half)))
+    send("snd", "o2b", (near[KN:], eng[N - 1:], "c2r", raw("snd", KN * CAPP, CAPP), raw("slots", s0, CAPP)))
+    send("snd", "o2b", (aides[1:], side, "rc", raw("snd", 0, KN * CAPP), raw("rl", 0, KN * CAPP)))
+    send("snds", "o2c", (aides[:1], side[:hs], "rs", sc(H - 1, KN), T.rls[:]), (aides[1:], side[hs:], "rs", sc(0, KN), T.rls[:]))
+    send("snds", "o2c", *[([others[c]], eng[2 * i:2 * i + 2], "c2r", sc(c), T.slotss[:, s0:s0 + CAPP])
+                          for i, c in enumerate(list(range(H, N - 1)) + [KN])])
+    arrive("l2", N - 1, "landL")
+    arrive("c2r", 5 * width + len(eng[N - 1:]), "slots")
+
+    cp("off", "ofo", T.ofo[:, 0:1], T.off[:, 1:2])
+    act("lst", "lown", T.landL[:, 4 * rr:4 * rr + 1], T.lst[:, 0:1], AF.Copy)
+    ts("row8 ph16", "m8", T.m8[:], T.row8[:], T.pf[:, 1:2], None, OP.is_equal)
+    quant("qw", 128 * W0, 512 - 128 * W0, "wt", "wt1", "qw1", at=512 * W0)
+    pick("slots", s0, s0 + CAPP, "qx", 128, "ofo", 0, 1, "qx ofo", "slown")
+    for k, (a, v) in enumerate(((0, d16), (4, d16), (2, q32), (6, q32))):
+        act("m8 ztb num2 q32", "w2%d" % k, T.ztb[:, a:64:8], T.m8[:], AF.Copy, scale=v)
+    ts("o1 st", "pl", pl, o1, -64.0, st, OP.add, OP.mult)
+    ts("st", "ph", ph, st, -float(s0 + 2 * CAPP), float(CAPP), OP.mult, OP.add)
+    ts("p31", "lo", T.lohi[:, 0:1], T.pf[:, 2:3], 143.5, -1.0, OP.is_lt, OP.mult)
+    ts("p31", "hi", T.lohi[:, 1:2], T.pf[:, 2:3], 143.5, -1.0, OP.is_gt, OP.mult)
+    for i in range(W0, 4):
+        mm(i % 2, "qw", 128 * i, "qx", 128, "qw1 qx")
+        layer(i, 4 * A, 128, "ho%d" % i, i % 2)
+    quant("qv", 0, 128, "vt", "vt", "qv")
 
     for c in range(4):
         la, lb = T.landL[:, 8 * c:8 * c + 1], T.landL[:, 8 * c + 4:8 * c + 5]
         if c < 2:
-            ts("landL lown zz", "lx%d" % c, T.lx[:, 32 * c:32 * c + 32], T.zz[:, 0:32], la, lb, OP.add, OP.add)
+            ts("landL lown zz", "lx%d" % c, T.lx[:, 32 * c:32 * c + 32], zz(32), la, lb, OP.add, OP.add)
         else:
             act("landL lown ones", "lx%d" % c, T.lx[:, 32 * c:32 * c + 32], T.ones[:, 0:32], AF.Identity, bias=lb, scale=la)
     act("m8 ztb pl", "w0", T.ztb[:, 64:96:4], T.m8[:], AF.Copy, scale=pl)
     act("m8 ztb ph", "w1", T.ztb[:, 66:96:4], T.m8[:], AF.Copy, scale=ph)
+    act("row8 pm", "jw", T.jw[:], T.row8[:], AF.Identity, scale=16.0, bias=T.pf[:, 0:1])
     op("V", "lx0 lx1 lx2 lx3", "arow", V.transpose, T.arow[:], T.lx[:])
-    H = [slice(0, 128), slice(128, 256)]
+    act("jw", "jn", T.jn[:], T.jw[:], AF.Identity, scale=-1.0, bias=144.0)
+    act("jw", "jf2", T.jf[:, 2:4], T.jw[:, 0:2], AF.Identity, bias=float(A))
+    W = 130
     for h in range(2):
-        ts("arow a0 a1c", "eq%d" % h, T.eq[:, H[h]], T.arow[:], T.pc[:, 1 + h:2 + h], None, OP.is_equal)
-    for h in range(2):
-        op("V", "ones eq%d" % h, "cc%d" % h, V.tensor_tensor_scan, T.cc[:, H[h]], T.ones[:], T.eq[:, H[h]], 0.0, OP.mult, OP.add)
-        act("cc%d" % h, "F%d j%d" % (h, h), T.j12[:, H[h]], T.cc[:, H[h]], AF.Relu, bias=1.0, scale=-1.0,
-            accum_out=T.F4[:, h:h + 1])
-    for h in range(2):
-        ts("cc%d" % h, "c2%d" % h, T.c2[:, H[h]], T.cc[:, H[h]], 1.5, None, OP.is_lt)
-    for h in range(2):
-        op("V", "c2%d" % h, "F%d" % (2 + h), V.tensor_reduce, T.F4[:, 2 + h:3 + h], T.c2[:, H[h]], X, OP.add)
-    quant("qb2", 0, 128, "ztb", "ztb ztv w0 w1 w2 w3", "qb2")
-    cp("F0 F1 F2 F3", "fs", T.fs[:], T.F4[:])
-    tt("F2 F3 lo hi", "sec", T.sec[:, 0:2], T.F4[:, 2:4], T.lohi[:, 0:2], OP.mult)
-    to_all("sec", T.sec[:, 0:2], T.land3[:, 4 * r:4 * r + 2], "m3", "o3a")
-    mm(3, "qa2", 0, "qb2", 128, "qa2 qb2")
+        ts("arow a0 a1c", "eq%d" % h, T.eq[:, 128 * h:128 * h + 128], T.arow[:], T.pc[:, 1 + h:2 + h], 512.0,
+           OP.is_equal, OP.mult)
+    for h in range(4):
+        k = h % 2
+        at = W * (h ^ 2)
+        op("V", "eq%d " % k + ("xc" if h < 2 else "rrz F%d" % k), "F%d" % h, V.tensor_tensor_scan,
+           T.rr[:, at + 1:at + 129], T.eq[:, 128 * k:128 * k + 128], T.xc[:] if h < 2 else T.rr[:, W * h:W * h + 128],
+           0.0, OP.max, OP.min)
+    cp("F0 F1 F2 F3", "fs", T.fs[:], T.rr[:, 128:4 * W:W])
+    tt("F2 F3 lo hi", "sec", T.sec[:, 0:2], T.rr[:, 128:2 * W:W], T.lohi[:, 0:2], OP.mult)
+    send("sec", "o3a", (ahead, eng, "m3", T.sec[:, 0:2], T.land3[:, 4 * r:4 * r + 2]))
 
-    pick("pk", 0, 64, "slots", 256, "fs", 0, 4, "slots slown slowns slz fs", "pk")
+    pick("qs", 64, 128, "slots", 256, "fs", 0, 4, "slots slown slowns slz slzs fs", "pk")
     for b in range(4):
-        mm(4 + b, "qe", 128 * b, "pk", 128, "qe%d pk pks pkz" % b, start=False)
+        mm(4 + b, "qe", 128 * b, "qs", 128, "qe%d qs pk pks" % b, start=False)
     act("sec", "adown", T.land3[:, 4 * r:4 * r + 2], T.sec[:, 0:2], AF.Copy)
-    ts("ps3", "posD", T.posD[:], T.ps3[:, 0:16], 16.0, None, OP.add)
-    tt("ps3 jn", "tmp", T.tmp[:], T.ps3[:, 0:16:2], T.jn[:], OP.add)
-    cp("ps3", "sl", T.sl[:], T.ps3[:, 16:24])
-    quant("hw", 0, 128, "hot", "ho0 ho1 ho2 ho3", "hwo")
+    quant("qb2", 0, 128, "ztb", "ztb ztv w0 w1 w20 w21 w22 w23", "qb2")
+    quant("hw", 0, 128, "hot", "ho0 ho1 ho2 ho3", "hwo", at=4 * A)
     for b in range(4):
         src, tb = T["ps%d" % (4 + b)], T.tb[:, 32 * b:32 * b + 32]
-        act("ps%d" % (4 + b), "tb%d" % b, tb, src[:, A:2 * A], AF.Copy)
-        tt("ps%d tb%d" % (4 + b, b), "mt%d" % b, T.mz[:, b:4 * A:4], src[:, 0:A], tb, OP.add)
-    quant("km", 0, 128, "mz", "mz mt0 mt1 mt2 mt3", "km")
-    ts("F0 F1", "jf0", T.jf[:, 0:2], T.F4[:, 0:2], 127.5, 128.0 + A * r, OP.is_lt, OP.mult)
+        act("ps%d" % (4 + b), "tb%d" % b, tb, src[:, n0 - A:n0], AF.Copy)
+        tt("ps%d tb%d" % (4 + b, b), "mt%d" % b, T.att[:, b:4 * A:4], src[:, n0:128], tb, OP.add)
+        if b == 0:
+            mm(4, "qa2", 0, "qb2", 128, "qa2 qb2")
+    quant("km", 0, 128, "att", "att mt0 mt1 mt2 mt3", "km")
+    ts("ps4", "posD", T.posD[:, 4:16], T.ps4[:, 4:16], 16.0, None, OP.add)
+    tt("ps4 jn", "tmp", T.tmp[:], T.ps4[:, 0:16:2], T.jn[:], OP.add)
+    cp("ps4", "sl", T.sl[:], T.ps4[:, 16:24])
     for i in range(4):
-        mm(i, "qw", 128 * i, "km", 128, "qw km")
-        layer(i, "mz", 512, A, "ht%d" % i, True)
-    quant("hq", 0, 128, "mz", "mz ht0 ht1 ht2 ht3", "hq", at=128)
+        mm(i, "qw", 128 * i, "km", 128, "qw0 qw1 km")
+        layer(i, 0, A, "ht%d" % i, i)
+        if i == 1:
+            ts("F0 F1", "jf0", T.jf[:, 0:2], T.rr[:, 128 + 2 * W:4 * W:W], 0.5, -float(A), OP.is_gt, OP.mult)
+    quant("hq", 0, 128, "hot", "ho0 ho1 ho2 ho3 ht0 ht1 ht2 ht3", "hq")
 
-    n0 = 128 - A
-    to_side("hq", [T.hqs[:, n0:128]] * 2, T.rhs[:], "rk", "o3c")
-    to_all("hq", T.hq[:, n0:128].bitcast(dt.uint8), T.hw[:, 128 + A * r:128 + A * r + A].bitcast(dt.uint8), "h3", "o3b")
+    h0 = 128 + A * r
+    send("hq", "o3c", (aides, side, "rk", T.hqs[:, 0:A], T.rhs[:]))
+    send("hq", "o3b", (ahead, eng, "h3", raw("hq", 0, A), raw("hw", h0, A)))
     arrive("m3", width * (N - 1), "land3")
     arrive("h3", 2 * width * (N - 1), "hwr")
-    tt("jf0 jw", "jf1", T.jf[:, 0:2], T.jf[:, 0:2], T.jw[:, 0:2], OP.add)
+    tt("jf0 jf2", "jf1", T.jf[:, 4:6], T.jf[:, 0:2], T.jf[:, 2:4], OP.add)
     for q in range(N):
         la, lb = T.land3[:, 4 * q:4 * q + 1], T.land3[:, 4 * q + 1:4 * q + 2]
         if q % 2:
-            ts("land3 adown zz", "ax%d" % q, T.ax[:, 32 * q:32 * q + 32], T.zz[:, 0:32], la, lb, OP.add, OP.add)
+            ts("land3 adown zz", "ax%d" % q, T.ax[:, 32 * q:32 * q + 32], zz(32), la, lb, OP.add, OP.add)
         else:
             act("land3 adown ones", "ax%d" % q, T.ax[:, 32 * q:32 * q + 32], T.ones[:, 0:32], AF.Identity, bias=lb, scale=la)
-    pick("hw", 128 + A * r, 128 + A * r + A, "hq", 128, "il", 0, 2, "hq il0 il1", "hwn", at=n0)
+    cp("jf1", "fa", T.fa[:], T.jf[:, 4:6])
     op("V", " ".join("ax%d" % q for q in range(N)), "ar", V.transpose, T.ar[:], T.ax[:])
-    quant("qv", 0, 128, "vt", "vt", "qv")
-    cp("ar posD", "aj", T.aj[:], T.ar[:].indirect(T.posD[:, 0:16]))
-    op("V", "aj", "ajt", V.transpose, T.ajt[:], T.aj[:])
-    tt("ajt sl", "adm", T.adm[:], T.ajt[:, 0:256:32], T.sl[:], OP.is_ge)
-    tt("adm tmp", "f1", T.f1[:], T.adm[:], T.tmp[:], OP.mult)
-    tt("adm m8", "mw2", T.mw2[:], T.adm[:], T.m8[:], OP.mult)
-    tt("f1 jf1 jf2", "f2", T.f2[:], T.f1[:], T.jf[:], OP.add)
-    op("V", "mw2", "mn", V.tensor_reduce, mn, T.mw2[:], X, OP.add)
-    cp("f2", "fin", T.fin[:], T.f2[:])
-    ts("mn gn", "mgc", mgc, mn, gn, -1.0, OP.mult, OP.add)
+    pick("hw", h0, h0 + A, "hq", 128, "il", 0, 2, "hq il0 il1", "hwn")
+    cp("ar posD", "aj0", T.aj[:, 64:160], T.ar[:].indirect(T.posD[:, 4:10]))
+    act("ar posD", "aj1", T.aj[:, 160:256], T.ar[:].indirect(T.posD[:, 10:16]), AF.Copy)
+    pick("fo", 0, A, "hq", 128, "fa", 0, 2, "hq fa", "foa")
+    op("V", "aj0 aj1", "ajt", V.transpose, T.ajt[:, 64:256], T.aj[:, 64:256])
+    tt("ajt sl", "adm", T.adm[:, 2:8], T.ajt[:, 64:256:32], T.sl[:, 2:8], OP.is_ge)
+    tt("adm tmp", "f1", T.f1[:, 2:8], T.adm[:, 2:8], T.tmp[:, 2:8], OP.mult)
+    tt("adm m8", "mw2", T.mw2[:, 2:8], T.adm[:, 2:8], T.m8[:, 2:8], OP.mult)
+    tt("f1 jw", "f2", T.f2[:, 2:8], T.f1[:, 2:8], T.jw[:, 2:8], OP.add)
+    act("mw2", "mn", T.mw3[:, 2:8], T.mw2[:, 2:8], AF.Identity, accum_out=mn)
+    cp("f2", "fin", T.fin[:, 2:8], T.f2[:, 2:8])
+    act("mn gn", "mgc", mgc, mn, AF.Identity, scale=gn, bias=-1.0)
     dma("S", "mgc", "mgo", T.mg[:], mgc)
 
-    pick("fo", 0, 128, "hw", 384, "fin", 0, 8, "hwo hwr hwn hwns fin", "fo")
-    mm(4, "qv", 0, "fo", 128, "qv fo fos")
-    dma("S", "fo", "oco", T.oc[:], T.fo[:].bitcast(dt.uint8))
+    pick("fo", A, 128, "hw", 384, "fin", 2, 8, "hwo hwr hwn hwns fin", "fo")
+    mm(5, "qv", 0, "fo", 128, "qv fo fos foa foas")
+    dma("S", "fo foa", "oco", T.oc[:], T.fo[:].bitcast(dt.uint8))
     for k in range(4):
-        dma("A", "fos", "osco%d" % k, T.osc[4 * k:4 * k + 4, :], T.fos[32 * k:32 * k + 4, :])
-    cp("ps4", "yo", T.yo[:], T.ps4[:, 0:128])
+        dma("A", "fos foas", "osco%d" % k, T.osc[4 * k:4 * k + 4, :], T.fos[32 * k:32 * k + 4, :])
+    cp("ps5", "yo", T.yo[:], T.ps5[:, 0:128])
     dma("S", "yo", "yout", T.y[:], T.yo[:])
     for s, v in count.items():
         if known["S"].get(s, 0) < v:

@@ -3,8 +3,31 @@ from concourse.mybir import dt, AluOpType, AxisListType, ActivationFunctionType
 
 F32, BF, U16, I32, MXC, U8 = "float32", "bfloat16", "uint16", "int32", "float8_e4m3fn_x4", "uint8"
 SCRATCH = {}
-KN = 2
 W0 = 2
+AIDES = "fnn"
+RANK = {
+    1: [[("S", "", (0, 1, 2), 0, 8)], [("C", "a0 a1 a2", None, 0, 8)], [("S", "a0 a1 a2", None, 0, 8)],
+        [("C", "b0 b1 b2 b3", None, 0, 8)]],
+    2: [[("L", "f0", None, 0, 8)], [("L", "f1", None, 0, 4), ("L", "n0", None, 4, 8)],
+        [("L", "f2", None, 0, 2), ("L", "f3", None, 2, 4), ("L", "n1", None, 4, 6), ("L", "n2", None, 6, 8)],
+        [("S", "f0 f1 f2 f3", (0,), 0, 8)],
+        [("C", "n0 n1 n2", (1,), 0, 8)],
+        [("S", "n0 n1 n2", (2,), 0, 8)],
+        [("C", "f1", None, 0, 2), ("C", "f2", None, 2, 4), ("C", "f3", None, 4, 6), ("C", "f0", None, 6, 8)]],
+    3: [[("C", "f1 f2 f3 n0 n1 n2 f0", None, 0, 8), ("W", "", (0, 1), 0, 8)]],
+}
+GATE = [6, [(2, 3)]]
+HAND = [
+    [(1, 0, [[("S", "b0 b1", 0, 8)]]),
+     (2, 3, [[("S", "f1", 0, 2), ("S", "f2", 2, 4), ("S", "f3", 4, 6), ("S", "f0", 6, 8)]]),
+     (3, 0, [[("S", "f1 f2 f3 f0", 0, 8)]])],
+    [(1, 0, [[("S", "b2", 0, 8)]]),
+     (2, 4, [[("C", "n0", 0, 4), ("C", "n1", 4, 8)], [("C", "n2", 0, 8)]]),
+     (3, 0, [[("S", "n0 n1 n2", 0, 8)]])],
+    [(1, 0, [[("S", "b3", 0, 8)]]),
+     (2, 5, [[("S", "n0", 0, 4), ("S", "n1", 4, 8)], [("S", "n2", 0, 8)]])],
+]
+SLOT, NEW = 32, 160
 
 
 def _buf(name, cols, dtype):
@@ -16,32 +39,27 @@ def _mx(name, cols):
     _buf(name + "s", cols, U8)
 
 
-for _n, _c in (("qx", 128), ("qn", 128), ("anc", 288), ("qtri", 128), ("qa2", 128), ("qe", 512), ("qz", 128), ("qab", 144),
-               ("qb2", 128), ("snd", 128), ("slots", 256), ("qw", 512), ("qv", 128), ("km", 128),
-               ("qs", 128), ("hq", 128), ("hw", 384), ("fo", 128)):
+for _n, _c in (("qx", 160), ("anc", 256), ("qtri", 128), ("qa2", 128), ("qe", 512), ("qz", 128), ("qab", 144),
+               ("snd", 128), ("slots", 288), ("qw", 512), ("qv", 152), ("km", 128),
+               ("hq", 128), ("hw", 416), ("via1", 128), ("via2", 128), ("via3", 128)):
     _mx(_n, _c)
-_buf("rl", 64, MXC)
-_buf("rls", 32, U8)
-_buf("rhs", 32, U8)
-_buf("ras", 32, U8)
-for _n, _c in (("xt", 512), ("wt", 2048), ("vt", 512), ("ztb", 768), ("att", 576), ("hot", 640), ("ones", 32),
-               ("pm1", 256), ("lx", 128), ("arow", 128), ("eq", 256), ("rr", 520), ("xc", 128),
-               ("t2", 96), ("us", 48), ("ax", 256), ("ar", 256), ("aj", 256), ("ajt", 256)):
+for _n, _c in (("wt", 2048), ("vt", 608), ("ztb", 1152), ("att", 576), ("hot", 640), ("dp", 128), ("da", 128), ("pk", 128),
+               ("pm1", 256), ("ih", 64), ("xs", 128), ("eqp", 256), ("eq", 256), ("thr", 64), ("t1", 160), ("rr", 520),
+               ("xc", 128), ("us", 48), ("pq", 32), ("land3", 64), ("ax", 256), ("ar", 256), ("aj", 256), ("ajt", 256)):
     _buf(_n, _c, BF)
-for _n, _c in (("R", 288), ("mrow", 32), ("thr", 64), ("t1", 64), ("kk", 1), ("pd", 160), ("n32", 8), ("tq", 8), ("sc", 16),
-               ("jr", 256), ("j7", 16), ("ab", 32), ("msk", 32), ("num", 32), ("qi", 8), ("qc", 32),
-               ("row8", 8), ("pf", 4), ("pc", 8), ("m8", 8), ("jw", 8), ("jn", 8),
-               ("lst", 8), ("landL", 32), ("tb", 128), ("tmp", 8), ("lohi", 4), ("sec", 4), ("land3", 32),
-               ("sl", 8), ("adm", 8), ("jf", 8), ("f1", 8), ("f2", 8), ("mw2", 8), ("mw3", 8), ("yo", 128)):
+for _n, _c in (("R", 288), ("mrow", 32), ("pd", 160), ("n32", 8), ("tq", 8), ("sc", 16),
+               ("jr", 256), ("j7", 16), ("ab", 32), ("msk", 32), ("num", 32), ("qc", 32),
+               ("pf", 8), ("m8", 16), ("r16", 16), ("mst", 8), ("jw", 8), ("jn", 8), ("lst", 8), ("landL", 32), ("axi", 16),
+               ("tb", 128), ("tmp", 16), ("sd", 16), ("sl", 8), ("adm", 16), ("f2", 16), ("jf", 8), ("mw3", 16),
+               ("yo", 128), ("viaL", 8)):
     _buf(_n, _c, F32)
-for _n, _c in (("il", 2), ("off", 10), ("ofo", 2), ("fs", 4), ("posD", 16), ("fin", 8), ("fa", 2)):
+for _n, _c in (("il", 2), ("off", 8), ("fs", 4), ("posD", 16), ("fin", 8), ("axl", 16), ("fa", 2), ("gl", 2)):
     _buf(_n, _c, U16)
-_buf("pi", 1, I32)
-_buf("pin", 4, I32)
 for _i in range(8):
     SCRATCH["ps%d" % _i] = ("psum", [128, 512], F32)
-SEMAPHORES = (["cV", "cA", "cP", "cG", "a1", "a2", "o1s", "l2", "c2r", "o2a", "o2b", "o2c", "m3", "o3a", "h3", "o3b", "o3c",
-               "ra", "rs", "rc", "rk", "hl"] + ["d%d" % _i for _i in range(12)])
+SEMAPHORES = (["cV", "cA", "cP", "cG", "a1", "a2", "c2", "m3", "h3", "o1", "o2", "o3", "om", "ol", "hl", "lh"]
+              + ["d%d" % _i for _i in range(14)] + ["l%d" % _i for _i in range(4)]
+              + ["k%d%d" % (_r, _i) for _r in (1, 2, 3) for _i in range(8)])
 
 
 def move(topo, cores, engines, sem, src, dst):
@@ -60,36 +78,69 @@ def plan(own, r, T, topo):
         order = [r ^ sum((c >> (2 - i) & 1) << b[i] for i in range(3)) for c in range(8)]
         if all(topo.same_plane(topo.chip(own), topo.chip(T.cores[q])) for q in order[1:4]):
             break
-    near, far = [T.cores[q] for q in order[1:4]], [T.cores[q] for q in order[4:]]
-    rest = sorted([c for c in topo.cores_of(own) if c != own], key=lambda c: topo.die(c) == topo.die(own))
-    f = [c for c in rest if all(topo.may_write(c, d) for d in far)][:2]
-    n = [c for c in rest if c not in f and all(topo.may_write(c, d) for d in near)]
-    return order, near, far, [f[0], n[0]]
+    cores = [T.cores[q] for q in order]
+    H = len(cores) // 2
+    name = {}
+    ahead = [cores.index(d) for d in longest_first(topo, own, cores[1:])]
+    for k, cs in (("a", [c for c in ahead if order[c] // H == r // H]), ("b", [c for c in ahead if order[c] // H != r // H]),
+                  ("n", range(1, H)), ("f", range(H, 2 * H))):
+        name.update(("%s%d" % (k, i), c) for i, c in enumerate(cs))
+    rest = sorted([c for c in topo.cores_of(own) if c != own], key=lambda c: topo.die(c) != topo.die(own))
+    every = [c for c in rest if all(topo.may_write(c, d) for d in cores[1:])]
+    some = [c for c in rest if c not in every and all(topo.may_write(c, d) for d in cores[1:H])]
+    aides = [(every if k == "f" else some).pop(0) for k in AIDES]
+    return order, name, aides
 
 
-def hand_on(g, core, r, role, near, far, T, topo):
-    S, CAPP, A = T.sem, 16, 32
-    goal = near if role else far
-    s0 = 128 + CAPP * (len(T.cores) - 1 - r)
-    eng = topo.engines(core, goal[0])
-    H = len(T.cores) // 2
-    late, a0 = [d for d in near + far if T.rank_of(d) // H != r // H][role:role + 1], A * (H + r % H)
-    g.wait_ge(S.ra, 8)
-    g.remote_dma_fused([move(topo, late, eng, S.a2, T.ras[:, 0:A], T.ancs[:, a0:a0 + A])], local_sem=S.hl)
-    g.wait_ge(S.rc, 8)
-    some = goal[:KN] if role else goal
-    k = len(eng) // len(some)
-    g.remote_dma_fused([move(topo, [d], eng[k * i:k * i + k], S.c2r, T.rl[:, CAPP * i:CAPP * (i + 1)].bitcast(dt.uint8),
-                             T.slots[:, s0:s0 + CAPP].bitcast(dt.uint8)) for i, d in enumerate(some)], local_sem=S.hl)
-    g.wait_ge(S.rs, 4)
-    some = goal[:KN] if role else goal[:1]
-    k = len(eng) // len(some)
-    g.remote_dma_fused([move(topo, [d], eng[k * i:k * i + k], S.c2r, T.rls[:, CAPP * i:CAPP * (i + 1)],
-                             T.slotss[:, s0:s0 + CAPP]) for i, d in enumerate(some)], local_sem=S.hl)
-    g.wait_ge(S.rk, 8)
-    g.remote_dma_fused([move(topo, longest_first(topo, core, goal), eng, S.h3, T.rhs[:, 0:A],
-                             T.hws[:, 128 + A * r:128 + A * r + A])], local_sem=S.hl)
-    g.wait_ge(S.hl, 4 * len(eng))
+def raw(T, buf, a, n):
+    return T[buf][:, a:a + n].bitcast(dt.uint8)
+
+
+def sides(T, rnd, kind, r, c, n=1, via=False):
+    N, A, CAPP = len(T.cores), 32, 16
+    H = N // 2
+    if kind == "L":
+        at = 4 * (N - 1 - r)
+        return (T.viaL if via else T.lst)[:, c:c + n], T.landL[:, at:at + 1]
+    if rnd == 1:
+        src, a, w, dst, b = "slots", 0, A, "anc", A * (r % H + H * (1 - c))
+    elif rnd == 2:
+        src, a, w, dst, b = "snd", CAPP * c, CAPP * n, "slots", SLOT + 128 + CAPP * (N - 1 - r)
+    else:
+        src, a, w, dst, b = "hq", 128 - A, A, "hw", NEW + A * r
+    if via:
+        src = "via%d" % rnd
+    one = CAPP if rnd == 2 else A
+    if kind == "C":
+        return raw(T, src, a, w), raw(T, dst, b, one)
+    if kind == "W":
+        a, w = 0, 4 * A
+    return T[src + "s"][:, a:a + w], T[dst + "s"][:, b:b + one]
+
+
+def there(rnd, kind, rank, call):
+    return "l%s" % call if kind == "L" else ("a2" if rank[0] == "b" else "a1", "c2", "h3")[rnd - 1]
+
+
+def moves(T, topo, rnd, call, k, r, order, name, eng, via):
+    out = []
+    for kind, names, lo, hi in call:
+        names = names.split()
+        src, dst = sides(T, rnd, kind, r, int(names[0][0] == "b") if rnd == 1 else name[names[0]], via=via)
+        out.append(move(topo, [T.cores[order[name[n]]] for n in names], eng[lo:hi], T.sem[there(rnd, kind, names[0], k)],
+                        src, dst))
+    return out
+
+
+def hand_on(g, core, r, role, order, name, T, topo):
+    eng = topo.engines(core, T.cores[order[1]])
+    sent = 0
+    for rnd, k, calls in HAND[role]:
+        g.wait_ge(T.sem["k%d%d" % (rnd, k)], sum(m[4] - m[3] for m in RANK[rnd][k] if m[2] and role in m[2]))
+        for call in calls:
+            g.remote_dma_fused(moves(T, topo, rnd, call, "h", r, order, name, eng, True), local_sem=T.sem.hl)
+            sent += sum(m[3] - m[2] for m in call)
+    g.wait_ge(T.sem.hl, sent)
 
 
 def rank_program(g, core, T, topo):
@@ -99,10 +150,10 @@ def rank_program(g, core, T, topo):
     if not mine:
         return
     r = T.rank_of(mine[0])
-    order, near, far, aides = plan(mine[0], r, T, topo)
+    order, name, aides = plan(mine[0], r, T, topo)
     if core != mine[0]:
         if core in aides:
-            hand_on(g, core, r, aides.index(core), near, far, T, topo)
+            hand_on(g, core, r, aides.index(core), order, name, T, topo)
         return
     OP, AF, X = AluOpType, ActivationFunctionType, AxisListType.X
     V, AC, PE, SY = g.vector, g.scalar, g.tensor, g.sync
@@ -172,13 +223,35 @@ def rank_program(g, core, T, topo):
     width = len(eng)
     side = [e for e in topo.engines(core, aides[0]) if e not in eng]
 
-    def send(rd, loc, *moves):
-        before("G", rd.split(), [])
-        g.remote_dma_fused([move(topo, c, e, S[s], src, dst) for c, e, s, src, dst in moves], local_sem=S[loc])
-        count[loc] = count.get(loc, 0) + sum(len(m[1]) for m in moves)
+    def send(rnd, k):
+        call, rd = RANK[rnd][k], []
+        out = moves(T, topo, rnd, [m[:2] + m[3:] for m in call if not m[2]], k, r, order, name, eng, False)
+        for kind, names, to, lo, hi in call:
+            cs = [name[n] for n in names.split()] or [0]
+            if rnd == 2:
+                rd += [{"L": "lst", "C": "snd%s", "S": "snd%ss"}[kind].replace("%s", n[0]) for n in names.split()] + ["l3z"]
+            else:
+                rd.append("qn" if rnd == 1 else "hq")
+            if to:
+                out.append(move(topo, [aides[i] for i in to], side[lo:hi], S["k%d%d" % (rnd, k)],
+                                sides(T, rnd, kind, r, cs[0], len(cs))[0], sides(T, rnd, kind, r, cs[0], len(cs), True)[0]))
+        before("G", rd, [])
+        loc = "ol" if (rnd, k) in GATE[1] else "o%d" % rnd
+        g.remote_dma_fused(out, local_sem=S[loc])
+        count[loc] = count.get(loc, 0) + sum(m[4] - m[3] for m in call)
 
-    def raw(name, a, n):
-        return T[name][:, a:a + n].bitcast(dt.uint8)
+    def arrivals(rnd):
+        got = [(k, m[:2] + m[3:]) for k, call in enumerate(RANK[rnd]) for m in call if not m[2]]
+        got += [("h", m) for role in HAND[:len(aides)] for q, k, calls in role if q == rnd for call in calls for m in call]
+        tot = {}
+        for k, (kind, names, lo, hi) in got:
+            for n in names.split():
+                e = tot.setdefault(there(rnd, kind, n, k), [0, []])
+                e[0] += hi - lo
+                e[1].append("%s%d_%d" % (kind, rnd, order[name[n]]))
+        for s, (n, keys) in tot.items():
+            arrive(s, n, " ".join(keys + [s]))
+        return tot
 
     def ts(rd, wr, out, in0, s1, s2, *ops):
         op("V", rd, wr, V.tensor_scalar, out, in0, s1, s2, *ops)
@@ -216,102 +289,97 @@ def rank_program(g, core, T, topo):
         else:
             act("ps%d" % bank, wr, out, src, AF.Relu, scale=0.0625)
 
-    def zz(n, lo=0, hi=128):
-        return T.ztb[lo:hi, 128:128 + n]
+    Z = 640
 
-    def const(wr, out, n, c, rd="", lo=0, hi=128):
-        act("zz " + rd, wr, out, zz(n, lo, hi), AF.Identity, bias=c)
+    def zz(n):
+        return T.ztb[:, Z:Z + n]
 
-    n0 = 128 - A
-    dma("S", "", "xa", T.ztb[:, 640:768], T.x[:, 0:4 * A])
-    dma("S", "", "xt", T.xt[:], T.x[:])
+    pp, sg, lo, hi, pm, khi = [T.pf[:, i:i + 1] for i in range(6)]
+    p31 = T.pq[:, 0:1]
+    dma("S", "", "xa", T.ztb[:, 512:Z], T.x[:, 0:4 * A])
+    iota("xc", T.xc[:], [[1, 128]])
+    iota("pp", pp, [[0, 1]], 0, 1)
+    iota("pk", T.pk[:], [[0, 8], [1, CAPP]])
+    fill("", "zz", T.ztb[:, Z:], 0.0)
+    dma("S", "zz", "xt", T.ztb[:, 4 * A:512], T.x[:, 4 * A:])
+    dma("S", "", "xd", T.ztb[:, 0:4 * A], T.x[:, 4 * A:8 * A])
     dma("S", "", "wt0", T.wt[:, 0:512 * W0], T.w[:, 0:512 * W0])
-    op("G", "", "pi", g.iota, T.pi[:], [[0, 1]], 0, 1)
-    iota("qi", T.qi[:], [[order[c] - r, 2] for c in (4, 2, 1)], r)
-    iota("xc", T.xc[:], [[1, 128]], 128)
-    fill("", "zz ztb", T.ztb[:, 0:640], 0.0)
     fill("", "att", T.att[:], 0.0)
-    ts("pi", "pin", T.pin[:, 0:1], T.pi[:], 15, None, OP.bitwise_and)
-    quant("qn", 0, 128, "ztb", "xa zz", "qn", at=256)
+    act("xc pp", "dp", T.dp[:], T.xc[:], AF.Abs, scale=-1.0, bias=pp)
+    op("V", "xc", "p31", V.transpose, T.pq[:], T.xc[:, 0:32])
+    act("dp att", "e", T.att[:, 4:516:4], T.dp[:], AF.Relu, scale=-0.5, bias=0.5)
+    quant("slots", 0, 128, "ztb", "xa zz", "qn", at=512)
 
     H = N // 2
-    p1 = A * (r % H)
-    p2 = p1 + A * H
-    first = [c for c in ahead if T.rank_of(c) // H == r // H]
-    late = [c for c in others if c not in first]
-    send("qn", "o1s", (aides, side, "ra", T.qns[:, n0:128], T.ras[:]))
-    send("qn", "o1s", (first, eng, "a1", raw("qn", n0, A), raw("anc", p1, A)))
-    send("qn", "o1s", (first, eng, "a1", T.qns[:, n0:128], T.ancs[:, p1:p1 + A]))
-    send("qn", "o1s", (late[len(aides):], eng, "a2", T.qns[:, n0:128], T.ancs[:, p2:p2 + A]))
-    send("qn", "o1s", (longest_first(topo, core, late), eng, "a2", raw("qn", n0, A), raw("anc", p2, A)))
-    arrive("a1", 2 * width * len(first), "anc1")
-    arrive("a2", 2 * width * len(late), "anc2")
-    left("o1s")
+    p1 = A * (H + r % H)
+    h0 = NEW + A * r
+    W = 130
+    for k in range(len(RANK[1])):
+        send(1, k)
+    arrivals(1)
+    left("o1")
     dma("S", "", "wt1", T.wt[:, 512 * W0:], T.w[:, 512 * W0:])
-    dma("S", "", "vt", T.vt[:], T.v[:])
+    dma("S", "", "vt", T.vt[:, 0:512], T.v[:])
 
+    iota("axi", T.axi[:], [[8 * 512, N], [0, 2]])
+    op("G", "zz", "thr1", g.affine_select, T.thr[:, 32:64], zz(32), [[0, 32]], OP.is_gt, tiny, 96, -1)
+    iota("t10 t1a t2", T.t1[0:32, 32:160], [[0, 128]], 4)
     for k in range(4):
-        act("qi", "qc%d" % k, T.qc[:, k // 2 * 16 + k % 2:k // 2 * 16 + 16:2], T.qi[:], AF.Copy)
-    for k in range(2):
-        act("xc", "pm1%d" % k, T.pm1[:, k:32:2], T.xc[:, 0:16], AF.Identity, scale=-1.0, bias=192.0 + CAPP)
-    const("thr1", T.thr[:, 32:64], 32, 0.0)
-    act("pm10 pm11", "pm12", T.pm1[:, 32:64], T.pm1[:, 0:32], AF.Copy)
-    const("kk", T.kk[:], 1, 1.0 - KM)
-    ts("pin", "il0", T.il[:, 0:1], T.pin[:, 0:1], 0, None, OP.add)
-    ts("pin", "il1", T.il[:, 1:2], T.pin[:, 0:1], 16, None, OP.add)
-    ts("pi", "p128", T.pf[:, 3:4], T.pi[:], 128.0, None, OP.add)
-    ts("pi", "pin1", T.pin[:, 1:2], T.pi[:], 4, None, OP.arith_shift_right)
-    act("pm12", "pm13", T.pm1[:, 64:128], T.pm1[:, 0:64], AF.Copy)
-    for a, k in ((p1, "own"), (N * A, "pad")):
-        pick("anc", a, a + A, "qn", 128, "il", 0, 2, "qn il0 il1", "anc" + k, at=n0)
-    act("pm13", "pm1", T.pm1[:, 128:256], T.pm1[:, 0:128], AF.Copy)
-    quant("qx", 0, 128, "xt", "xt", "qx")
-    act("xt", "xt", T.xt[:, 0:4 * A], T.xt[:, 4 * A:8 * A], AF.Copy)
-    ts("pi", "pin2", T.pin[:, 2:3], T.pi[:], 31, None, OP.bitwise_and)
-    cp("pin", "pm", T.pf[:, 0:1], T.pin[:, 0:1])
-    ts("xc p128", "att", T.att[:, 0:512:4], T.xc[:], T.pf[:, 3:4], None, OP.is_ge)
-    cp("pin1", "ph16", T.pf[:, 1:2], T.pin[:, 1:2])
-    ts("xc p128 att", "cid", T.att[:, 2:512:4], T.xc[:], T.pf[:, 3:4], 64.0, OP.is_equal, OP.mult)
-    ts("pin2", "p31", T.pf[:, 2:3], T.pin[:, 2:3], 128.0, None, OP.add)
-    quant("qs", 0, 128, "xt", "xt", "qs")
-    quant("qtri", 0, 128, "att", "att cid", "qtri")
-    const("t10", T.t1[0:32, 32:64], 32, 0.0, hi=32)
-    const("t20", T.t2[0:32, 64:96], 32, 0.0, hi=32)
-    const("thr2", T.thr[96:128, 32:64], 32, tiny, "thr1", lo=96)
-    const("kk0", T.kk[0:32, :], 1, 1000.0, "kk", hi=32)
-    if r >= H:
-        const("pdz", T.pd[:, 0:128], 128, -9.0e29)
-    act("ph16", "khi", T.pc[:, 0:1], T.pf[:, 1:2], AF.Copy, scale=16.0)
-    act("pm", "a65", T.pc[:, 4:5], T.pf[:, 0:1], AF.Identity, scale=-1.0, bias=64.0 + CAPP)
-    act("zz pm", "num0", T.num[:, 0:16:2], zz(8), AF.Identity, bias=T.pf[:, 0:1])
-    act("zz khi", "num1", T.num[:, 1:16:2], zz(8), AF.Identity, bias=T.pc[:, 0:1])
-    const("num3", T.num[:, 17:32:2], 8, 32.0)
-    const("n32", T.n32[:], 8, -float(A))
-    ts("xc p31", "thr0", T.thr[:, 0:32], T.xc[:, 0:32], T.pf[:, 2:3], tiny, OP.is_lt, OP.mult)
-    fill("", "cid att", T.att[:, 2:512:4], 0.0)
-    ts("p31", "hp", T.pc[:, 3:4], T.pf[:, 2:3], 143.5, float(rr % 2), OP.is_gt, OP.is_equal)
-    ts("xc p128 att", "e", T.att[:, 4:516:4], T.xc[:], T.pf[:, 3:4], 0.5, OP.is_equal, OP.mult)
-    pick("slots", 0, CAPP, "qn", n0, "il", 0, 1, "qn il0", "slz")
+        iota("qc%d" % k, T.qc[:, k // 2 * 16 + k % 2:k // 2 * 16 + 16:2], [[order[c] - r, 2] for c in (4, 2, 1)], r)
+    iota("n32", T.n32[:], [[0, 8]], -A)
+    iota("num3", T.num[:, 17:32:2], [[0, 8]], 32)
+    iota("pm1", T.pm1[:], [[0, 8], [-1, CAPP], [0, 2]], 64 + CAPP)
+    iota("r16", T.r16[:], [[16, 8], [0, 2]])
+    iota("l3z", T.land3[:], [[0, 64]])
+    iota("vz", T.vt[:, 512:608], [[0, 96]])
+    iota("ih", T.ih[:], [[0, 2], [-512, 16], [-8192, 2]], -8192)
+    iota("rrz", T.rr[:, 0:W + 1:W], [[0, 2]])
+    iota("admz", T.adm[:], [[0, 16]])
+
+    act("p31", "sg", sg, p31, AF.Sign, bias=-15.5)
+    act("sg", "hi", hi, sg, AF.Identity, scale=-256.0, bias=-256.0)
+    act("hi p31", "pm", pm, hi, AF.Identity, scale=1.0 / 32, bias=p31)
+    act("sg", "lo", lo, sg, AF.Identity, scale=256.0, bias=-256.0)
+    act("xc", "xs", T.xs[:], T.xc[:], AF.Identity, scale=1.0 / 512, bias=0.25)
+    act("pm pp", "khi", khi, pm, AF.Identity, scale=-1.0, bias=pp)
+    act("zz pm", "num0", T.num[:, 0:16:2], zz(8), AF.Identity, bias=pm)
+    act("pk pm", "da", T.da[:], T.pk[:], AF.Abs, scale=-1.0, bias=pm)
+    act("zz khi", "num1", T.num[:, 1:16:2], zz(8), AF.Identity, bias=khi)
     for b in range(4):
         quant("qe", 128 * b, 128, "att", "att e", "qe%d" % b, at=4 - b)
-        mm(4 + b, "qe", 128 * b, "qn", 128, "qe%d qn" % b, stop=False)
+        mm(4 + b, "qe", 128 * b, "slots", 128, "qe%d qn" % b, stop=False)
+        if b == 1:
+            ts("xc pm", "il", T.il[:], T.xc[:, 0:17:16], pm, None, OP.add)
+        if b == 2:
+            pick("anc", p1, p1 + A, "slots", A, "il", 0, 2, "qn il", "ancown")
+    ts("xc pp", "att e", T.att[:, 0:512:4], T.xc[:], pp, None, OP.is_ge)
+    act("dp qe3", "cid", T.att[:, 2:512:4], T.dp[:], AF.Relu, scale=-64.0, bias=64.0)
+    if r >= H:
+        act("zz", "pdz", T.pd[:, 0:128], zz(128), AF.Identity, bias=-9.0e29)
+    act("xc pm", "jw", T.jw[:], T.xc[:, 0:128:16], AF.Identity, bias=pm)
+    quant("qx", 0, 160, "ztb", "xa xt xd", "qx")
+    quant("qtri", 0, 128, "att", "att cid", "qtri")
+    ts("xc p31", "thr0", T.thr[:, 0:32], T.xc[:, 0:32], p31, tiny, OP.is_lt, OP.mult)
+    act("da", "att", T.att[:, 0:512:4], T.da[:], AF.Relu, scale=-1.0, bias=1.0)
+    act("da", "cid", T.att[:, 2:512:4], T.da[:], AF.Relu, scale=-1.0, bias=1.0)
     quant("qw", 0, 128 * W0, "wt", "wt0", "qw0")
     for i in range(W0):
-        mm(2 + i % 2, "qw", 128 * i, "qx", 128, "qw0 qx")
-        layer(i, 4 * A, 128, "ho%d" % i, 2 + i % 2, False)
-    ts("pm1 a65", "att e", T.att[:, 0:512:2], T.pm1[:], T.pc[:, 4:5], None, OP.is_equal)
-    quant("qa2", 0, 128, "att", "att", "qa2")
+        mm(2 + i % 2, "qw", 128 * i, "qx", 128, "qw0 qx", xv=A)
+        layer(i, 0, 128, "ho%d" % i, 2 + i % 2, False)
+    ts("khi", "gl", T.gl[:, 0:1], khi, 1.0 / 8, 1.0, OP.mult, OP.add)
+    quant("qa2", 0, 128, "att", "att cid", "qa2")
+    ts("axi hi", "axl", T.axl[:], T.axi[:], hi, 1.0 / 512, OP.subtract, OP.mult)
 
-    best, q1, o1, st2, st, pl, ph, q32, gn, mn, mgc, q0, b0, qx, bx = [T.sc[:, i:i + 1] for i in range(15)]
+    best, q1, o1, st2, st, q32, gn, mgc, q0, b0, qx, bx, o0 = [T.sc[:, i:i + 1] for i in range(13)]
     M, u, d16 = T.R[:, 287:288], T.us[:, 47:48], T.num[:, 16:17]
     M1 = T.R[:, 127:128]
-    mm(0, "qs", 0, "anc", 128, "qs anc1 ancown ancowns")
+    mm(0, "qx", 0, "anc", 128, "qx a1 ancown ancowns", xv=128)
     op("V", "ps0 zz", "R1", V.tensor_tensor_scan, T.R[:, 0:128], T.ps0[:, 0:128], zz(128), -9.0e29, OP.max, OP.add)
     if r >= H:
         act("R1 zz", "pd", T.pd[:, 128:160], zz(A), AF.Identity, bias=M1)
         act("R1", "q0 j7", T.j7[:, 0:H], T.R[:, A - 1:H * A:A], AF.Sign, bias=M1, scale=-1.0, accum_out=q0)
         act("R1", "b0 jr", T.jr[:, 0:128], T.R[:, 0:128], AF.Sign, bias=M1, scale=-1.0, accum_out=b0)
-    mm(1, "qs", 0, "anc", 160, "qs anc2 ancpad ancpads", xv=128)
+    mm(1, "qx", 0, "anc", 160, "qx a2 a1 ancown ancowns")
     if r >= H:
         op("V", "ps1 pd pdz", "R", V.tensor_tensor_scan, T.R[:, 128:288], T.ps1[:, 0:160], T.pd[:], -9.0e29, OP.max, OP.max)
     else:
@@ -319,7 +387,7 @@ def rank_program(g, core, T, topo):
     op("V", "R", "m0", V.transpose, T.mrow[:], T.R[:, 256:288])
     flag = T.j7[:, N - 1:N]
     if r >= H:
-        act("R", "qx fl", T.j7[:, H:N], T.R[:, (H + 1) * A - 1:N * A:A], AF.Sign, bias=M, scale=-1.0, accum_out=qx)
+        act("R", "qq fl", T.j7[:, H:N], T.R[:, (H + 1) * A - 1:N * A:A], AF.Sign, bias=M, scale=-1.0, accum_out=qx)
     else:
         act("R R1", "q1 j7", T.j7[:, 0:N], T.R[:, A - 1:N * A:A], AF.Sign, bias=M, scale=-1.0, accum_out=q1)
 
@@ -330,13 +398,12 @@ def rank_program(g, core, T, topo):
         return T.R[32 * q:32 * (q + n), 287:288]
 
     ts("R m0", "t1a", T.t1[:, 0:32], T.mrow[:], M, -1.0, OP.subtract, OP.mult)
-    for a in (1, 2):
-        act("R m0", "t1%d" % a, quad("t1", a, 32), quad("mrow", a + 1, 0), AF.Identity, scale=-1.0, bias=top(a))
+    for a, b in ((1, 2), (2, 3), (3, 2)):
+        act("R m0", "t1%d" % a, quad("t1", a, 32), quad("mrow", b, 0), AF.Identity, scale=-1.0, bias=top(a))
     if r >= H:
-        act("qx fl q0", "q1", q1, flag, AF.Identity, scale=q0, bias=qx)
-    ts("R m0", "t13", quad("t1", 3, 32), quad("mrow", 2, 0), top(3), -1.0, OP.subtract, OP.mult)
-    ts("R m0", "t21", quad("t2", 1, 64), quad("mrow", 3, 0), top(1), None, OP.is_gt)
-    ts("R m0", "t22", quad("t2", 2, 64, 2), quad("mrow", 0, 0, 2), top(2, 2), None, OP.is_ge)
+        act("qq fl q0", "q1", q1, flag, AF.Identity, scale=q0, bias=qx)
+    ts("R m0", "t21", quad("t1", 1, 128), quad("mrow", 3, 0), top(1), None, OP.is_gt)
+    ts("R m0", "t22", quad("t1", 2, 128, 2), quad("mrow", 0, 0, 2), top(2, 2), None, OP.is_ge)
     act("q1 qc0 qc1 qc2 qc3", "ab", T.ab[:], T.qc[:], AF.Abs, bias=q1, scale=-1.0)
     if r >= H:
         act("R", "bx jr2", T.jr[:, 128:256], T.R[:, 128:256], AF.Sign, bias=M, scale=-1.0, accum_out=bx)
@@ -347,147 +414,131 @@ def rank_program(g, core, T, topo):
         act("bx fl b0", "best", best, flag, AF.Identity, scale=b0, bias=bx)
     act("tq best", "num2", T.num[:, 16:32:2], T.tq[:], AF.Identity, bias=best)
     act("q1", "q32", q32, q1, AF.Copy, scale=float(A))
-    act("q1 best", "gn", gn, q1, AF.Identity, scale=128.0 - A, bias=best)
-    tt("t1a t11 t12 t13 t10 thr0 thr1 thr2", "t2", T.t2[:, 0:64], T.t1[:], T.thr[:], OP.is_lt)
-    op("V", "t2 t20 t21 t22 kk kk0", "u", V.tensor_tensor_scan, T.us[:], T.t2[:, 0:48], T.t2[:, 48:96], T.kk[:],
+    act("r16 khi", "m7", T.sd[:], T.r16[:], AF.Abs, scale=-1.0, bias=khi)
+    tt("t1a t11 t12 t13 t10 thr0 thr1", "t2", T.t1[:, 64:128], T.t1[:, 0:64], T.thr[:], OP.is_lt)
+    op("V", "t2 t10 t21 t22", "u", V.tensor_tensor_scan, T.us[:], T.t1[:, 64:112], T.t1[:, 112:160], 1.0 - KM,
        OP.add, OP.add)
-    ts("ab u ztb", "ztv", T.ztb[:, 96:128:2], T.ab[:, 0:16], u, 0.5, OP.max, OP.is_lt)
-    quant("qz", 0, 128, "ztb", "ztv ztb", "qz", at=96)
+    ts("ab u zz", "ztv", T.ztb[:, Z + 480:Z + 512:2], T.ab[:, 0:16], u, 0.5, OP.max, OP.is_lt)
+    quant("qz", 0, 128, "ztb", "ztv zz", "qz", at=Z)
     mm(1, "qtri", 0, "qz", 128, "qtri qz")
     ts("ab", "msk", T.msk[:], T.ab[:], 0.5, None, OP.is_lt)
-    op("V", "ps1", "o1", V.tensor_reduce, o1, T.ps1[:, 0:8], X, OP.max)
+    op("V", "ps1", "o1v", V.tensor_reduce, o1, T.ps1[:, 120:128], X, OP.max)
+    act("o1v", "st2", st2, o1, AF.Abs, bias=-(64.5 + CAPP / 2))
+    act("o1v", "o0", o0, o1, AF.Identity, bias=-65.0)
+    act("m7", "m8", T.m8[:], T.sd[:], AF.Relu, scale=-1.0, bias=1.0)
     tt("msk num0 num1 num2 num3", "bt e", T.att[:, 512:576:2], T.msk[:], T.num[:], OP.mult)
-    ts("pm1 o1", "at0 att", T.att[:, 0:512:2], T.pm1[:], o1, None, OP.is_equal)
+    ts("pm1 o1v", "at0 att cid", T.att[:, 0:512:2], T.pm1[:], o1, None, OP.is_equal)
     quant("qab", 0, 144, "att", "att at0 bt", "qab")
     mm(2, "qab", 0, "qab", 128, "qab", xv=16)
-    ts("o1", "st2", st2, o1, 64.0 + CAPP + 0.5, None, OP.is_lt)
-    act("xc", "row8", T.row8[:], T.xc[:, 0:8], AF.Identity, bias=-128.0)
-    act("gn", "gn", gn, gn, AF.Identity, bias=1.0)
-    act("pm", "a0", T.pc[:, 1:2], T.pf[:, 0:1], AF.Identity, bias=16.0)
-    act("pm", "a1c", T.pc[:, 2:3], T.pf[:, 0:1], AF.Identity, bias=32.0)
-    const("rrz", T.rr[:, 260:391:130], 2, 0.0)
-    const("ones", T.ones[:], 32, 1.0)
+    ts("st2", "st", st, st2, CAPP / 2, None, OP.is_lt)
+    for k, v in enumerate((d16, q32)):
+        act("m8 vz num2 q32", "w2%d" % k, T.vt[:, 512 + 2 * k:576:4], T.m8[:], AF.Copy, scale=v)
+    act("m8 st", "mst", T.mst[:], T.m8[:, 0:16:2], AF.Copy, scale=st)
 
-    ts("ps2 hp", "lst", T.lst[:], T.ps2[:, 120:128], T.pc[:, 3:4], None, OP.mult)
-    cp("ps2", "off", T.off[:, 1:9], T.ps2[:, 112:120])
-    send("lst", "o2a", *[([others[c - 1]], eng[c - 1:c], "l2", T.lst[:, c:c + 1], T.landL[:, 4 * rr:4 * rr + 1])
-                         for c in range(1, N)])
-    ts("o1 st2", "st", st, o1, 64.5, st2, OP.is_gt, OP.mult)
-    away, half, hs = CAPP * (N - 1), CAPP * H, len(side) // 2
-    pick("snd", 0, away, "qx", 128, "off", 2, 9, "qx off", "snd")
+    ts("ps2 lo hi", "lst", T.lst[:], T.ps2[:, 120:128], hi if rr % 2 else lo, None, OP.mult)
+    cp("ps2", "off", T.off[:], T.ps2[:, 112:120])
+    lists = [k for k, call in enumerate(RANK[2]) if call[0][0] == "L"]
+    for k in lists:
+        send(2, k)
+    half = CAPP * H
+    pick("snd", half, 2 * half, "qx", 128, "off", H, N, "qx off", "sndf")
+    pick("snd", 0, half, "qx", 128, "off", 0, H, "qx off", "sndn")
+    for k in range(len(lists), len(RANK[2])):
+        if k == GATE[0]:
+            g.wait_ge(S.ol, count["ol"])
+            known["S"]["ol"] = count["ol"]
+        send(2, k)
+    got = arrivals(2)
 
-    def sc(c, n=1):
-        return T.snds[:, CAPP * c:CAPP * (c + n)]
-
-    send("snd", "o2b", (aides[:1], side, "rc", raw("snd", away - half, half), raw("rl", 0, half)))
-    send("snd", "o2b", (near[KN:], eng[N - 1:], "c2r", raw("snd", KN * CAPP, CAPP), raw("slots", s0, CAPP)))
-    send("snd", "o2b", (aides[1:], side, "rc", raw("snd", 0, KN * CAPP), raw("rl", 0, KN * CAPP)))
-    send("snds", "o2c", (aides[:1], side[:hs], "rs", sc(H - 1, KN), T.rls[:]), (aides[1:], side[hs:], "rs", sc(0, KN), T.rls[:]))
-    send("snds", "o2c", *[([others[c]], eng[2 * i:2 * i + 2], "c2r", sc(c), T.slotss[:, s0:s0 + CAPP])
-                          for i, c in enumerate(list(range(H, N - 1)) + [KN])])
-    arrive("l2", N - 1, "landL")
-    arrive("c2r", 5 * width + len(eng[N - 1:]), "slots")
-
-    cp("off", "ofo", T.ofo[:, 0:1], T.off[:, 1:2])
-    act("lst", "lown", T.landL[:, 4 * rr:4 * rr + 1], T.lst[:, 0:1], AF.Copy)
-    ts("row8 ph16", "m8", T.m8[:], T.row8[:], T.pf[:, 1:2], None, OP.is_equal)
+    act("lst", "L2_%d" % r, T.landL[:, 4 * rr:4 * rr + 1], T.lst[:, 0:1], AF.Copy)
+    act("mst vz o0", "w0", T.vt[:, 576:608:4], T.mst[:], AF.Copy, scale=o0)
+    act("mst vz", "w1", T.vt[:, 578:608:4], T.mst[:], AF.Copy, scale=-float(s0 + CAPP))
     quant("qw", 128 * W0, 512 - 128 * W0, "wt", "wt1", "qw1", at=512 * W0)
-    pick("slots", s0, s0 + CAPP, "qx", 128, "ofo", 0, 1, "qx ofo", "slown")
-    for k, (a, v) in enumerate(((0, d16), (4, d16), (2, q32), (6, q32))):
-        act("m8 ztb num2 q32", "w2%d" % k, T.ztb[:, a:64:8], T.m8[:], AF.Copy, scale=v)
-    ts("o1 st", "pl", pl, o1, -64.0, st, OP.add, OP.mult)
-    ts("st", "ph", ph, st, -float(s0 + 2 * CAPP), float(CAPP), OP.mult, OP.add)
-    ts("p31", "lo", T.lohi[:, 0:1], T.pf[:, 2:3], 143.5, -1.0, OP.is_lt, OP.mult)
-    ts("p31", "hi", T.lohi[:, 1:2], T.pf[:, 2:3], 143.5, -1.0, OP.is_gt, OP.mult)
+    pick("slots", SLOT + s0, SLOT + s0 + CAPP, "qx", 128, "off", 0, 1, "qx off", "slown")
     for i in range(W0, 4):
-        mm(i % 2, "qw", 128 * i, "qx", 128, "qw1 qx")
-        layer(i, 4 * A, 128, "ho%d" % i, i % 2)
-    quant("qv", 0, 128, "vt", "vt", "qv")
+        mm(i % 2, "qw", 128 * i, "qx", 128, "qw1 qx", xv=A)
+        layer(i, 0, 128, "ho%d" % i, i % 2, False)
+    act("jw", "jn", T.jn[:], T.jw[:], AF.Identity, scale=-1.0, bias=NEW + 16.0)
+    act("q1 best", "gn", gn, q1, AF.Identity, scale=128.0 - A, bias=best)
+    act("jw", "jw2", T.tmp[:, 5:16:2], T.jw[:, 2:8], AF.Copy)
+    act("jw", "jf2", T.jf[:, 2:4], T.jw[:, 0:2], AF.Identity, bias=64.0)
+    act("gn", "gn", gn, gn, AF.Identity, bias=1.0)
 
-    for c in range(4):
+    when = {key: i for i, s in enumerate(got) for key in got[s][1]}
+    pair = [["L2_%d" % (N - 1 - 2 * c - k) for k in range(2)] for c in range(H)]
+    for i, c in enumerate(sorted(range(H), key=lambda c: max(when.get(k, -1) for k in pair[c]))):
         la, lb = T.landL[:, 8 * c:8 * c + 1], T.landL[:, 8 * c + 4:8 * c + 5]
-        if c < 2:
-            ts("landL lown zz", "lx%d" % c, T.lx[:, 32 * c:32 * c + 32], zz(32), la, lb, OP.add, OP.add)
-        else:
-            act("landL lown ones", "lx%d" % c, T.lx[:, 32 * c:32 * c + 32], T.ones[:, 0:32], AF.Identity, bias=lb, scale=la)
-    act("m8 ztb pl", "w0", T.ztb[:, 64:96:4], T.m8[:], AF.Copy, scale=pl)
-    act("m8 ztb ph", "w1", T.ztb[:, 66:96:4], T.m8[:], AF.Copy, scale=ph)
-    act("row8 pm", "jw", T.jw[:], T.row8[:], AF.Identity, scale=16.0, bias=T.pf[:, 0:1])
-    op("V", "lx0 lx1 lx2 lx3", "arow", V.transpose, T.arow[:], T.lx[:])
-    act("jw", "jn", T.jn[:], T.jw[:], AF.Identity, scale=-1.0, bias=144.0)
-    act("jw", "jf2", T.jf[:, 2:4], T.jw[:, 0:2], AF.Identity, bias=float(A))
-    W = 130
+        if i == 2:
+            quant("qv", 0, 152, "vt", "vt w0 w1 w20 w21", "qv")
+        ts("ih " + " ".join(pair[c]), "ep%d" % c, T.eqp[:, 64 * c:64 * c + 64], T.ih[:], la, lb, OP.subtract, OP.is_equal)
     for h in range(2):
-        ts("arow a0 a1c", "eq%d" % h, T.eq[:, 128 * h:128 * h + 128], T.arow[:], T.pc[:, 1 + h:2 + h], 512.0,
-           OP.is_equal, OP.mult)
+        op("V", " ".join("ep%d" % c for c in range(H)), "eq%d" % h, V.transpose, T.eq[:, 128 * h:128 * h + 128],
+           T.eqp[:, h:256:2])
     for h in range(4):
         k = h % 2
-        at = W * (h ^ 2)
-        op("V", "eq%d " % k + ("xc" if h < 2 else "rrz F%d" % k), "F%d" % h, V.tensor_tensor_scan,
-           T.rr[:, at + 1:at + 129], T.eq[:, 128 * k:128 * k + 128], T.xc[:] if h < 2 else T.rr[:, W * h:W * h + 128],
+        op("V", "eq%d " % k + ("xs" if h < 2 else "rrz F%d" % k), "F%d" % h, V.tensor_tensor_scan,
+           T.rr[:, W * h + 1:W * h + 129], T.eq[:, 128 * k:128 * k + 128], T.xs[:] if h < 2 else T.rr[:, W * k:W * k + 128],
            0.0, OP.max, OP.min)
-    cp("F0 F1 F2 F3", "fs", T.fs[:], T.rr[:, 128:4 * W:W])
-    tt("F2 F3 lo hi", "sec", T.sec[:, 0:2], T.rr[:, 128:2 * W:W], T.lohi[:, 0:2], OP.mult)
-    send("sec", "o3a", (ahead, eng, "m3", T.sec[:, 0:2], T.land3[:, 4 * r:4 * r + 2]))
+    ts("F0 F1 F2 F3", "fs", T.fs[:], T.rr[:, 128:4 * W:W], 512.0, None, OP.mult)
+    sec = T.land3[:, 8 * r:8 * r + 2]
+    act("F2 F3 l3z", "sec", sec, T.rr[:, 2 * W + 128:4 * W:W], AF.Copy, scale=-512.0)
+    before("G", ["sec"], [])
+    g.remote_dma_fused([move(topo, ahead, eng, S.m3, sec, sec)], local_sem=S.om)
+    count["om"] = width
 
-    pick("qs", 64, 128, "slots", 256, "fs", 0, 4, "slots slown slowns slz slzs fs", "pk")
+    pick("anc", 0, 64, "slots", 288, "fs", 0, 4, "c2 slown slowns qn fs", "pk", at=SLOT)
     for b in range(4):
-        mm(4 + b, "qe", 128 * b, "qs", 128, "qe%d qs pk pks" % b, start=False)
-    act("sec", "adown", T.land3[:, 4 * r:4 * r + 2], T.sec[:, 0:2], AF.Copy)
-    quant("qb2", 0, 128, "ztb", "ztb ztv w0 w1 w20 w21 w22 w23", "qb2")
-    quant("hw", 0, 128, "hot", "ho0 ho1 ho2 ho3", "hwo", at=4 * A)
-    for b in range(4):
+        mm(4 + b, "qe", 128 * b, "anc", 128, "qe%d pk pks" % b, start=False, stop=b < 3)
+    mm(7, "qe", 384, "anc", 128, "qe3 pk pks", xv=A, start=False)
+    quant("hw", A, 128, "hot", "ho0 ho1 ho2 ho3", "hwo")
+    for b in range(3):
         src, tb = T["ps%d" % (4 + b)], T.tb[:, 32 * b:32 * b + 32]
-        act("ps%d" % (4 + b), "tb%d" % b, tb, src[:, n0 - A:n0], AF.Copy)
-        tt("ps%d tb%d" % (4 + b, b), "mt%d" % b, T.att[:, b:4 * A:4], src[:, n0:128], tb, OP.add)
+        act("ps%d" % (4 + b), "tb%d" % b, tb, src[:, A:2 * A], AF.Copy)
+        tt("ps%d tb%d" % (4 + b, b), "mt%d" % b, T.att[:, b:4 * A:4], src[:, 0:A], tb, OP.add)
         if b == 0:
-            mm(4, "qa2", 0, "qb2", 128, "qa2 qb2")
+            mm(4, "qa2", 0, "qv", 128, "qa2 qv", xv=24)
+    act("ps7", "mt3", T.att[:, 3:4 * A:4], T.ps7[:, 0:A], AF.Copy)
+    act("F0 F1", "jf0", T.jf[:, 0:2], T.rr[:, 128:2 * W:W], AF.Sign)
+    act("jf0 jf2", "jf10", T.jf[:, 4:5], T.jf[:, 0:1], AF.Identity, scale=float(A), bias=T.jf[:, 2:3])
     quant("km", 0, 128, "att", "att mt0 mt1 mt2 mt3", "km")
-    ts("ps4", "posD", T.posD[:, 4:16], T.ps4[:, 4:16], 16.0, None, OP.add)
-    tt("ps4 jn", "tmp", T.tmp[:], T.ps4[:, 0:16:2], T.jn[:], OP.add)
-    cp("ps4", "sl", T.sl[:], T.ps4[:, 16:24])
+    ts("ps4", "posD", T.posD[:, 4:16], T.ps4[:, 108:120], 16.0, None, OP.add)
+    tt("ps4 jn", "tmp", T.tmp[:, 4:16:2], T.ps4[:, 108:120:2], T.jn[:, 2:8], OP.add)
     for i in range(4):
         mm(i, "qw", 128 * i, "km", 128, "qw0 qw1 km")
-        layer(i, 0, A, "ht%d" % i, i)
-        if i == 1:
-            ts("F0 F1", "jf0", T.jf[:, 0:2], T.rr[:, 128 + 2 * W:4 * W:W], 0.5, -float(A), OP.is_gt, OP.mult)
-    quant("hq", 0, 128, "hot", "ho0 ho1 ho2 ho3 ht0 ht1 ht2 ht3", "hq")
+        layer(i, 512, A, "ht%d" % i, i)
+    act("jf0 jf2", "jf11", T.jf[:, 5:6], T.jf[:, 1:2], AF.Identity, scale=float(A), bias=T.jf[:, 3:4])
+    act("ps4", "sl", T.sl[:], T.ps4[:, 120:128], AF.Copy)
+    quant("hq", 0, 128, "hot", "ho0 ho1 ho2 ho3 ht0 ht1 ht2 ht3", "hq", at=128)
 
-    h0 = 128 + A * r
-    send("hq", "o3c", (aides, side, "rk", T.hqs[:, 0:A], T.rhs[:]))
-    send("hq", "o3b", (ahead, eng, "h3", raw("hq", 0, A), raw("hw", h0, A)))
+    for k in range(len(RANK[3])):
+        send(3, k)
     arrive("m3", width * (N - 1), "land3")
-    arrive("h3", 2 * width * (N - 1), "hwr")
-    tt("jf0 jf2", "jf1", T.jf[:, 4:6], T.jf[:, 0:2], T.jf[:, 2:4], OP.add)
-    for q in range(N):
-        la, lb = T.land3[:, 4 * q:4 * q + 1], T.land3[:, 4 * q + 1:4 * q + 2]
-        if q % 2:
-            ts("land3 adown zz", "ax%d" % q, T.ax[:, 32 * q:32 * q + 32], zz(32), la, lb, OP.add, OP.add)
-        else:
-            act("land3 adown ones", "ax%d" % q, T.ax[:, 32 * q:32 * q + 32], T.ones[:, 0:32], AF.Identity, bias=lb, scale=la)
-    cp("jf1", "fa", T.fa[:], T.jf[:, 4:6])
-    op("V", " ".join("ax%d" % q for q in range(N)), "ar", V.transpose, T.ar[:], T.ax[:])
-    pick("hw", h0, h0 + A, "hq", 128, "il", 0, 2, "hq il0 il1", "hwn")
+    arrivals(3)
+    act("land3 sec axl", "ax1", T.ax[:, 96:256], T.land3[:].indirect(T.axl[:, 6:16]), AF.Copy)
+    cp("jf10 jf11", "fa", T.fa[:], T.jf[:, 4:6])
+    cp("land3 sec axl", "ax0", T.ax[:, 0:96], T.land3[:].indirect(T.axl[:, 0:6]))
+    pick("hw", h0, h0 + A, "hq", 128, "il", 0, 2, "hq il", "hwn", at=128 - A)
+    op("V", "ax0 ax1", "ar", V.transpose, T.ar[:], T.ax[:])
     cp("ar posD", "aj0", T.aj[:, 64:160], T.ar[:].indirect(T.posD[:, 4:10]))
     act("ar posD", "aj1", T.aj[:, 160:256], T.ar[:].indirect(T.posD[:, 10:16]), AF.Copy)
-    pick("fo", 0, A, "hq", 128, "fa", 0, 2, "hq fa", "foa")
+    pick("qz", 0, A, "hq", 128, "fa", 0, 2, "hq fa", "foa")
+    mm(6, "qv", 0, "qz", 128, "qv foa foas")
     op("V", "aj0 aj1", "ajt", V.transpose, T.ajt[:, 64:256], T.aj[:, 64:256])
-    tt("ajt sl", "adm", T.adm[:, 2:8], T.ajt[:, 64:256:32], T.sl[:, 2:8], OP.is_ge)
-    tt("adm tmp", "f1", T.f1[:, 2:8], T.adm[:, 2:8], T.tmp[:, 2:8], OP.mult)
-    tt("adm m8", "mw2", T.mw2[:, 2:8], T.adm[:, 2:8], T.m8[:, 2:8], OP.mult)
-    tt("f1 jw", "f2", T.f2[:, 2:8], T.f1[:, 2:8], T.jw[:, 2:8], OP.add)
-    act("mw2", "mn", T.mw3[:, 2:8], T.mw2[:, 2:8], AF.Identity, accum_out=mn)
-    cp("f2", "fin", T.fin[:, 2:8], T.f2[:, 2:8])
-    act("mn gn", "mgc", mgc, mn, AF.Identity, scale=gn, bias=-1.0)
+    tt("ajt sl admz", "adm", T.adm[:, 5:16:2], T.ajt[:, 64:256:32], T.sl[:, 2:8], OP.is_gt)
+    act("ps6", "ya", T.yo[:, 0:A], T.ps6[:, 0:A], AF.Copy)
+    op("V", "adm tmp jw2", "f2", V.tensor_tensor_scan, T.f2[:, 4:16], T.adm[:, 4:16], T.tmp[:, 4:16], 0.0, OP.mult, OP.add)
+    act("adm gl", "mn", T.mw3[:], T.adm[:].indirect(T.gl[:, 0:1]), AF.Copy)
+    cp("f2", "fin", T.fin[:, 2:8], T.f2[:, 5:16:2])
+    act("mn gn", "mgc", mgc, T.mw3[:, 0:1], AF.Identity, scale=gn, bias=-1.0)
     dma("S", "mgc", "mgo", T.mg[:], mgc)
 
-    pick("fo", A, 128, "hw", 384, "fin", 2, 8, "hwo hwr hwn hwns fin", "fo")
-    mm(5, "qv", 0, "fo", 128, "qv fo fos foa foas")
-    dma("S", "fo foa", "oco", T.oc[:], T.fo[:].bitcast(dt.uint8))
+    pick("qz", A, 128, "hw", 416, "fin", 2, 8, "hwo h3 hwn hwns fin ya", "fo")
+    mm(5, "qv", 0, "qz", 128, "qv fo fos foa foas")
+    dma("S", "fo foa", "oco", T.oc[:], T.qz[:].bitcast(dt.uint8))
     for k in range(4):
-        dma("A", "fos foas", "osco%d" % k, T.osc[4 * k:4 * k + 4, :], T.fos[32 * k:32 * k + 4, :])
-    cp("ps5", "yo", T.yo[:], T.ps5[:, 0:128])
-    dma("S", "yo", "yout", T.y[:], T.yo[:])
+        dma("SAAA"[k], "fos foas", "osco%d" % k, T.osc[4 * k:4 * k + 4, :], T.qzs[32 * k:32 * k + 4, :])
+    cp("ps5", "yo", T.yo[:, A:], T.ps5[:, A:128])
+    dma("S", "yo ya", "yout", T.y[:], T.yo[:])
     for s, v in count.items():
         if known["S"].get(s, 0) < v:
             SY.wait_ge(S[s], v)

from concourse.bass import DstId, RemoteDMATransfer
from concourse.mybir import dt, AluOpType, AxisListType, ActivationFunctionType

F32, BF, U16, I32, MXC, U8 = "float32", "bfloat16", "uint16", "int32", "float8_e4m3fn_x4", "uint8"
SCRATCH = {}
W0 = 2
AIDES = "fnn"
RANK = {
    1: [[("S", "", (0, 1, 2), 0, 8)], [("C", "a0 a1 a2", None, 0, 8)], [("S", "a0 a1 a2", None, 0, 8)],
        [("C", "b0 b1 b2 b3", None, 0, 8)]],
    2: [[("L", "f0", None, 0, 8)], [("L", "f1", None, 0, 4), ("L", "n0", None, 4, 8)],
        [("L", "f2", None, 0, 2), ("L", "f3", None, 2, 4), ("L", "n1", None, 4, 6), ("L", "n2", None, 6, 8)],
        [("S", "f0 f1 f2 f3", (0,), 0, 8)],
        [("C", "n0 n1 n2", (1,), 0, 8)],
        [("S", "n0 n1 n2", (2,), 0, 8)],
        [("C", "f1", None, 0, 2), ("C", "f2", None, 2, 4), ("C", "f3", None, 4, 6), ("C", "f0", None, 6, 8)]],
    3: [[("C", "f1 f2 f3 n0 n1 n2 f0", None, 0, 8), ("W", "", (0, 1), 0, 8)]],
}
GATE = [6, [(2, 3)]]
HAND = [
    [(1, 0, [[("S", "b0 b1", 0, 8)]]),
     (2, 3, [[("S", "f1", 0, 2), ("S", "f2", 2, 4), ("S", "f3", 4, 6), ("S", "f0", 6, 8)]]),
     (3, 0, [[("S", "f1 f2 f3 f0", 0, 8)]])],
    [(1, 0, [[("S", "b2", 0, 8)]]),
     (2, 4, [[("C", "n0", 0, 4), ("C", "n1", 4, 8)], [("C", "n2", 0, 8)]]),
     (3, 0, [[("S", "n0 n1 n2", 0, 8)]])],
    [(1, 0, [[("S", "b3", 0, 8)]]),
     (2, 5, [[("S", "n0", 0, 4), ("S", "n1", 4, 8)], [("S", "n2", 0, 8)]])],
]
SLOT, NEW = 32, 160


def _buf(name, cols, dtype):
    SCRATCH[name] = ("sbuf", [128, cols], dtype)


def _mx(name, cols):
    _buf(name, cols, MXC)
    _buf(name + "s", cols, U8)


for _n, _c in (("qx", 160), ("anc", 256), ("qtri", 128), ("qa2", 128), ("qe", 512), ("qz", 128), ("qab", 144),
               ("snd", 128), ("slots", 288), ("qw", 512), ("qv", 152), ("km", 128),
               ("hq", 128), ("hw", 416), ("via1", 128), ("via2", 128), ("via3", 128)):
    _mx(_n, _c)
for _n, _c in (("wt", 2048), ("vt", 608), ("ztb", 1152), ("att", 576), ("hot", 640), ("dp", 128), ("da", 128), ("pk", 128),
               ("pm1", 256), ("ih", 64), ("xs", 128), ("eqp", 256), ("eq", 256), ("thr", 64), ("t1", 160), ("rr", 520),
               ("xc", 128), ("us", 48), ("pq", 32), ("land3", 64), ("ax", 256), ("ar", 256), ("aj", 256), ("ajt", 256)):
    _buf(_n, _c, BF)
for _n, _c in (("R", 288), ("mrow", 32), ("pd", 160), ("n32", 8), ("tq", 8), ("sc", 16),
               ("jr", 256), ("j7", 16), ("ab", 32), ("msk", 32), ("num", 32), ("qc", 32),
               ("pf", 8), ("m8", 16), ("r16", 16), ("mst", 8), ("jw", 8), ("jn", 8), ("lst", 8), ("landL", 32), ("axi", 16),
               ("tb", 128), ("tmp", 16), ("sd", 16), ("sl", 8), ("adm", 16), ("f2", 16), ("jf", 8), ("mw3", 16),
               ("yo", 128), ("viaL", 8)):
    _buf(_n, _c, F32)
for _n, _c in (("il", 2), ("off", 8), ("fs", 4), ("posD", 16), ("fin", 8), ("axl", 16), ("fa", 2), ("gl", 2)):
    _buf(_n, _c, U16)
for _i in range(8):
    SCRATCH["ps%d" % _i] = ("psum", [128, 512], F32)
SEMAPHORES = (["cV", "cA", "cP", "cG", "a1", "a2", "c2", "m3", "h3", "o1", "o2", "o3", "om", "ol", "hl", "lh"]
              + ["d%d" % _i for _i in range(14)] + ["l%d" % _i for _i in range(4)]
              + ["k%d%d" % (_r, _i) for _r in (1, 2, 3) for _i in range(8)])


def move(topo, cores, engines, sem, src, dst):
    ids = [DstId(rid=topo.addr(c)[0], pnc=topo.addr(c)[1]) for c in cores]
    return RemoteDMATransfer(dst_ids=ids, dma_engine_mask=sum(1 << e for e in engines), remote_sem=sem, srcs=[src],
                             dsts=[dst] * len(ids))


def longest_first(topo, core, cores):
    a = topo.chip(core)
    return sorted(cores, key=lambda c: topo.mates(a, topo.chip(c)) or topo.same_plane(a, topo.chip(c)))


def plan(own, r, T, topo):
    for b in ((2, 1, 0), (0, 2, 1), (1, 2, 0)):
        order = [r ^ sum((c >> (2 - i) & 1) << b[i] for i in range(3)) for c in range(8)]
        if all(topo.same_plane(topo.chip(own), topo.chip(T.cores[q])) for q in order[1:4]):
            break
    cores = [T.cores[q] for q in order]
    H = len(cores) // 2
    name = {}
    ahead = [cores.index(d) for d in longest_first(topo, own, cores[1:])]
    for k, cs in (("a", [c for c in ahead if order[c] // H == r // H]), ("b", [c for c in ahead if order[c] // H != r // H]),
                  ("n", range(1, H)), ("f", range(H, 2 * H))):
        name.update(("%s%d" % (k, i), c) for i, c in enumerate(cs))
    rest = sorted([c for c in topo.cores_of(own) if c != own], key=lambda c: topo.die(c) != topo.die(own))
    every = [c for c in rest if all(topo.may_write(c, d) for d in cores[1:])]
    some = [c for c in rest if c not in every and all(topo.may_write(c, d) for d in cores[1:H])]
    aides = [(every if k == "f" else some).pop(0) for k in AIDES]
    return order, name, aides


def raw(T, buf, a, n):
    return T[buf][:, a:a + n].bitcast(dt.uint8)


def sides(T, rnd, kind, r, c, n=1, via=False):
    N, A, CAPP = len(T.cores), 32, 16
    H = N // 2
    if kind == "L":
        at = 4 * (N - 1 - r)
        return (T.viaL if via else T.lst)[:, c:c + n], T.landL[:, at:at + 1]
    if rnd == 1:
        src, a, w, dst, b = "slots", 0, A, "anc", A * (r % H + H * (1 - c))
    elif rnd == 2:
        src, a, w, dst, b = "snd", CAPP * c, CAPP * n, "slots", SLOT + 128 + CAPP * (N - 1 - r)
    else:
        src, a, w, dst, b = "hq", 128 - A, A, "hw", NEW + A * r
    if via:
        src = "via%d" % rnd
    one = CAPP if rnd == 2 else A
    if kind == "C":
        return raw(T, src, a, w), raw(T, dst, b, one)
    if kind == "W":
        a, w = 0, 4 * A
    return T[src + "s"][:, a:a + w], T[dst + "s"][:, b:b + one]


def there(rnd, kind, rank, call):
    return "l%s" % call if kind == "L" else ("a2" if rank[0] == "b" else "a1", "c2", "h3")[rnd - 1]


def moves(T, topo, rnd, call, k, r, order, name, eng, via):
    out = []
    for kind, names, lo, hi in call:
        names = names.split()
        src, dst = sides(T, rnd, kind, r, int(names[0][0] == "b") if rnd == 1 else name[names[0]], via=via)
        out.append(move(topo, [T.cores[order[name[n]]] for n in names], eng[lo:hi], T.sem[there(rnd, kind, names[0], k)],
                        src, dst))
    return out


def hand_on(g, core, r, role, order, name, T, topo):
    eng = topo.engines(core, T.cores[order[1]])
    sent = 0
    for rnd, k, calls in HAND[role]:
        g.wait_ge(T.sem["k%d%d" % (rnd, k)], sum(m[4] - m[3] for m in RANK[rnd][k] if m[2] and role in m[2]))
        for call in calls:
            g.remote_dma_fused(moves(T, topo, rnd, call, "h", r, order, name, eng, True), local_sem=T.sem.hl)
            sent += sum(m[3] - m[2] for m in call)
    g.wait_ge(T.sem.hl, sent)


def rank_program(g, core, T, topo):
    N, S = len(T.cores), T.sem
    A, CAPP, KM = 32, 16, 48
    mine = [c for c in T.cores if topo.chip(c) == topo.chip(core)]
    if not mine:
        return
    r = T.rank_of(mine[0])
    order, name, aides = plan(mine[0], r, T, topo)
    if core != mine[0]:
        if core in aides:
            hand_on(g, core, r, aides.index(core), order, name, T, topo)
        return
    OP, AF, X = AluOpType, ActivationFunctionType, AxisListType.X
    V, AC, PE, SY = g.vector, g.scalar, g.tensor, g.sync
    rr = N - 1 - r
    s0 = 128 + CAPP * rr
    tiny = 1e-29

    qs = {"V": V, "A": AC, "P": PE, "G": g, "S": SY}
    count, known = {}, {q: {} for q in qs}
    writer, readers = {}, {}

    def before(q, rd, wr):
        need = [writer[k] for k in rd if k in writer]
        for k in list(wr) + [k for k in rd if k.startswith("ps")]:
            if k in writer:
                need.append(writer[k])
            need += [t for t in readers.get(k, []) if k in wr or t[0] != "c" + q]
        best = {}
        for s, v, clk in need:
            if known[q].get(s, 0) < v and best.get(s, (0,))[0] < v:
                best[s] = (v, clk)
        for s in list(best):
            if not any(o != s and best[o][1].get(s, 0) >= best[s][0] for o in best):
                qs[q].wait_ge(S[s], best[s][0])
        for s, (v, clk) in best.items():
            known[q][s] = max(known[q].get(s, 0), v)
            for a, b in clk.items():
                known[q][a] = max(known[q].get(a, 0), b)

    def after(tok, rd, wr):
        for k in wr:
            writer[k] = tok
            readers[k] = []
        for k in rd:
            readers.setdefault(k, []).append(tok)

    def op(q, rd, wr, fn, *args, **kw):
        rd, wr = rd.split(), wr.split()
        before(q, rd, wr)
        s = "c" + q
        count[s] = count.get(s, 0) + 1
        fn(*args, **kw).then_inc(S[s], 1)
        after((s, count[s], dict(known[q])), rd, wr)

    dn = [0]

    def dma(q, rd, wr, out, in_):
        rd, wr = rd.split(), wr.split()
        before(q, rd, wr)
        s = "d%d" % dn[0]
        dn[0] += 1
        count[s] = 16
        qs[q].dma_start(out, in_).then_inc(S[s], 16)
        after((s, 16, dict(known[q])), rd, wr)

    def arrive(s, n, wr):
        count[s] = n
        after((s, n, {}), [], wr.split())

    def left(s):
        SY.wait_ge(S[s], count[s])
        known["S"][s] = count[s]

    others = [T.cores[q] for q in order[1:]]
    ahead = longest_first(topo, core, others)
    eng = [e for e in topo.engines(core, others[0]) if all(e in topo.engines(core, c) for c in others)]
    width = len(eng)
    side = [e for e in topo.engines(core, aides[0]) if e not in eng]

    def send(rnd, k):
        call, rd = RANK[rnd][k], []
        out = moves(T, topo, rnd, [m[:2] + m[3:] for m in call if not m[2]], k, r, order, name, eng, False)
        for kind, names, to, lo, hi in call:
            cs = [name[n] for n in names.split()] or [0]
            if rnd == 2:
                rd += [{"L": "lst", "C": "snd%s", "S": "snd%ss"}[kind].replace("%s", n[0]) for n in names.split()] + ["l3z"]
            else:
                rd.append("qn" if rnd == 1 else "hq")
            if to:
                out.append(move(topo, [aides[i] for i in to], side[lo:hi], S["k%d%d" % (rnd, k)],
                                sides(T, rnd, kind, r, cs[0], len(cs))[0], sides(T, rnd, kind, r, cs[0], len(cs), True)[0]))
        before("G", rd, [])
        loc = "ol" if (rnd, k) in GATE[1] else "o%d" % rnd
        g.remote_dma_fused(out, local_sem=S[loc])
        count[loc] = count.get(loc, 0) + sum(m[4] - m[3] for m in call)

    def arrivals(rnd):
        got = [(k, m[:2] + m[3:]) for k, call in enumerate(RANK[rnd]) for m in call if not m[2]]
        got += [("h", m) for role in HAND[:len(aides)] for q, k, calls in role if q == rnd for call in calls for m in call]
        tot = {}
        for k, (kind, names, lo, hi) in got:
            for n in names.split():
                e = tot.setdefault(there(rnd, kind, n, k), [0, []])
                e[0] += hi - lo
                e[1].append("%s%d_%d" % (kind, rnd, order[name[n]]))
        for s, (n, keys) in tot.items():
            arrive(s, n, " ".join(keys + [s]))
        return tot

    def ts(rd, wr, out, in0, s1, s2, *ops):
        op("V", rd, wr, V.tensor_scalar, out, in0, s1, s2, *ops)

    def tt(rd, wr, out, in0, in1, o):
        op("V", rd, wr, V.tensor_tensor, out, in0, in1, o)

    def cp(rd, wr, out, in_):
        op("V", rd, wr, V.tensor_copy, out, in_)

    def fill(rd, wr, out, c):
        op("V", rd, wr, V.memset, out, c)

    def act(rd, wr, out, in_, f, **kw):
        op("A", rd, wr, AC.activation, out, in_, f, **kw)

    def iota(wr, out, pattern, base=0, mult=0):
        op("G", "", wr, g.iota, out, pattern, base, mult, allow_small_or_imprecise_dtypes=True)

    def mm(bank, w, wv, x, n, rd, xv=0, start=True, stop=True):
        op("P", rd, "ps%d" % bank, PE.matmul_mx, T["ps%d" % bank][:, 0:n], T[w][:, wv:wv + 128], T[w + "s"][:, wv:wv + 128],
           T[x][:, xv:xv + n], T[x + "s"][:, xv:xv + n], start, stop)

    def quant(out, a, n, tile, rd, wr, at=0):
        op("V", rd, wr, V.quantize_mx, T[out][:, a:a + n], T[out + "s"][:, a:a + n], T[tile][:, at:at + 4 * n])

    def pick(out, a, b, win, w, lists, la, lb, rd, wr, at=0):
        cp(rd, wr, T[out][:, a:b].bitcast(dt.uint32), T[win][:, at:w].bitcast(dt.uint32).indirect(T[lists][:, la:lb]))
        act(rd, wr + "s", T[out + "s"][:, a:b], T[win + "s"][:, at:w].indirect(T[lists][:, la:lb]), AF.Copy)

    def layer(i, a, n, wr, bank, both=True):
        src, out = T["ps%d" % bank][:, 0:n], T.hot[:, a + i:a + 4 * n:4]
        if i % 2 and both:
            ts("ps%d" % bank, wr, out, src, 0.0, 0.0625, OP.max, OP.mult)
        else:
            act("ps%d" % bank, wr, out, src, AF.Relu, scale=0.0625)

    Z = 640

    def zz(n):
        return T.ztb[:, Z:Z + n]

    pp, sg, lo, hi, pm, khi = [T.pf[:, i:i + 1] for i in range(6)]
    p31 = T.pq[:, 0:1]
    dma("S", "", "xa", T.ztb[:, 512:Z], T.x[:, 0:4 * A])
    iota("xc", T.xc[:], [[1, 128]])
    iota("pp", pp, [[0, 1]], 0, 1)
    iota("pk", T.pk[:], [[0, 8], [1, CAPP]])
    fill("", "zz", T.ztb[:, Z:], 0.0)
    dma("S", "zz", "xt", T.ztb[:, 4 * A:512], T.x[:, 4 * A:])
    dma("S", "", "xd", T.ztb[:, 0:4 * A], T.x[:, 4 * A:8 * A])
    dma("S", "", "wt0", T.wt[:, 0:512 * W0], T.w[:, 0:512 * W0])
    fill("", "att", T.att[:], 0.0)
    act("xc pp", "dp", T.dp[:], T.xc[:], AF.Abs, scale=-1.0, bias=pp)
    op("V", "xc", "p31", V.transpose, T.pq[:], T.xc[:, 0:32])
    act("dp att", "e", T.att[:, 4:516:4], T.dp[:], AF.Relu, scale=-0.5, bias=0.5)
    quant("slots", 0, 128, "ztb", "xa zz", "qn", at=512)

    H = N // 2
    p1 = A * (H + r % H)
    h0 = NEW + A * r
    W = 130
    for k in range(len(RANK[1])):
        send(1, k)
    arrivals(1)
    left("o1")
    dma("S", "", "wt1", T.wt[:, 512 * W0:], T.w[:, 512 * W0:])
    dma("S", "", "vt", T.vt[:, 0:512], T.v[:])

    iota("axi", T.axi[:], [[8 * 512, N], [0, 2]])
    op("G", "zz", "thr1", g.affine_select, T.thr[:, 32:64], zz(32), [[0, 32]], OP.is_gt, tiny, 96, -1)
    iota("t10 t1a t2", T.t1[0:32, 32:160], [[0, 128]], 4)
    for k in range(4):
        iota("qc%d" % k, T.qc[:, k // 2 * 16 + k % 2:k // 2 * 16 + 16:2], [[order[c] - r, 2] for c in (4, 2, 1)], r)
    iota("n32", T.n32[:], [[0, 8]], -A)
    iota("num3", T.num[:, 17:32:2], [[0, 8]], 32)
    iota("pm1", T.pm1[:], [[0, 8], [-1, CAPP], [0, 2]], 64 + CAPP)
    iota("r16", T.r16[:], [[16, 8], [0, 2]])
    iota("l3z", T.land3[:], [[0, 64]])
    iota("vz", T.vt[:, 512:608], [[0, 96]])
    iota("ih", T.ih[:], [[0, 2], [-512, 16], [-8192, 2]], -8192)
    iota("rrz", T.rr[:, 0:W + 1:W], [[0, 2]])
    iota("admz", T.adm[:], [[0, 16]])

    act("p31", "sg", sg, p31, AF.Sign, bias=-15.5)
    act("sg", "hi", hi, sg, AF.Identity, scale=-256.0, bias=-256.0)
    act("hi p31", "pm", pm, hi, AF.Identity, scale=1.0 / 32, bias=p31)
    act("sg", "lo", lo, sg, AF.Identity, scale=256.0, bias=-256.0)
    act("xc", "xs", T.xs[:], T.xc[:], AF.Identity, scale=1.0 / 512, bias=0.25)
    act("pm pp", "khi", khi, pm, AF.Identity, scale=-1.0, bias=pp)
    act("zz pm", "num0", T.num[:, 0:16:2], zz(8), AF.Identity, bias=pm)
    act("pk pm", "da", T.da[:], T.pk[:], AF.Abs, scale=-1.0, bias=pm)
    act("zz khi", "num1", T.num[:, 1:16:2], zz(8), AF.Identity, bias=khi)
    for b in range(4):
        quant("qe", 128 * b, 128, "att", "att e", "qe%d" % b, at=4 - b)
        mm(4 + b, "qe", 128 * b, "slots", 128, "qe%d qn" % b, stop=False)
        if b == 1:
            ts("xc pm", "il", T.il[:], T.xc[:, 0:17:16], pm, None, OP.add)
        if b == 2:
            pick("anc", p1, p1 + A, "slots", A, "il", 0, 2, "qn il", "ancown")
    ts("xc pp", "att e", T.att[:, 0:512:4], T.xc[:], pp, None, OP.is_ge)
    act("dp qe3", "cid", T.att[:, 2:512:4], T.dp[:], AF.Relu, scale=-64.0, bias=64.0)
    if r >= H:
        act("zz", "pdz", T.pd[:, 0:128], zz(128), AF.Identity, bias=-9.0e29)
    act("xc pm", "jw", T.jw[:], T.xc[:, 0:128:16], AF.Identity, bias=pm)
    quant("qx", 0, 160, "ztb", "xa xt xd", "qx")
    quant("qtri", 0, 128, "att", "att cid", "qtri")
    ts("xc p31", "thr0", T.thr[:, 0:32], T.xc[:, 0:32], p31, tiny, OP.is_lt, OP.mult)
    act("da", "att", T.att[:, 0:512:4], T.da[:], AF.Relu, scale=-1.0, bias=1.0)
    act("da", "cid", T.att[:, 2:512:4], T.da[:], AF.Relu, scale=-1.0, bias=1.0)
    quant("qw", 0, 128 * W0, "wt", "wt0", "qw0")
    for i in range(W0):
        mm(2 + i % 2, "qw", 128 * i, "qx", 128, "qw0 qx", xv=A)
        layer(i, 0, 128, "ho%d" % i, 2 + i % 2, False)
    ts("khi", "gl", T.gl[:, 0:1], khi, 1.0 / 8, 1.0, OP.mult, OP.add)
    quant("qa2", 0, 128, "att", "att cid", "qa2")
    ts("axi hi", "axl", T.axl[:], T.axi[:], hi, 1.0 / 512, OP.subtract, OP.mult)

    best, q1, o1, st2, st, q32, gn, mgc, q0, b0, qx, bx, o0 = [T.sc[:, i:i + 1] for i in range(13)]
    M, u, d16 = T.R[:, 287:288], T.us[:, 47:48], T.num[:, 16:17]
    M1 = T.R[:, 127:128]
    mm(0, "qx", 0, "anc", 128, "qx a1 ancown ancowns", xv=128)
    op("V", "ps0 zz", "R1", V.tensor_tensor_scan, T.R[:, 0:128], T.ps0[:, 0:128], zz(128), -9.0e29, OP.max, OP.add)
    if r >= H:
        act("R1 zz", "pd", T.pd[:, 128:160], zz(A), AF.Identity, bias=M1)
        act("R1", "q0 j7", T.j7[:, 0:H], T.R[:, A - 1:H * A:A], AF.Sign, bias=M1, scale=-1.0, accum_out=q0)
        act("R1", "b0 jr", T.jr[:, 0:128], T.R[:, 0:128], AF.Sign, bias=M1, scale=-1.0, accum_out=b0)
    mm(1, "qx", 0, "anc", 160, "qx a2 a1 ancown ancowns")
    if r >= H:
        op("V", "ps1 pd pdz", "R", V.tensor_tensor_scan, T.R[:, 128:288], T.ps1[:, 0:160], T.pd[:], -9.0e29, OP.max, OP.max)
    else:
        op("V", "ps1 zz R1", "R", V.tensor_tensor_scan, T.R[:, 128:288], T.ps1[:, 0:160], zz(160), M1, OP.max, OP.add)
    op("V", "R", "m0", V.transpose, T.mrow[:], T.R[:, 256:288])
    flag = T.j7[:, N - 1:N]
    if r >= H:
        act("R", "qq fl", T.j7[:, H:N], T.R[:, (H + 1) * A - 1:N * A:A], AF.Sign, bias=M, scale=-1.0, accum_out=qx)
    else:
        act("R R1", "q1 j7", T.j7[:, 0:N], T.R[:, A - 1:N * A:A], AF.Sign, bias=M, scale=-1.0, accum_out=q1)

    def quad(t, q, c, n=1):
        return T[t][32 * q:32 * (q + n), c:c + 32]

    def top(q, n=1):
        return T.R[32 * q:32 * (q + n), 287:288]

    ts("R m0", "t1a", T.t1[:, 0:32], T.mrow[:], M, -1.0, OP.subtract, OP.mult)
    for a, b in ((1, 2), (2, 3), (3, 2)):
        act("R m0", "t1%d" % a, quad("t1", a, 32), quad("mrow", b, 0), AF.Identity, scale=-1.0, bias=top(a))
    if r >= H:
        act("qq fl q0", "q1", q1, flag, AF.Identity, scale=q0, bias=qx)
    ts("R m0", "t21", quad("t1", 1, 128), quad("mrow", 3, 0), top(1), None, OP.is_gt)
    ts("R m0", "t22", quad("t1", 2, 128, 2), quad("mrow", 0, 0, 2), top(2, 2), None, OP.is_ge)
    act("q1 qc0 qc1 qc2 qc3", "ab", T.ab[:], T.qc[:], AF.Abs, bias=q1, scale=-1.0)
    if r >= H:
        act("R", "bx jr2", T.jr[:, 128:256], T.R[:, 128:256], AF.Sign, bias=M, scale=-1.0, accum_out=bx)
    else:
        act("R R1", "best jr", T.jr[:], T.R[:, 0:256], AF.Sign, bias=M, scale=-1.0, accum_out=best)
    act("q1 n32", "tq", T.tq[:], T.n32[:], AF.Identity, scale=q1, bias=-16.0)
    if r >= H:
        act("bx fl b0", "best", best, flag, AF.Identity, scale=b0, bias=bx)
    act("tq best", "num2", T.num[:, 16:32:2], T.tq[:], AF.Identity, bias=best)
    act("q1", "q32", q32, q1, AF.Copy, scale=float(A))
    act("r16 khi", "m7", T.sd[:], T.r16[:], AF.Abs, scale=-1.0, bias=khi)
    tt("t1a t11 t12 t13 t10 thr0 thr1", "t2", T.t1[:, 64:128], T.t1[:, 0:64], T.thr[:], OP.is_lt)
    op("V", "t2 t10 t21 t22", "u", V.tensor_tensor_scan, T.us[:], T.t1[:, 64:112], T.t1[:, 112:160], 1.0 - KM,
       OP.add, OP.add)
    ts("ab u zz", "ztv", T.ztb[:, Z + 480:Z + 512:2], T.ab[:, 0:16], u, 0.5, OP.max, OP.is_lt)
    quant("qz", 0, 128, "ztb", "ztv zz", "qz", at=Z)
    mm(1, "qtri", 0, "qz", 128, "qtri qz")
    ts("ab", "msk", T.msk[:], T.ab[:], 0.5, None, OP.is_lt)
    op("V", "ps1", "o1v", V.tensor_reduce, o1, T.ps1[:, 120:128], X, OP.max)
    act("o1v", "st2", st2, o1, AF.Abs, bias=-(64.5 + CAPP / 2))
    act("o1v", "o0", o0, o1, AF.Identity, bias=-65.0)
    act("m7", "m8", T.m8[:], T.sd[:], AF.Relu, scale=-1.0, bias=1.0)
    tt("msk num0 num1 num2 num3", "bt e", T.att[:, 512:576:2], T.msk[:], T.num[:], OP.mult)
    ts("pm1 o1v", "at0 att cid", T.att[:, 0:512:2], T.pm1[:], o1, None, OP.is_equal)
    quant("qab", 0, 144, "att", "att at0 bt", "qab")
    mm(2, "qab", 0, "qab", 128, "qab", xv=16)
    ts("st2", "st", st, st2, CAPP / 2, None, OP.is_lt)
    for k, v in enumerate((d16, q32)):
        act("m8 vz num2 q32", "w2%d" % k, T.vt[:, 512 + 2 * k:576:4], T.m8[:], AF.Copy, scale=v)
    act("m8 st", "mst", T.mst[:], T.m8[:, 0:16:2], AF.Copy, scale=st)

    ts("ps2 lo hi", "lst", T.lst[:], T.ps2[:, 120:128], hi if rr % 2 else lo, None, OP.mult)
    cp("ps2", "off", T.off[:], T.ps2[:, 112:120])
    lists = [k for k, call in enumerate(RANK[2]) if call[0][0] == "L"]
    for k in lists:
        send(2, k)
    half = CAPP * H
    pick("snd", half, 2 * half, "qx", 128, "off", H, N, "qx off", "sndf")
    pick("snd", 0, half, "qx", 128, "off", 0, H, "qx off", "sndn")
    for k in range(len(lists), len(RANK[2])):
        if k == GATE[0]:
            g.wait_ge(S.ol, count["ol"])
            known["S"]["ol"] = count["ol"]
        send(2, k)
    got = arrivals(2)

    act("lst", "L2_%d" % r, T.landL[:, 4 * rr:4 * rr + 1], T.lst[:, 0:1], AF.Copy)
    act("mst vz o0", "w0", T.vt[:, 576:608:4], T.mst[:], AF.Copy, scale=o0)
    act("mst vz", "w1", T.vt[:, 578:608:4], T.mst[:], AF.Copy, scale=-float(s0 + CAPP))
    quant("qw", 128 * W0, 512 - 128 * W0, "wt", "wt1", "qw1", at=512 * W0)
    pick("slots", SLOT + s0, SLOT + s0 + CAPP, "qx", 128, "off", 0, 1, "qx off", "slown")
    for i in range(W0, 4):
        mm(i % 2, "qw", 128 * i, "qx", 128, "qw1 qx", xv=A)
        layer(i, 0, 128, "ho%d" % i, i % 2, False)
    act("jw", "jn", T.jn[:], T.jw[:], AF.Identity, scale=-1.0, bias=NEW + 16.0)
    act("q1 best", "gn", gn, q1, AF.Identity, scale=128.0 - A, bias=best)
    act("jw", "jw2", T.tmp[:, 5:16:2], T.jw[:, 2:8], AF.Copy)
    act("jw", "jf2", T.jf[:, 2:4], T.jw[:, 0:2], AF.Identity, bias=64.0)
    act("gn", "gn", gn, gn, AF.Identity, bias=1.0)

    when = {key: i for i, s in enumerate(got) for key in got[s][1]}
    pair = [["L2_%d" % (N - 1 - 2 * c - k) for k in range(2)] for c in range(H)]
    for i, c in enumerate(sorted(range(H), key=lambda c: max(when.get(k, -1) for k in pair[c]))):
        la, lb = T.landL[:, 8 * c:8 * c + 1], T.landL[:, 8 * c + 4:8 * c + 5]
        if i == 2:
            quant("qv", 0, 152, "vt", "vt w0 w1 w20 w21", "qv")
        ts("ih " + " ".join(pair[c]), "ep%d" % c, T.eqp[:, 64 * c:64 * c + 64], T.ih[:], la, lb, OP.subtract, OP.is_equal)
    for h in range(2):
        op("V", " ".join("ep%d" % c for c in range(H)), "eq%d" % h, V.transpose, T.eq[:, 128 * h:128 * h + 128],
           T.eqp[:, h:256:2])
    for h in range(4):
        k = h % 2
        op("V", "eq%d " % k + ("xs" if h < 2 else "rrz F%d" % k), "F%d" % h, V.tensor_tensor_scan,
           T.rr[:, W * h + 1:W * h + 129], T.eq[:, 128 * k:128 * k + 128], T.xs[:] if h < 2 else T.rr[:, W * k:W * k + 128],
           0.0, OP.max, OP.min)
    ts("F0 F1 F2 F3", "fs", T.fs[:], T.rr[:, 128:4 * W:W], 512.0, None, OP.mult)
    sec = T.land3[:, 8 * r:8 * r + 2]
    act("F2 F3 l3z", "sec", sec, T.rr[:, 2 * W + 128:4 * W:W], AF.Copy, scale=-512.0)
    before("G", ["sec"], [])
    g.remote_dma_fused([move(topo, ahead, eng, S.m3, sec, sec)], local_sem=S.om)
    count["om"] = width

    pick("anc", 0, 64, "slots", 288, "fs", 0, 4, "c2 slown slowns qn fs", "pk", at=SLOT)
    for b in range(4):
        mm(4 + b, "qe", 128 * b, "anc", 128, "qe%d pk pks" % b, start=False, stop=b < 3)
    mm(7, "qe", 384, "anc", 128, "qe3 pk pks", xv=A, start=False)
    quant("hw", A, 128, "hot", "ho0 ho1 ho2 ho3", "hwo")
    for b in range(3):
        src, tb = T["ps%d" % (4 + b)], T.tb[:, 32 * b:32 * b + 32]
        act("ps%d" % (4 + b), "tb%d" % b, tb, src[:, A:2 * A], AF.Copy)
        tt("ps%d tb%d" % (4 + b, b), "mt%d" % b, T.att[:, b:4 * A:4], src[:, 0:A], tb, OP.add)
        if b == 0:
            mm(4, "qa2", 0, "qv", 128, "qa2 qv", xv=24)
    act("ps7", "mt3", T.att[:, 3:4 * A:4], T.ps7[:, 0:A], AF.Copy)
    act("F0 F1", "jf0", T.jf[:, 0:2], T.rr[:, 128:2 * W:W], AF.Sign)
    act("jf0 jf2", "jf10", T.jf[:, 4:5], T.jf[:, 0:1], AF.Identity, scale=float(A), bias=T.jf[:, 2:3])
    quant("km", 0, 128, "att", "att mt0 mt1 mt2 mt3", "km")
    ts("ps4", "posD", T.posD[:, 4:16], T.ps4[:, 108:120], 16.0, None, OP.add)
    tt("ps4 jn", "tmp", T.tmp[:, 4:16:2], T.ps4[:, 108:120:2], T.jn[:, 2:8], OP.add)
    for i in range(4):
        mm(i, "qw", 128 * i, "km", 128, "qw0 qw1 km")
        layer(i, 512, A, "ht%d" % i, i)
    act("jf0 jf2", "jf11", T.jf[:, 5:6], T.jf[:, 1:2], AF.Identity, scale=float(A), bias=T.jf[:, 3:4])
    act("ps4", "sl", T.sl[:], T.ps4[:, 120:128], AF.Copy)
    quant("hq", 0, 128, "hot", "ho0 ho1 ho2 ho3 ht0 ht1 ht2 ht3", "hq", at=128)

    for k in range(len(RANK[3])):
        send(3, k)
    arrive("m3", width * (N - 1), "land3")
    arrivals(3)
    act("land3 sec axl", "ax1", T.ax[:, 96:256], T.land3[:].indirect(T.axl[:, 6:16]), AF.Copy)
    cp("jf10 jf11", "fa", T.fa[:], T.jf[:, 4:6])
    cp("land3 sec axl", "ax0", T.ax[:, 0:96], T.land3[:].indirect(T.axl[:, 0:6]))
    pick("hw", h0, h0 + A, "hq", 128, "il", 0, 2, "hq il", "hwn", at=128 - A)
    op("V", "ax0 ax1", "ar", V.transpose, T.ar[:], T.ax[:])
    cp("ar posD", "aj0", T.aj[:, 64:160], T.ar[:].indirect(T.posD[:, 4:10]))
    act("ar posD", "aj1", T.aj[:, 160:256], T.ar[:].indirect(T.posD[:, 10:16]), AF.Copy)
    pick("qz", 0, A, "hq", 128, "fa", 0, 2, "hq fa", "foa")
    mm(6, "qv", 0, "qz", 128, "qv foa foas")
    op("V", "aj0 aj1", "ajt", V.transpose, T.ajt[:, 64:256], T.aj[:, 64:256])
    tt("ajt sl admz", "adm", T.adm[:, 5:16:2], T.ajt[:, 64:256:32], T.sl[:, 2:8], OP.is_gt)
    act("ps6", "ya", T.yo[:, 0:A], T.ps6[:, 0:A], AF.Copy)
    op("V", "adm tmp jw2", "f2", V.tensor_tensor_scan, T.f2[:, 4:16], T.adm[:, 4:16], T.tmp[:, 4:16], 0.0, OP.mult, OP.add)
    act("adm gl", "mn", T.mw3[:], T.adm[:].indirect(T.gl[:, 0:1]), AF.Copy)
    cp("f2", "fin", T.fin[:, 2:8], T.f2[:, 5:16:2])
    act("mn gn", "mgc", mgc, T.mw3[:, 0:1], AF.Identity, scale=gn, bias=-1.0)
    dma("S", "mgc", "mgo", T.mg[:], mgc)

    pick("qz", A, 128, "hw", 416, "fin", 2, 8, "hwo h3 hwn hwns fin ya", "fo")
    mm(5, "qv", 0, "qz", 128, "qv fo fos foa foas")
    dma("S", "fo foa", "oco", T.oc[:], T.qz[:].bitcast(dt.uint8))
    for k in range(4):
        dma("SAAA"[k], "fos foas", "osco%d" % k, T.osc[4 * k:4 * k + 4, :], T.qzs[32 * k:32 * k + 4, :])
    cp("ps5", "yo", T.yo[:, A:], T.ps5[:, A:128])
    dma("S", "yo ya", "yout", T.y[:], T.yo[:])
    for s, v in count.items():
        if known["S"].get(s, 0) < v:
            SY.wait_ge(S[s], v)
